import numpy as np
import ml_dtypes


def mxq(x, axis, fmt="e4m3"):
    dtype, down = {"e4m3": (ml_dtypes.float8_e4m3fn, 7), "e5m2": (ml_dtypes.float8_e5m2, 14)}[fmt]
    v = np.moveaxis(np.asarray(x, np.float32).astype(ml_dtypes.bfloat16).astype(np.float64), axis, -1)
    blocks = v.reshape(v.shape[:-1] + (-1, 32))
    amax = np.abs(blocks).max(-1, keepdims=True)
    byte = np.maximum(np.where(amax > 0, np.frexp(amax)[1] - 1 + 127, 0) - down, 1)
    scale = np.exp2(byte - 127.0)
    codes = (blocks / scale).astype(np.float32).astype(dtype).astype(np.float64)
    return np.moveaxis((codes * scale).reshape(v.shape), -1, axis)


WIDE = False


def mx_kscale(k):
    if not WIDE:
        return np.ones(k)
    levels = np.array([10, -10, 5, -5, 0])
    if k % 512:
        return np.exp2(np.random.permutation(np.resize(levels, k // 32))).repeat(32)
    a = np.empty((k // 512, 16))
    for p in range(k // 512):
        a[p, :8] = np.random.permutation(np.resize(levels, 8))
        for g in range(8):
            far = levels[np.abs(levels - a[p, g]) >= 10]
            a[p, g + 8] = far[np.random.randint(len(far))]
    return np.exp2(a.ravel()).repeat(32)


def f64(x):
    return np.asarray(x).astype(np.float64)


def striped(idx):
    return np.tile(idx.reshape(-1, 16).T, (8, 1)).astype(np.uint16)


def unstriped(offs):
    return offs[:16].T.reshape(-1).astype(np.int64)


def pack_weight(w):
    k, n = w.shape
    w = f64(np.asarray(w, np.float32).astype(ml_dtypes.bfloat16)).reshape(k // 32, 32, n)
    amax = np.abs(w).max(1)
    byte = np.clip(np.where(amax > 0, np.frexp(amax)[1] - 1 + 127 - 7, 1), 1, 254)
    scaled = (w * np.exp2(127.0 - byte)[:, None, :]).reshape(k, n).astype(np.float32)
    words = np.ascontiguousarray(scaled.reshape(k // 512, 128, 4, n).transpose(0, 1, 3, 2)).astype(ml_dtypes.float8_e4m3fn).view(np.uint8)
    return words, np.ascontiguousarray(byte.astype(np.uint8).reshape(k // 512, 16, n))


def unpack_weight(words, scales):
    g, p, n, _ = words.shape
    vals = np.ascontiguousarray(words).view(ml_dtypes.float8_e4m3fn).astype(np.float64) * np.repeat(np.exp2(scales.astype(np.float64) - 127.0), 8, axis=1)[..., None]
    return vals.transpose(0, 1, 3, 2).reshape(g * 512, n)


def relu(v):
    return np.maximum(v, 0.0)

def planes(y):
    n, m = y.shape
    v = y.astype(np.float32).astype(ml_dtypes.bfloat16).astype(np.float64).reshape(n // 32, 32, m)
    top = np.abs(v).max(1)
    byte = np.clip(np.where(top > 0, np.frexp(top)[1] - 1 + 127 - 7, 1), 1, 254)
    codes = (v * np.exp2(127.0 - byte)[:, None, :]).reshape(n, m).astype(np.float32).astype(ml_dtypes.float8_e4m3fn).view(np.uint8)
    words = codes.reshape(n // 512, 128, 4, m).transpose(0, 1, 3, 2)
    return np.ascontiguousarray(words), np.ascontiguousarray(byte.astype(np.uint8).reshape(n // 512, 16, m))


K, T, H = 512, 512, 512


def setup_inputs():
    n = np.random.standard_normal
    s = mx_kscale(K)[:, None]
    u = mx_kscale(H)
    packed_xT = pack_weight(n((K, T)) * s)
    packed_w3 = pack_weight(n((H, H)) / np.sqrt(H) / u[:, None])
    return {
        "x_words": packed_xT[0],
        "x_scales": packed_xT[1],
        "w1": (n((K, H)) / np.sqrt(2 * K) / s * u).astype(np.float32),
        "w2": (n((K, H)) / np.sqrt(2 * K) / s * u).astype(np.float32),
        "w3_words": packed_w3[0],
        "w3_scales": packed_w3[1],
        "pos1": striped(np.random.permutation(T)),
        "pos2": striped(np.random.permutation(T)),
        "pos3": striped(np.random.permutation(T)),
    }


def reference(x_words, x_scales, w1, w2, w3_words, w3_scales, pos1, pos2, pos3):
    xq = unpack_weight(x_words, x_scales)
    y = mxq(f64(w1), 0, "e4m3").T @ xq
    e = mxq(f64(w2), 0, "e4m3").T @ xq
    z = np.maximum(np.maximum(relu(y + e[:, unstriped(pos1)]), relu(y + e[:, unstriped(pos2)])), relu(y + e[:, unstriped(pos3)]))
    out_0 = unpack_weight(w3_words, w3_scales).T @ mxq(z, 0, "e4m3")
    return (out_0,) + planes(out_0)

@@ -1,0 +1,252 @@
+from contextlib import ExitStack
+
+import concourse.mybir as mybir
+from concourse.masks import make_identity
+
+K, T, H = 512, 512, 512
+FLOPS = 3 * 2 * K * T * H
+
+F32 = mybir.dt.float32
+BF16 = mybir.dt.bfloat16
+I32 = mybir.dt.int32
+U32 = mybir.dt.uint32
+U16 = mybir.dt.uint16
+U8 = mybir.dt.uint8
+FP8X4 = mybir.dt.float8_e4m3fn_x4
+RELU = mybir.ActivationFunctionType.Relu
+MAX = mybir.AluOpType.max
+
+P = 128
+TILES = H // P
+CHUNKS = [(0, 256), (256, 128), (384, 128)]
+
+
+def tile_picked_wedgecv_relu_lo_kernel(
+    tc, x_words, x_scales, w1, w2, w3_words, w3_scales, pos1, pos2, pos3, out_0, out_1, out_2
+):
+    nc = tc.nc
+    with ExitStack() as ctx:
+        keep = ctx.enter_context(tc.tile_pool(name="keep", bufs=1))
+        psum = ctx.enter_context(tc.psum_pool(name="psum", bufs=1))
+
+        def sb(shape, dtype, name, tag=None):
+            return keep.tile(shape, dtype, name=name, tag=tag or name, align_bytes=64)
+
+        lists = [keep.tile([P, T // 16], U16, name="pos%d" % d) for d in range(3)]
+        x_codes = sb([P, T], U32, "x_codes")
+        x_plane = sb([P, T], U8, "x_plane")
+        w3_raw = sb([P, H], U32, "w3_raw")
+        w3_raw_plane = sb([P, H], U8, "w3_raw_plane")
+        w3_codes = sb([P, H], U32, "w3_codes")
+        w3_plane = sb([P, H], U8, "w3_plane")
+        ident = sb([P, P], F32, "ident")
+        warm = sb([P, 16], F32, "warm")
+
+        nc.vector.memset(x_plane[:].bitcast(I32), 0)
+        nc.vector.memset(w3_raw_plane[:].bitcast(I32), 0)
+        nc.vector.memset(warm[:, 0:8], 0.0)
+        make_identity(nc, ident[:])
+
+        def load_scales(queue, plane, scales):
+            for q in range(4):
+                queue.dma_start(
+                    out=plane[32 * q : 32 * q + 4, :].bitcast(I32),
+                    in_=scales[0, 4 * q : 4 * q + 4, :].bitcast(I32),
+                )
+
+        def load_weight(w, first, count, name):
+            raw = sb([P, 4, count * P], F32, name)
+            nc.sync.dma_start(
+                out=raw[:], in_=w.rearrange("(p j) c -> p j c", j=4)[:, :, first * P : (first + count) * P]
+            )
+            return [raw[:, :, n * P : (n + 1) * P] for n in range(count)]
+
+        w2_raw = load_weight(w2, 0, 1, "w2_raw0")
+        nc.sync.dma_start(out=x_codes[:].bitcast(I32), in_=x_words[0].rearrange("p n t -> p (n t)").bitcast(I32))
+        load_scales(nc.scalar, x_plane, x_scales)
+        w2_raw = w2_raw + load_weight(w2, 1, 1, "w2_raw1")
+        for offsets, pos in zip(lists, (pos1, pos2, pos3)):
+            nc.sync.dma_start(offsets[:], pos)
+        w2_raw = w2_raw + load_weight(w2, 2, 2, "w2_raw2")
+        w1_raw = load_weight(w1, 0, 2, "w1_raw0") + load_weight(w1, 2, 2, "w1_raw2")
+        nc.sync.dma_start(out=w3_raw[:].bitcast(I32), in_=w3_words[0].rearrange("p n t -> p (n t)").bitcast(I32))
+        load_scales(nc.sync, w3_raw_plane, w3_scales)
+        nc.scalar.activation(warm[:, 8:16], warm[:, 0:8], RELU)
+
+        first_banks = [psum.tile([P, T], F32, name="first%d" % n) for n in range(3)]
+        sum_banks = [psum.tile([P, T], F32, name="sum%d" % n) for n in range(2)]
+        word_bank = psum.tile([P, T], F32, name="word_bank")
+        out_banks = [psum.tile([P, T], F32, name="out%d" % n) for n in range(2)]
+
+        def first_product(raw, name, n, cast_on_vector):
+            grouped = sb([P, 4 * P], BF16, name + "_bf")
+            dst = grouped[:].rearrange("p (u q e j) -> p q j u e", u=2, e=2, j=4)
+            src = raw.rearrange("p j (q u e) -> p q j u e", u=2, e=2)
+            if cast_on_vector:
+                nc.vector.tensor_copy(out=dst, in_=src)
+            else:
+                nc.scalar.copy(out=dst, in_=src)
+            codes = sb([P, P], U32, name + "_codes")
+            plane = sb([P, P], U8, name + "_plane")
+            nc.vector.quantize_mx(out=codes[:].bitcast(FP8X4), scales=plane[:], in_=grouped[:])
+            bank = first_banks[n % 3]
+            nc.tensor.matmul_mx(
+                out=bank[:],
+                lhsT=codes[:].bitcast(FP8X4),
+                lhsT_scale=plane[:],
+                rhs=x_codes[:].bitcast(FP8X4),
+                rhs_scale=x_plane[:],
+                start=True,
+                stop=True,
+            )
+            rows = sb([P, T], F32, name)
+            nc.scalar.copy(out=rows[:], in_=bank[:])
+            return rows
+
+        rings = [[sb([P, 256], F32, "ring%d_%d" % (d, n)) for n in range(2)] for d in range(4)]
+        z_turned = [sb([P, 4 * width], BF16, "z_turned%d" % n) for n, (start, width) in enumerate(CHUNKS)]
+        out_codes = sb([P, T], U32, "out_codes")
+        out_plane = sb([P, T], U8, "out_plane")
+        e = []
+        y = []
+        largest = {}
+        z_q = {}
+
+        def neighbours(chunk, c, behind=None):
+            start, width = CHUNKS[chunk]
+            turn = (chunk * TILES + c) % 2
+            got = [rings[d][turn][:, 0:width] for d in range(3)]
+            if behind is not None:
+                held = sb([P, width], F32, "held%d_%d" % (chunk, c), tag=behind)
+                got[0] = held[:]
+            for d in range(3):
+                nc.vector.tensor_copy(got[d], e[c][:].indirect(lists[d][:, start // 16 : (start + width) // 16]))
+            pair = rings[3][turn][:, 0:width]
+            nc.vector.tensor_tensor(pair, got[0], got[1], MAX)
+            top = sb([P, width], F32, "top%d_%d" % (chunk, c))
+            nc.vector.tensor_tensor(top[:], pair, got[2], MAX)
+            largest[(chunk, c)] = top
+
+        def edge_sum(chunk, c):
+            start, width = CHUNKS[chunk]
+            bank = sum_banks[(chunk * TILES + c) % 2]
+            for b in range(width // P):
+                cols = slice(b * P, (b + 1) * P)
+                nc.tensor.matmul(
+                    bank[:, cols], y[c][:, start + b * P : start + (b + 1) * P], ident[:],
+                    start=True, stop=False, is_transpose=True,
+                )
+                nc.tensor.matmul(
+                    bank[:, cols], largest[(chunk, c)][:, cols], ident[:],
+                    start=False, stop=True, is_transpose=True,
+                )
+            dst = z_turned[chunk][:].rearrange("v (b u c r) -> v c b u r", u=2, c=TILES, r=64)[:, c, :, :, :]
+            src = bank[:, 0:width].rearrange("v (b u r) -> v b u r", u=2, r=64)
+            nc.scalar.activation(dst, src, RELU)
+
+        def quantize_z(chunk):
+            start, width = CHUNKS[chunk]
+            words = z_turned[chunk][:].bitcast(F32)
+            for n in range(2 * width // P):
+                nc.tensor.transpose(word_bank[:, n * P : (n + 1) * P], words[:, n * P : (n + 1) * P], ident[:])
+            grouped = sb([P, 4 * width], BF16, "z_bf%d" % chunk)
+            nc.scalar.copy(
+                out=grouped[:].bitcast(F32).rearrange("p (b v u) -> p b v u", v=P, u=2),
+                in_=word_bank[:, 0 : 2 * width].rearrange("p (b u v) -> p b v u", v=P, u=2),
+            )
+            codes = sb([P, width], U32, "z_codes%d" % chunk)
+            plane = sb([P, width], U8, "z_plane%d" % chunk)
+            nc.vector.quantize_mx(out=codes[:].bitcast(FP8X4), scales=plane[:], in_=grouped[:])
+            z_q[chunk] = (codes, plane)
+
+        def project(chunk, b, last=False):
+            start, width = CHUNKS[chunk]
+            block = start // P + b
+            codes, plane = z_q[chunk]
+            bank = out_banks[block % 2]
+            for t in range(4):
+                nc.tensor.matmul_mx(
+                    out=bank[:, t * P : (t + 1) * P],
+                    lhsT=w3_codes[:, t * P : (t + 1) * P].bitcast(FP8X4),
+                    lhsT_scale=w3_plane[:, t * P : (t + 1) * P],
+                    rhs=codes[:, b * P : (b + 1) * P].bitcast(FP8X4),
+                    rhs_scale=plane[:, b * P : (b + 1) * P],
+                    start=True,
+                    stop=True,
+                )
+            cols = slice(block * P, (block + 1) * P)
+            result = sb([P, T], F32, "result%d" % block)
+            grouped = sb([P, T], BF16, "out_bf%d" % block)
+            nc.scalar.copy(out=result[:], in_=bank[:])
+            nc.sync.dma_start(
+                out=out_0.rearrange("(p t) v -> p t v", t=4)[:, :, cols],
+                in_=result[:].rearrange("p (t v) -> p t v", t=4),
+            )
+            if last:
+                nc.vector.tensor_copy(
+                    out=grouped[:].rearrange("p (s i t) -> p s t i", i=4, t=4),
+                    in_=result[:].rearrange("p (t s i) -> p s t i", i=4, t=4),
+                )
+            else:
+                nc.scalar.copy(
+                    out=grouped[:].rearrange("p (v t) -> p v t", t=4),
+                    in_=bank[:].rearrange("p (t v) -> p v t", t=4),
+                )
+            nc.vector.quantize_mx(out=out_codes[:, cols].bitcast(FP8X4), scales=out_plane[:, cols], in_=grouped[:])
+            nc.sync.dma_start(
+                out=out_1[0].rearrange("p n t -> p (n t)").bitcast(I32)[:, cols],
+                in_=out_codes[:, cols].bitcast(I32),
+            )
+
+        e.append(first_product(w2_raw[0], "e0", 0, True))
+        e.append(first_product(w2_raw[1], "e1", 1, True))
+        neighbours(0, 0)
+        e.append(first_product(w2_raw[2], "e2", 2, False))
+        e.append(first_product(w2_raw[3], "e3", 3, False))
+        neighbours(0, 1)
+        y.append(first_product(w1_raw[0], "y0", 4, False))
+        y.append(first_product(w1_raw[1], "y1", 5, False))
+        neighbours(0, 2)
+        edge_sum(0, 0)
+        y.append(first_product(w1_raw[2], "y2", 6, False))
+        edge_sum(0, 1)
+        y.append(first_product(w1_raw[3], "y3", 7, False))
+        nc.vector.tensor_copy(
+            out=w3_codes[:].bitcast(I32).rearrange("p (t m) -> p m t", t=4),
+            in_=w3_raw[:].bitcast(I32).rearrange("p (m t) -> p m t", t=4),
+        )
+        nc.vector.tensor_copy(
+            out=w3_plane[:].rearrange("p (t m) -> p m t", t=4), in_=w3_raw_plane[:].rearrange("p (m t) -> p m t", t=4)
+        )
+        neighbours(0, 3)
+        edge_sum(0, 2)
+        edge_sum(0, 3)
+        neighbours(1, 0)
+        neighbours(1, 1)
+        quantize_z(0)
+        edge_sum(1, 0)
+        edge_sum(1, 1)
+        neighbours(1, 2, "z_bf0")
+        neighbours(1, 3)
+        edge_sum(1, 2)
+        project(0, 0)
+        edge_sum(1, 3)
+        neighbours(2, 0)
+        neighbours(2, 1, "out_bf0")
+        quantize_z(1)
+        project(0, 1)
+        edge_sum(2, 0)
+        edge_sum(2, 1)
+        neighbours(2, 2, "z_bf1")
+        neighbours(2, 3, "out_bf1")
+        edge_sum(2, 2)
+        edge_sum(2, 3)
+        project(1, 0)
+        quantize_z(2)
+        project(2, 0, last=True)
+        for q in range(4):
+            queue = nc.scalar if q % 2 else nc.sync
+            queue.dma_start(
+                out=out_2[0, 4 * q : 4 * q + 4, :].bitcast(I32),
+                in_=out_plane[32 * q : 32 * q + 4, :].bitcast(I32),
+            )

@@ -18,7 +18,11 @@ MAX = mybir.AluOpType.max
 
 P = 128
 TILES = H // P
-CHUNKS = [(0, 256), (256, 128), (384, 128)]
+UNITS = [
+    (0, 0, 512),
+    (1, 0, 256), (2, 0, 256), (3, 0, 256),
+    (1, 256, 256), (2, 256, 256), (3, 256, 128), (3, 384, 128),
+]
 
 
 def tile_picked_wedgecv_relu_lo_kernel(
@@ -41,10 +45,13 @@ def tile_picked_wedgecv_relu_lo_kernel(
         w3_plane = sb([P, H], U8, "w3_plane")
         ident = sb([P, P], F32, "ident")
         warm = sb([P, 16], F32, "warm")
+        e = [sb([P, 2 * T if c == 0 else T], F32, "e%d" % c) for c in range(TILES)]
+        y = [sb([P, T], F32, "y%d" % c) for c in range(TILES)]
 
-        nc.vector.memset(x_plane[:].bitcast(I32), 0)
-        nc.vector.memset(w3_raw_plane[:].bitcast(I32), 0)
+        nc.gpsimd.memset(x_plane[:].bitcast(I32), 0)
+        nc.gpsimd.memset(w3_raw_plane[:].bitcast(I32), 0)
         nc.vector.memset(warm[:, 0:8], 0.0)
+        nc.vector.memset(e[0][:, T : 2 * T], 0.0)
         make_identity(nc, ident[:])
 
         def load_scales(queue, plane, scales):
@@ -63,73 +70,91 @@ def tile_picked_wedgecv_relu_lo_kernel(
 
         w2_raw = load_weight(w2, 0, 1, "w2_raw0")
         nc.sync.dma_start(out=x_codes[:].bitcast(I32), in_=x_words[0].rearrange("p n t -> p (n t)").bitcast(I32))
-        load_scales(nc.scalar, x_plane, x_scales)
+        load_scales(nc.sync, x_plane, x_scales)
         w2_raw = w2_raw + load_weight(w2, 1, 1, "w2_raw1")
+        nc.sync.dma_start(out=w3_raw[:].bitcast(I32), in_=w3_words[0].rearrange("p n t -> p (n t)").bitcast(I32))
         for offsets, pos in zip(lists, (pos1, pos2, pos3)):
             nc.sync.dma_start(offsets[:], pos)
         w2_raw = w2_raw + load_weight(w2, 2, 2, "w2_raw2")
         w1_raw = load_weight(w1, 0, 2, "w1_raw0") + load_weight(w1, 2, 2, "w1_raw2")
-        nc.sync.dma_start(out=w3_raw[:].bitcast(I32), in_=w3_words[0].rearrange("p n t -> p (n t)").bitcast(I32))
         load_scales(nc.sync, w3_raw_plane, w3_scales)
         nc.scalar.activation(warm[:, 8:16], warm[:, 0:8], RELU)
 
-        first_banks = [psum.tile([P, T], F32, name="first%d" % n) for n in range(3)]
-        sum_banks = [psum.tile([P, T], F32, name="sum%d" % n) for n in range(2)]
-        word_bank = psum.tile([P, T], F32, name="word_bank")
-        out_banks = [psum.tile([P, T], F32, name="out%d" % n) for n in range(2)]
+        banks = [psum.tile([P, T], F32, name="bank%d" % n) for n in range(8)]
+        first_banks = banks[0:3]
+        sum_banks = [banks[n] for n in (3, 4, 3, 4, 5, 6, 7, 4)]
+        word_banks = {0: banks[5], 2: banks[0], 3: banks[1]}
+        out_banks = [banks[6], banks[7], banks[2], banks[5]]
 
-        def first_product(raw, name, n, cast_on_vector):
-            grouped = sb([P, 4 * P], BF16, name + "_bf")
-            dst = grouped[:].rearrange("p (u q e j) -> p q j u e", u=2, e=2, j=4)
-            src = raw.rearrange("p j (q u e) -> p q j u e", u=2, e=2)
-            if cast_on_vector:
-                nc.vector.tensor_copy(out=dst, in_=src)
-            else:
-                nc.scalar.copy(out=dst, in_=src)
-            codes = sb([P, P], U32, name + "_codes")
-            plane = sb([P, P], U8, name + "_plane")
+        def first_products(raws, results, name, bank, cast_on_vector):
+            count = len(raws)
+            grouped = sb([P, count * 4 * P], BF16, name + "_bf")
+            for n, raw in enumerate(raws):
+                dst = grouped[:, n * 4 * P : (n + 1) * 4 * P].rearrange("p (u q e j) -> p q j u e", u=2, e=2, j=4)
+                src = raw.rearrange("p j (q u e) -> p q j u e", u=2, e=2)
+                if cast_on_vector:
+                    nc.vector.tensor_copy(out=dst, in_=src)
+                else:
+                    nc.scalar.copy(out=dst, in_=src)
+            codes = sb([P, count * P], U32, name + "_codes")
+            plane = sb([P, count * P], U8, name + "_plane")
             nc.vector.quantize_mx(out=codes[:].bitcast(FP8X4), scales=plane[:], in_=grouped[:])
-            bank = first_banks[n % 3]
-            nc.tensor.matmul_mx(
-                out=bank[:],
-                lhsT=codes[:].bitcast(FP8X4),
-                lhsT_scale=plane[:],
-                rhs=x_codes[:].bitcast(FP8X4),
-                rhs_scale=x_plane[:],
-                start=True,
-                stop=True,
-            )
-            rows = sb([P, T], F32, name)
-            nc.scalar.copy(out=rows[:], in_=bank[:])
-            return rows
+            for n, rows in enumerate(results):
+                acc = first_banks[(bank + n) % 3]
+                nc.tensor.matmul_mx(
+                    out=acc[:],
+                    lhsT=codes[:, n * P : (n + 1) * P].bitcast(FP8X4),
+                    lhsT_scale=plane[:, n * P : (n + 1) * P],
+                    rhs=x_codes[:].bitcast(FP8X4),
+                    rhs_scale=x_plane[:],
+                    start=True,
+                    stop=True,
+                )
+                nc.scalar.copy(out=rows[:, 0:T], in_=acc[:])
 
-        rings = [[sb([P, 256], F32, "ring%d_%d" % (d, n)) for n in range(2)] for d in range(4)]
-        z_turned = [sb([P, 4 * width], BF16, "z_turned%d" % n) for n, (start, width) in enumerate(CHUNKS)]
+        z_turned = [sb([P, 4 * 256], BF16, "z_turned%d" % n) for n in range(2)]
+        results = [sb([P, 2 * T], F32, "result%d" % n) for n in range(2)]
         out_codes = sb([P, T], U32, "out_codes")
         out_plane = sb([P, T], U8, "out_plane")
-        e = []
-        y = []
+        got = {}
         largest = {}
         z_q = {}
 
-        def neighbours(chunk, c, behind=None):
-            start, width = CHUNKS[chunk]
-            turn = (chunk * TILES + c) % 2
-            got = [rings[d][turn][:, 0:width] for d in range(3)]
-            if behind is not None:
-                held = sb([P, width], F32, "held%d_%d" % (chunk, c), tag=behind)
-                got[0] = held[:]
-            for d in range(3):
-                nc.vector.tensor_copy(got[d], e[c][:].indirect(lists[d][:, start // 16 : (start + width) // 16]))
-            pair = rings[3][turn][:, 0:width]
-            nc.vector.tensor_tensor(pair, got[0], got[1], MAX)
-            top = sb([P, width], F32, "top%d_%d" % (chunk, c))
-            nc.vector.tensor_tensor(top[:], pair, got[2], MAX)
-            largest[(chunk, c)] = top
+        reuse = {"g0": ("pair", 2), "g1": ("g0", 1), "g2": ("g2", 1), "pair": ("g1", 1)}
 
-        def edge_sum(chunk, c):
-            start, width = CHUNKS[chunk]
-            bank = sum_banks[(chunk * TILES + c) % 2]
+        def place(kind, unit):
+            width = UNITS[unit][2]
+            if (kind, unit) not in got:
+                older, back = reuse[kind]
+                if unit >= back:
+                    got[(kind, unit)] = got[(older, unit - back)][:, 0:width]
+                else:
+                    got[(kind, unit)] = sb([P, width], F32, "%s_%d" % (kind, unit))[:]
+            return got[(kind, unit)]
+
+        def hold(tag, steps):
+            held = sb([P, len(steps) * T], F32, "held_" + tag, tag=tag)
+            for n, (kind, unit) in enumerate(steps):
+                got[(kind, unit)] = held[:, n * T : n * T + UNITS[unit][2]]
+
+        def gather(unit, d):
+            c, start, width = UNITS[unit]
+            nc.vector.tensor_copy(
+                place("g%d" % d, unit), e[c][:].indirect(lists[d][:, start // 16 : (start + width) // 16])
+            )
+
+        def first_max(unit):
+            nc.vector.tensor_tensor(place("pair", unit), got[("g0", unit)], got[("g1", unit)], MAX)
+
+        def second_max(unit):
+            width = UNITS[unit][2]
+            top = sb([P, width], F32, "top%d" % unit)
+            nc.vector.tensor_tensor(top[:], got[("pair", unit)], got[("g2", unit)], MAX)
+            largest[unit] = top
+
+        def edge_sum(unit):
+            c, start, width = UNITS[unit]
+            bank = sum_banks[unit]
             for b in range(width // P):
                 cols = slice(b * P, (b + 1) * P)
                 nc.tensor.matmul(
@@ -137,113 +162,108 @@ def tile_picked_wedgecv_relu_lo_kernel(
                     start=True, stop=False, is_transpose=True,
                 )
                 nc.tensor.matmul(
-                    bank[:, cols], largest[(chunk, c)][:, cols], ident[:],
+                    bank[:, cols], largest[unit][:, cols], ident[:],
                     start=False, stop=True, is_transpose=True,
                 )
-            dst = z_turned[chunk][:].rearrange("v (b u c r) -> v c b u r", u=2, c=TILES, r=64)[:, c, :, :, :]
-            src = bank[:, 0:width].rearrange("v (b u r) -> v b u r", u=2, r=64)
-            nc.scalar.activation(dst, src, RELU)
+            for first in range(start, start + width, 256):
+                count = min(256, start + width - first) // P
+                b = first % 256 // P
+                view = z_turned[first // 256][:].rearrange("v (b u c r) -> v c b u r", u=2, c=TILES, r=64)
+                src = bank[:, first - start : first - start + count * P].rearrange("v (b u r) -> v b u r", u=2, r=64)
+                nc.scalar.activation(view[:, c, b : b + count, :, :], src, RELU)
 
-        def quantize_z(chunk):
-            start, width = CHUNKS[chunk]
-            words = z_turned[chunk][:].bitcast(F32)
-            for n in range(2 * width // P):
-                nc.tensor.transpose(word_bank[:, n * P : (n + 1) * P], words[:, n * P : (n + 1) * P], ident[:])
-            grouped = sb([P, 4 * width], BF16, "z_bf%d" % chunk)
+        def quantize_z(block, count):
+            words = z_turned[block // 2][:].bitcast(F32)
+            bank = word_banks[block]
+            for n in range(2 * count):
+                at = (block % 2 * 2 + n) * P
+                nc.tensor.transpose(bank[:, n * P : (n + 1) * P], words[:, at : at + P], ident[:])
+            grouped = sb([P, count * T], BF16, "z_bf%d" % block)
             nc.scalar.copy(
                 out=grouped[:].bitcast(F32).rearrange("p (b v u) -> p b v u", v=P, u=2),
-                in_=word_bank[:, 0 : 2 * width].rearrange("p (b u v) -> p b v u", v=P, u=2),
+                in_=bank[:, 0 : 2 * count * P].rearrange("p (b u v) -> p b v u", v=P, u=2),
             )
-            codes = sb([P, width], U32, "z_codes%d" % chunk)
-            plane = sb([P, width], U8, "z_plane%d" % chunk)
+            codes = sb([P, count * P], U32, "z_codes%d" % block)
+            plane = sb([P, count * P], U8, "z_plane%d" % block)
             nc.vector.quantize_mx(out=codes[:].bitcast(FP8X4), scales=plane[:], in_=grouped[:])
-            z_q[chunk] = (codes, plane)
+            for n in range(count):
+                z_q[block + n] = (codes[:, n * P : (n + 1) * P], plane[:, n * P : (n + 1) * P])
 
-        def project(chunk, b, last=False):
-            start, width = CHUNKS[chunk]
-            block = start // P + b
-            codes, plane = z_q[chunk]
-            bank = out_banks[block % 2]
+        def project(block):
+            codes, plane = z_q[block]
+            bank = out_banks[block]
+            second = banks[3] if block == 3 else bank
             for t in range(4):
                 nc.tensor.matmul_mx(
-                    out=bank[:, t * P : (t + 1) * P],
+                    out=(bank if t < 2 else second)[:, t * P : (t + 1) * P],
                     lhsT=w3_codes[:, t * P : (t + 1) * P].bitcast(FP8X4),
                     lhsT_scale=w3_plane[:, t * P : (t + 1) * P],
-                    rhs=codes[:, b * P : (b + 1) * P].bitcast(FP8X4),
-                    rhs_scale=plane[:, b * P : (b + 1) * P],
+                    rhs=codes.bitcast(FP8X4),
+                    rhs_scale=plane,
                     start=True,
                     stop=True,
                 )
-            cols = slice(block * P, (block + 1) * P)
-            result = sb([P, T], F32, "result%d" % block)
-            grouped = sb([P, T], BF16, "out_bf%d" % block)
-            nc.scalar.copy(out=result[:], in_=bank[:])
-            nc.sync.dma_start(
-                out=out_0.rearrange("(p t) v -> p t v", t=4)[:, :, cols],
-                in_=result[:].rearrange("p (t v) -> p t v", t=4),
-            )
-            if last:
-                nc.vector.tensor_copy(
-                    out=grouped[:].rearrange("p (s i t) -> p s t i", i=4, t=4),
-                    in_=result[:].rearrange("p (t s i) -> p s t i", i=4, t=4),
-                )
+            result = results[block // 2][:, block % 2 * T : (block % 2 + 1) * T]
+            if block == 3:
+                nc.scalar.copy(out=result[:, 0:256], in_=bank[:, 0:256])
+                nc.vector.tensor_copy(out=result[:, 256:512], in_=second[:, 256:512])
             else:
-                nc.scalar.copy(
-                    out=grouped[:].rearrange("p (v t) -> p v t", t=4),
-                    in_=bank[:].rearrange("p (t v) -> p v t", t=4),
-                )
+                nc.scalar.copy(out=result, in_=bank[:])
+            nc.sync.dma_start(
+                out=out_0.rearrange("(p t) v -> p t v", t=4)[:, :, block * P : (block + 1) * P],
+                in_=result.rearrange("p (t v) -> p t v", t=4),
+            )
+
+        def hand_on(block, count):
+            cols = slice(block * P, (block + count) * P)
+            result = results[block // 2][:, block % 2 * T : (block % 2 + count) * T]
+            grouped = sb([P, count * T], BF16, "out_bf%d" % block)
+            nc.vector.tensor_copy(
+                out=grouped[:].rearrange("p (b s i t) -> p b s t i", b=count, i=4, t=4),
+                in_=result.rearrange("p (b t s i) -> p b s t i", b=count, i=4, t=4),
+            )
             nc.vector.quantize_mx(out=out_codes[:, cols].bitcast(FP8X4), scales=out_plane[:, cols], in_=grouped[:])
             nc.sync.dma_start(
                 out=out_1[0].rearrange("p n t -> p (n t)").bitcast(I32)[:, cols],
                 in_=out_codes[:, cols].bitcast(I32),
             )
 
-        e.append(first_product(w2_raw[0], "e0", 0, True))
-        e.append(first_product(w2_raw[1], "e1", 1, True))
-        neighbours(0, 0)
-        e.append(first_product(w2_raw[2], "e2", 2, False))
-        e.append(first_product(w2_raw[3], "e3", 3, False))
-        neighbours(0, 1)
-        y.append(first_product(w1_raw[0], "y0", 4, False))
-        y.append(first_product(w1_raw[1], "y1", 5, False))
-        neighbours(0, 2)
-        edge_sum(0, 0)
-        y.append(first_product(w1_raw[2], "y2", 6, False))
-        edge_sum(0, 1)
-        y.append(first_product(w1_raw[3], "y3", 7, False))
+        first_products(w2_raw[0:1], e[0:1], "w2a", 0, True)
+        first_products(w2_raw[1:2], e[1:2], "w2b", 1, True)
         nc.vector.tensor_copy(
-            out=w3_codes[:].bitcast(I32).rearrange("p (t m) -> p m t", t=4),
-            in_=w3_raw[:].bitcast(I32).rearrange("p (m t) -> p m t", t=4),
+            out=w3_codes[:].bitcast(I32).rearrange("p (t s i) -> p s t i", t=4, i=4),
+            in_=w3_raw[:].bitcast(I32).rearrange("p (s i t) -> p s t i", t=4, i=4),
         )
+        first_products(w2_raw[2:4], e[2:4], "w2c", 2, False)
+        first_products(w1_raw, y, "w1", 1, False)
         nc.vector.tensor_copy(
-            out=w3_plane[:].rearrange("p (t m) -> p m t", t=4), in_=w3_raw_plane[:].rearrange("p (m t) -> p m t", t=4)
+            out=w3_plane[:].rearrange("p (t s i) -> p s t i", t=4, i=16),
+            in_=w3_raw_plane[:].rearrange("p (s i t) -> p s t i", t=4, i=16),
         )
-        neighbours(0, 3)
-        edge_sum(0, 2)
-        edge_sum(0, 3)
-        neighbours(1, 0)
-        neighbours(1, 1)
-        quantize_z(0)
-        edge_sum(1, 0)
-        edge_sum(1, 1)
-        neighbours(1, 2, "z_bf0")
-        neighbours(1, 3)
-        edge_sum(1, 2)
-        project(0, 0)
-        edge_sum(1, 3)
-        neighbours(2, 0)
-        neighbours(2, 1, "out_bf0")
-        quantize_z(1)
-        project(0, 1)
-        edge_sum(2, 0)
-        edge_sum(2, 1)
-        neighbours(2, 2, "z_bf1")
-        neighbours(2, 3, "out_bf1")
-        edge_sum(2, 2)
-        edge_sum(2, 3)
-        project(1, 0)
-        quantize_z(2)
-        project(2, 0, last=True)
+        hold("w2c_bf", [("g2", 0), ("pair", 0), ("g0", 1)])
+        hold("w1_bf", [("g2", 1), ("pair", 1), ("g0", 2)])
+        for unit in range(len(UNITS)):
+            gather(unit, 0)
+            if unit > 0:
+                second_max(unit - 1)
+                edge_sum(unit - 1)
+            if unit == 4:
+                quantize_z(0, 2)
+                hold("z_bf0", [("g2", 5), ("pair", 5), ("g0", 6)])
+                project(0)
+                project(1)
+            gather(unit, 1)
+            gather(unit, 2)
+            first_max(unit)
+        second_max(7)
+        quantize_z(2, 1)
+        edge_sum(7)
+        quantize_z(3, 1)
+        hand_on(0, 2)
+        project(2)
+        project(3)
+        hand_on(2, 1)
+        hand_on(3, 1)
         for q in range(4):
             queue = nc.scalar if q % 2 else nc.sync
             queue.dma_start(

@@ -15,14 +15,11 @@ U8 = mybir.dt.uint8
 FP8X4 = mybir.dt.float8_e4m3fn_x4
 RELU = mybir.ActivationFunctionType.Relu
 MAX = mybir.AluOpType.max
+SUBTRACT = mybir.AluOpType.subtract
 
 P = 128
 TILES = H // P
-UNITS = [
-    (0, 0, 512),
-    (1, 0, 256), (2, 0, 256), (3, 0, 256),
-    (1, 256, 256), (2, 256, 256), (3, 256, 128), (3, 384, 128),
-]
+UNITS = [(c, 0, 256) for c in range(4)] + [(c, 256, 256) for c in range(3)] + [(3, 256, 128), (3, 384, 128)]
 
 
 def tile_picked_wedgecv_relu_lo_kernel(
@@ -45,13 +42,12 @@ def tile_picked_wedgecv_relu_lo_kernel(
         w3_plane = sb([P, H], U8, "w3_plane")
         ident = sb([P, P], F32, "ident")
         warm = sb([P, 16], F32, "warm")
-        e = [sb([P, 2 * T if c == 0 else T], F32, "e%d" % c) for c in range(TILES)]
+        e = [sb([P, T], F32, "e%d" % c) for c in range(TILES)]
         y = [sb([P, T], F32, "y%d" % c) for c in range(TILES)]
 
         nc.gpsimd.memset(x_plane[:].bitcast(I32), 0)
         nc.gpsimd.memset(w3_raw_plane[:].bitcast(I32), 0)
         nc.vector.memset(warm[:, 0:8], 0.0)
-        nc.vector.memset(e[0][:, T : 2 * T], 0.0)
         make_identity(nc, ident[:])
 
         def load_scales(queue, plane, scales):
@@ -82,7 +78,7 @@ def tile_picked_wedgecv_relu_lo_kernel(
 
         banks = [psum.tile([P, T], F32, name="bank%d" % n) for n in range(8)]
         first_banks = banks[0:3]
-        sum_banks = [banks[n] for n in (3, 4, 3, 4, 5, 6, 7, 4)]
+        sum_banks = [banks[n] for n in (3, 4, 3, 4, 5, 3, 4, 3, 4)]
         word_banks = {0: banks[5], 2: banks[0], 3: banks[1]}
         out_banks = [banks[6], banks[7], banks[2], banks[5]]
 
@@ -99,6 +95,20 @@ def tile_picked_wedgecv_relu_lo_kernel(
             codes = sb([P, count * P], U32, name + "_codes")
             plane = sb([P, count * P], U8, name + "_plane")
             nc.vector.quantize_mx(out=codes[:].bitcast(FP8X4), scales=plane[:], in_=grouped[:])
+            if name == "w2a":
+                for half, acc in enumerate((banks[0], banks[3])):
+                    cols = slice(half * 256, (half + 1) * 256)
+                    nc.tensor.matmul_mx(
+                        out=acc[:, 0:256],
+                        lhsT=codes[:].bitcast(FP8X4),
+                        lhsT_scale=plane[:],
+                        rhs=x_codes[:, cols].bitcast(FP8X4),
+                        rhs_scale=x_plane[:, cols],
+                        start=True,
+                        stop=True,
+                    )
+                    nc.scalar.copy(out=results[0][:, cols], in_=acc[:, 0:256])
+                return
             for n, rows in enumerate(results):
                 acc = first_banks[(bank + n) % 3]
                 nc.tensor.matmul_mx(
@@ -120,12 +130,12 @@ def tile_picked_wedgecv_relu_lo_kernel(
         largest = {}
         z_q = {}
 
-        reuse = {"g0": ("pair", 2), "g1": ("g0", 1), "g2": ("g2", 1), "pair": ("g1", 1)}
+        reuse = {"g0": ("g1", 2), "g1": ("g0", 2)}
 
         def place(kind, unit):
             width = UNITS[unit][2]
             if (kind, unit) not in got:
-                older, back = reuse[kind]
+                older, back = reuse.get(kind, (kind, len(UNITS)))
                 if unit >= back:
                     got[(kind, unit)] = got[(older, unit - back)][:, 0:width]
                 else:
@@ -133,9 +143,9 @@ def tile_picked_wedgecv_relu_lo_kernel(
             return got[(kind, unit)]
 
         def hold(tag, steps):
-            held = sb([P, len(steps) * T], F32, "held_" + tag, tag=tag)
+            held = sb([P, len(steps) * 256], F32, "held_" + tag, tag=tag)
             for n, (kind, unit) in enumerate(steps):
-                got[(kind, unit)] = held[:, n * T : n * T + UNITS[unit][2]]
+                got[(kind, unit)] = held[:, n * 256 : n * 256 + UNITS[unit][2]]
 
         def gather(unit, d):
             c, start, width = UNITS[unit]
@@ -150,7 +160,18 @@ def tile_picked_wedgecv_relu_lo_kernel(
             width = UNITS[unit][2]
             top = sb([P, width], F32, "top%d" % unit)
             nc.vector.tensor_tensor(top[:], got[("pair", unit)], got[("g2", unit)], MAX)
-            largest[unit] = top
+            largest[unit] = [top[:]]
+
+        def excess(unit):
+            c, start, width = UNITS[unit]
+            nc.vector.tensor_tensor(
+                place("diff", unit),
+                e[c][:].indirect(lists[2][:, start // 16 : (start + width) // 16]),
+                got[("pair", unit)],
+                SUBTRACT,
+            )
+            nc.scalar.activation(place("lift", unit), got[("diff", unit)], RELU)
+            largest[unit] = [got[("pair", unit)], got[("lift", unit)]]
 
         def edge_sum(unit):
             c, start, width = UNITS[unit]
@@ -161,10 +182,11 @@ def tile_picked_wedgecv_relu_lo_kernel(
                     bank[:, cols], y[c][:, start + b * P : start + (b + 1) * P], ident[:],
                     start=True, stop=False, is_transpose=True,
                 )
-                nc.tensor.matmul(
-                    bank[:, cols], largest[unit][:, cols], ident[:],
-                    start=False, stop=True, is_transpose=True,
-                )
+                for n, term in enumerate(largest[unit]):
+                    nc.tensor.matmul(
+                        bank[:, cols], term[:, cols], ident[:],
+                        start=False, stop=n == len(largest[unit]) - 1, is_transpose=True,
+                    )
             for first in range(start, start + width, 256):
                 count = min(256, start + width - first) // P
                 b = first % 256 // P
@@ -192,7 +214,7 @@ def tile_picked_wedgecv_relu_lo_kernel(
         def project(block):
             codes, plane = z_q[block]
             bank = out_banks[block]
-            second = banks[3] if block == 3 else bank
+            second = banks[6] if block == 3 else bank
             for t in range(4):
                 nc.tensor.matmul_mx(
                     out=(bank if t < 2 else second)[:, t * P : (t + 1) * P],
@@ -240,24 +262,27 @@ def tile_picked_wedgecv_relu_lo_kernel(
             out=w3_plane[:].rearrange("p (t s i) -> p s t i", t=4, i=16),
             in_=w3_raw_plane[:].rearrange("p (s i t) -> p s t i", t=4, i=16),
         )
-        hold("w2c_bf", [("g2", 0), ("pair", 0), ("g0", 1)])
-        hold("w1_bf", [("g2", 1), ("pair", 1), ("g0", 2)])
-        for unit in range(len(UNITS)):
-            gather(unit, 0)
-            if unit > 0:
-                second_max(unit - 1)
-                edge_sum(unit - 1)
-            if unit == 4:
+        hold("w2c_bf", [("g1", 1), ("diff", 0)])
+        hold("w1_bf", [("g0", 3), ("pair", 2), ("g1", 3)])
+        gather(0, 0)
+        gather(0, 1)
+        for unit in range(8):
+            gather(unit + 1, 0)
+            first_max(unit)
+            gather(unit + 1, 1)
+            excess(unit)
+            edge_sum(unit)
+            if unit == 3:
                 quantize_z(0, 2)
-                hold("z_bf0", [("g2", 5), ("pair", 5), ("g0", 6)])
+                hold("z_turned0", [("lift", 4), ("lift", 5)])
+                hold("z_bf0", [("diff", 5), ("g0", 7), ("pair", 6), ("g1", 7)])
                 project(0)
                 project(1)
-            gather(unit, 1)
-            gather(unit, 2)
-            first_max(unit)
-        second_max(7)
+        gather(8, 2)
+        first_max(8)
+        second_max(8)
         quantize_z(2, 1)
-        edge_sum(7)
+        edge_sum(8)
         quantize_z(3, 1)
         hand_on(0, 2)
         project(2)

@@ -68,11 +68,12 @@ def tile_picked_wedgecv_relu_lo_kernel(
         nc.sync.dma_start(out=x_codes[:].bitcast(I32), in_=x_words[0].rearrange("p n t -> p (n t)").bitcast(I32))
         load_scales(nc.sync, x_plane, x_scales)
         w2_raw = w2_raw + load_weight(w2, 1, 1, "w2_raw1")
-        nc.sync.dma_start(out=w3_raw[:].bitcast(I32), in_=w3_words[0].rearrange("p n t -> p (n t)").bitcast(I32))
-        for offsets, pos in zip(lists, (pos1, pos2, pos3)):
-            nc.sync.dma_start(offsets[:], pos)
+        nc.sync.dma_start(lists[0][:], pos1)
+        nc.sync.dma_start(lists[1][:], pos2)
         w2_raw = w2_raw + load_weight(w2, 2, 2, "w2_raw2")
+        nc.sync.dma_start(lists[2][:], pos3)
         w1_raw = load_weight(w1, 0, 2, "w1_raw0") + load_weight(w1, 2, 2, "w1_raw2")
+        nc.sync.dma_start(out=w3_raw[:].bitcast(I32), in_=w3_words[0].rearrange("p n t -> p (n t)").bitcast(I32))
         load_scales(nc.sync, w3_raw_plane, w3_scales)
         nc.scalar.activation(warm[:, 8:16], warm[:, 0:8], RELU)
 
@@ -252,12 +253,12 @@ def tile_picked_wedgecv_relu_lo_kernel(
 
         first_products(w2_raw[0:1], e[0:1], "w2a", 0, True)
         first_products(w2_raw[1:2], e[1:2], "w2b", 1, True)
+        first_products(w2_raw[2:4], e[2:4], "w2c", 2, False)
+        first_products(w1_raw, y, "w1", 1, False)
         nc.vector.tensor_copy(
             out=w3_codes[:].bitcast(I32).rearrange("p (t s i) -> p s t i", t=4, i=4),
             in_=w3_raw[:].bitcast(I32).rearrange("p (s i t) -> p s t i", t=4, i=4),
         )
-        first_products(w2_raw[2:4], e[2:4], "w2c", 2, False)
-        first_products(w1_raw, y, "w1", 1, False)
         nc.vector.tensor_copy(
             out=w3_plane[:].rearrange("p (t s i) -> p s t i", t=4, i=16),
             in_=w3_raw_plane[:].rearrange("p (s i t) -> p s t i", t=4, i=16),
@@ -275,7 +276,7 @@ def tile_picked_wedgecv_relu_lo_kernel(
             if unit == 3:
                 quantize_z(0, 2)
                 hold("z_turned0", [("lift", 4), ("lift", 5)])
-                hold("z_bf0", [("diff", 5), ("g0", 7), ("pair", 6), ("g1", 7)])
+                hold("z_bf0", [("g0", 7), ("pair", 6), ("g1", 7)])
                 project(0)
                 project(1)
         gather(8, 2)

@@ -15,11 +15,11 @@ U8 = mybir.dt.uint8
 FP8X4 = mybir.dt.float8_e4m3fn_x4
 RELU = mybir.ActivationFunctionType.Relu
 MAX = mybir.AluOpType.max
+ADD = mybir.AluOpType.add
 SUBTRACT = mybir.AluOpType.subtract
 
 P = 128
-TILES = H // P
-UNITS = [(c, 0, 256) for c in range(4)] + [(c, 256, 256) for c in range(3)] + [(3, 256, 128), (3, 384, 128)]
+HALF = 256
 
 
 def tile_picked_wedgecv_relu_lo_kernel(
@@ -42,194 +42,179 @@ def tile_picked_wedgecv_relu_lo_kernel(
         w3_plane = sb([P, H], U8, "w3_plane")
         ident = sb([P, P], F32, "ident")
         warm = sb([P, 16], F32, "warm")
-        e = [sb([P, T], F32, "e%d" % c) for c in range(TILES)]
-        y = [sb([P, T], F32, "y%d" % c) for c in range(TILES)]
+        e = [sb([P, T], F32, "e%d" % c) for c in range(4)]
+        y_low = [sb([P, T], F32, "y%d" % c) for c in range(2)]
+        y_high = sb([P, 2 * T], F32, "y_high")
+        y = [y_low[0][:], y_low[1][:], y_high[:, 0:T], y_high[:, T : 2 * T]]
 
         nc.gpsimd.memset(x_plane[:].bitcast(I32), 0)
         nc.gpsimd.memset(w3_raw_plane[:].bitcast(I32), 0)
         nc.vector.memset(warm[:, 0:8], 0.0)
         make_identity(nc, ident[:])
 
-        def load_scales(queue, plane, scales):
+        def load_scales(plane, scales):
             for q in range(4):
-                queue.dma_start(
+                nc.sync.dma_start(
                     out=plane[32 * q : 32 * q + 4, :].bitcast(I32),
                     in_=scales[0, 4 * q : 4 * q + 4, :].bitcast(I32),
                 )
 
-        def load_weight(w, first, count, name):
-            raw = sb([P, 4, count * P], F32, name)
+        def load_weight(w, half, name):
+            raw = sb([P, 4, HALF], F32, name)
             nc.sync.dma_start(
-                out=raw[:], in_=w.rearrange("(p j) c -> p j c", j=4)[:, :, first * P : (first + count) * P]
+                out=raw[:], in_=w.rearrange("(p j) c -> p j c", j=4)[:, :, half * HALF : (half + 1) * HALF]
             )
-            return [raw[:, :, n * P : (n + 1) * P] for n in range(count)]
+            return raw[:].rearrange("p j (m t) -> p m j t", t=4)
 
-        w2_raw = load_weight(w2, 0, 1, "w2_raw0")
+        w2_raw = [load_weight(w2, 0, "w2_raw0")]
         nc.sync.dma_start(out=x_codes[:].bitcast(I32), in_=x_words[0].rearrange("p n t -> p (n t)").bitcast(I32))
-        load_scales(nc.sync, x_plane, x_scales)
-        w2_raw = w2_raw + load_weight(w2, 1, 1, "w2_raw1")
-        nc.sync.dma_start(lists[0][:], pos1)
-        nc.sync.dma_start(lists[1][:], pos2)
-        w2_raw = w2_raw + load_weight(w2, 2, 2, "w2_raw2")
-        nc.sync.dma_start(lists[2][:], pos3)
-        w1_raw = load_weight(w1, 0, 2, "w1_raw0") + load_weight(w1, 2, 2, "w1_raw2")
+        load_scales(x_plane, x_scales)
+        for d, pos in enumerate((pos1, pos2, pos3)):
+            nc.sync.dma_start(lists[d][:], pos)
+        w2_raw.append(load_weight(w2, 1, "w2_raw1"))
+        w1_raw = [load_weight(w1, half, "w1_raw%d" % half) for half in range(2)]
         nc.sync.dma_start(out=w3_raw[:].bitcast(I32), in_=w3_words[0].rearrange("p n t -> p (n t)").bitcast(I32))
-        load_scales(nc.sync, w3_raw_plane, w3_scales)
+        load_scales(w3_raw_plane, w3_scales)
         nc.scalar.activation(warm[:, 8:16], warm[:, 0:8], RELU)
 
         banks = [psum.tile([P, T], F32, name="bank%d" % n) for n in range(8)]
-        first_banks = banks[0:3]
-        sum_banks = [banks[n] for n in (3, 4, 3, 4, 5, 3, 4, 3, 4)]
-        word_banks = {0: banks[5], 2: banks[0], 3: banks[1]}
-        out_banks = [banks[6], banks[7], banks[2], banks[5]]
 
-        def first_products(raws, results, name, bank, cast_on_vector):
-            count = len(raws)
-            grouped = sb([P, count * 4 * P], BF16, name + "_bf")
-            for n, raw in enumerate(raws):
-                dst = grouped[:, n * 4 * P : (n + 1) * 4 * P].rearrange("p (u q e j) -> p q j u e", u=2, e=2, j=4)
-                src = raw.rearrange("p j (q u e) -> p q j u e", u=2, e=2)
-                if cast_on_vector:
-                    nc.vector.tensor_copy(out=dst, in_=src)
-                else:
-                    nc.scalar.copy(out=dst, in_=src)
-            codes = sb([P, count * P], U32, name + "_codes")
-            plane = sb([P, count * P], U8, name + "_plane")
-            nc.vector.quantize_mx(out=codes[:].bitcast(FP8X4), scales=plane[:], in_=grouped[:])
-            if name == "w2a":
-                for half, acc in enumerate((banks[0], banks[3])):
-                    cols = slice(half * 256, (half + 1) * 256)
-                    nc.tensor.matmul_mx(
-                        out=acc[:, 0:256],
-                        lhsT=codes[:].bitcast(FP8X4),
-                        lhsT_scale=plane[:],
-                        rhs=x_codes[:, cols].bitcast(FP8X4),
-                        rhs_scale=x_plane[:, cols],
-                        start=True,
-                        stop=True,
-                    )
-                    nc.scalar.copy(out=results[0][:, cols], in_=acc[:, 0:256])
-                return
-            for n, rows in enumerate(results):
-                acc = first_banks[(bank + n) % 3]
-                nc.tensor.matmul_mx(
-                    out=acc[:],
-                    lhsT=codes[:, n * P : (n + 1) * P].bitcast(FP8X4),
-                    lhsT_scale=plane[:, n * P : (n + 1) * P],
-                    rhs=x_codes[:].bitcast(FP8X4),
-                    rhs_scale=x_plane[:],
-                    start=True,
-                    stop=True,
+        def low_view(grouped):
+            return grouped.rearrange("p (m t j) -> p m j t", t=2, j=4)
+
+        def high_view(grouped, half):
+            return grouped.rearrange("p (t h m j) -> p h m j t", t=2, h=2, j=4)[:, half]
+
+        def quantize(grouped, name):
+            width = grouped.shape[1] // 4
+            codes = sb([P, width], U32, name + "_codes")
+            plane = sb([P, width], U8, name + "_plane")
+            nc.vector.quantize_mx(out=codes[:].bitcast(FP8X4), scales=plane[:], in_=grouped)
+            return [(codes[:, n * P : (n + 1) * P], plane[:, n * P : (n + 1) * P]) for n in range(width // P)]
+
+        def product(weight, acc, rows, cols):
+            nc.tensor.matmul_mx(
+                out=acc,
+                lhsT=weight[0].bitcast(FP8X4),
+                lhsT_scale=weight[1],
+                rhs=x_codes[:, cols].bitcast(FP8X4),
+                rhs_scale=x_plane[:, cols],
+                start=True,
+                stop=True,
+            )
+            nc.scalar.copy(out=rows[:, cols], in_=acc)
+
+        got = {}
+
+        def hold(tag, steps):
+            held = sb([P, len(steps) * HALF], F32, "held_%s_%s" % steps[0], tag=tag)
+            for n, step in enumerate(steps):
+                got[step] = held[:, n * HALF : (n + 1) * HALF]
+
+        def place(kind, unit):
+            if (kind, unit) not in got:
+                got[(kind, unit)] = sb([P, HALF], F32, "%s_%d" % (kind, unit))[:]
+            return got[(kind, unit)]
+
+        def gathers(*units):
+            return [("g%d" % d, unit) for unit in units for d in range(3)]
+
+        def window(c, d, first, width):
+            return e[c][:].indirect(lists[d][:, first // 16 : (first + width) // 16])
+
+        def larger(kind, unit, a, b):
+            nc.vector.tensor_tensor(place(kind, unit), got[(a, unit)], got[(b, unit)], MAX)
+
+        def gather_low(unit, d):
+            c, half = divmod(unit, 2)
+            nc.vector.tensor_copy(place("g%d" % d, unit), window(c, d, half * HALF, HALF))
+
+        def lift_low(unit):
+            nc.gpsimd.tensor_tensor(place("diff", unit), got[("g2", unit)], got[("pair", unit)], SUBTRACT)
+            nc.scalar.activation(place("lift", unit), got[("diff", unit)], RELU)
+
+        z_turned = [sb([P, 2 * HALF], BF16, "z_turned%d" % half) for half in range(2)]
+        z_bf = [sb([P, 4 * P], BF16, "z_bf%d" % block) for block in range(4)]
+
+        def sum_low(unit, bank):
+            c, half = divmod(unit, 2)
+            for b in range(2):
+                cols = slice(b * P, (b + 1) * P)
+                first = half * HALF + b * P
+                terms = [got[("lift", unit)][:, cols], got[("pair", unit)][:, cols], y[c][:, first : first + P]]
+                for n, term in enumerate(terms):
+                    nc.tensor.matmul(bank[:, cols], term, ident[:], start=n == 0, stop=n == 2, is_transpose=True)
+            nc.scalar.activation(
+                z_turned[half][:].rearrange("v (b c s) -> v c b s", b=2, c=2)[:, c],
+                bank[:, 0:HALF].rearrange("v (b s) -> v b s", b=2),
+                RELU,
+            )
+
+        def turn_low(half, bank):
+            words = z_turned[half][:].bitcast(F32)
+            for b in range(2):
+                nc.tensor.transpose(bank[:, b * P : (b + 1) * P], words[:, b * P : (b + 1) * P], ident[:])
+            for b in range(2):
+                nc.scalar.copy(
+                    out=z_bf[2 * half + b][:].bitcast(F32).rearrange("p (v u) -> p v u", u=2)[:, :, 0],
+                    in_=bank[:, b * P : (b + 1) * P],
                 )
-                nc.scalar.copy(out=rows[:, 0:T], in_=acc[:])
 
-        z_turned = [sb([P, 4 * 256], BF16, "z_turned%d" % n) for n in range(2)]
+        def gather_high(block, d, t):
+            nc.vector.tensor_copy(place("g%d" % d, 4 + block)[:, t * P : (t + 1) * P], window(2 + t, d, block * P, P))
+
+        def centre_high(block):
+            return y_high[:].rearrange("p (t v) -> p t v", t=2)[:, :, block * P : (block + 1) * P]
+
+        def by_tile(ap):
+            return ap.rearrange("p (t v) -> p t v", t=2)
+
+        def by_centre(ap):
+            return ap.rearrange("p (t v) -> p v t", t=2)
+
+        def z_high(block):
+            return z_bf[block][:].rearrange("p (v u t) -> p v u t", u=2, t=2)[:, :, 1, :]
+
+        def fetch_high(block):
+            unit = 4 + block
+            for d, t in ((0, 0), (0, 1), (1, 0), (1, 1), (2, 0)):
+                gather_high(block, d, t)
+            larger("pair", unit, "g0", "g1")
+            gather_high(block, 2, 1)
+            larger("top", unit, "pair", "g2")
+
+        def sum_high(block):
+            unit = 4 + block
+            nc.gpsimd.tensor_tensor(by_tile(place("sum", unit)), by_tile(got[("top", unit)]), centre_high(block), ADD)
+            nc.scalar.activation(z_high(block), by_centre(got[("sum", unit)]), RELU)
+
+        def edge_gather(block, t):
+            nc.vector.tensor_tensor(
+                place("g2", 4 + block)[:, t * P : (t + 1) * P],
+                window(2 + t, 2, block * P, P),
+                y[2 + t][:, block * P : (block + 1) * P],
+                ADD,
+            )
+
         results = [sb([P, 2 * T], F32, "result%d" % n) for n in range(2)]
         out_codes = sb([P, T], U32, "out_codes")
         out_plane = sb([P, T], U8, "out_plane")
-        got = {}
-        largest = {}
-        z_q = {}
 
-        reuse = {"g0": ("g1", 2), "g1": ("g0", 2)}
-
-        def place(kind, unit):
-            width = UNITS[unit][2]
-            if (kind, unit) not in got:
-                older, back = reuse.get(kind, (kind, len(UNITS)))
-                if unit >= back:
-                    got[(kind, unit)] = got[(older, unit - back)][:, 0:width]
-                else:
-                    got[(kind, unit)] = sb([P, width], F32, "%s_%d" % (kind, unit))[:]
-            return got[(kind, unit)]
-
-        def hold(tag, steps):
-            held = sb([P, len(steps) * 256], F32, "held_" + tag, tag=tag)
-            for n, (kind, unit) in enumerate(steps):
-                got[(kind, unit)] = held[:, n * 256 : n * 256 + UNITS[unit][2]]
-
-        def gather(unit, d):
-            c, start, width = UNITS[unit]
-            nc.vector.tensor_copy(
-                place("g%d" % d, unit), e[c][:].indirect(lists[d][:, start // 16 : (start + width) // 16])
-            )
-
-        def first_max(unit):
-            nc.vector.tensor_tensor(place("pair", unit), got[("g0", unit)], got[("g1", unit)], MAX)
-
-        def second_max(unit):
-            width = UNITS[unit][2]
-            top = sb([P, width], F32, "top%d" % unit)
-            nc.vector.tensor_tensor(top[:], got[("pair", unit)], got[("g2", unit)], MAX)
-            largest[unit] = [top[:]]
-
-        def excess(unit):
-            c, start, width = UNITS[unit]
-            nc.vector.tensor_tensor(
-                place("diff", unit),
-                e[c][:].indirect(lists[2][:, start // 16 : (start + width) // 16]),
-                got[("pair", unit)],
-                SUBTRACT,
-            )
-            nc.scalar.activation(place("lift", unit), got[("diff", unit)], RELU)
-            largest[unit] = [got[("pair", unit)], got[("lift", unit)]]
-
-        def edge_sum(unit):
-            c, start, width = UNITS[unit]
-            bank = sum_banks[unit]
-            for b in range(width // P):
-                cols = slice(b * P, (b + 1) * P)
-                nc.tensor.matmul(
-                    bank[:, cols], y[c][:, start + b * P : start + (b + 1) * P], ident[:],
-                    start=True, stop=False, is_transpose=True,
-                )
-                for n, term in enumerate(largest[unit]):
-                    nc.tensor.matmul(
-                        bank[:, cols], term[:, cols], ident[:],
-                        start=False, stop=n == len(largest[unit]) - 1, is_transpose=True,
-                    )
-            for first in range(start, start + width, 256):
-                count = min(256, start + width - first) // P
-                b = first % 256 // P
-                view = z_turned[first // 256][:].rearrange("v (b u c r) -> v c b u r", u=2, c=TILES, r=64)
-                src = bank[:, first - start : first - start + count * P].rearrange("v (b u r) -> v b u r", u=2, r=64)
-                nc.scalar.activation(view[:, c, b : b + count, :, :], src, RELU)
-
-        def quantize_z(block, count):
-            words = z_turned[block // 2][:].bitcast(F32)
-            bank = word_banks[block]
-            for n in range(2 * count):
-                at = (block % 2 * 2 + n) * P
-                nc.tensor.transpose(bank[:, n * P : (n + 1) * P], words[:, at : at + P], ident[:])
-            grouped = sb([P, count * T], BF16, "z_bf%d" % block)
-            nc.scalar.copy(
-                out=grouped[:].bitcast(F32).rearrange("p (b v u) -> p b v u", v=P, u=2),
-                in_=bank[:, 0 : 2 * count * P].rearrange("p (b u v) -> p b v u", v=P, u=2),
-            )
-            codes = sb([P, count * P], U32, "z_codes%d" % block)
-            plane = sb([P, count * P], U8, "z_plane%d" % block)
-            nc.vector.quantize_mx(out=codes[:].bitcast(FP8X4), scales=plane[:], in_=grouped[:])
-            for n in range(count):
-                z_q[block + n] = (codes[:, n * P : (n + 1) * P], plane[:, n * P : (n + 1) * P])
-
-        def project(block):
-            codes, plane = z_q[block]
-            bank = out_banks[block]
-            second = banks[6] if block == 3 else bank
+        def project(block, z_q, bank, second):
             for t in range(4):
                 nc.tensor.matmul_mx(
                     out=(bank if t < 2 else second)[:, t * P : (t + 1) * P],
                     lhsT=w3_codes[:, t * P : (t + 1) * P].bitcast(FP8X4),
                     lhsT_scale=w3_plane[:, t * P : (t + 1) * P],
-                    rhs=codes.bitcast(FP8X4),
-                    rhs_scale=plane,
+                    rhs=z_q[0].bitcast(FP8X4),
+                    rhs_scale=z_q[1],
                     start=True,
                     stop=True,
                 )
             result = results[block // 2][:, block % 2 * T : (block % 2 + 1) * T]
             if block == 3:
-                nc.scalar.copy(out=result[:, 0:256], in_=bank[:, 0:256])
-                nc.vector.tensor_copy(out=result[:, 256:512], in_=second[:, 256:512])
+                nc.scalar.copy(out=result[:, 0:HALF], in_=bank[:, 0:HALF])
+                nc.vector.tensor_copy(out=result[:, HALF:T], in_=second[:, HALF:T])
             else:
                 nc.scalar.copy(out=result, in_=bank[:])
             nc.sync.dma_start(
@@ -237,24 +222,43 @@ def tile_picked_wedgecv_relu_lo_kernel(
                 in_=result.rearrange("p (t v) -> p t v", t=4),
             )
 
-        def hand_on(block, count):
-            cols = slice(block * P, (block + count) * P)
-            result = results[block // 2][:, block % 2 * T : (block % 2 + count) * T]
-            grouped = sb([P, count * T], BF16, "out_bf%d" % block)
-            nc.vector.tensor_copy(
-                out=grouped[:].rearrange("p (b s i t) -> p b s t i", b=count, i=4, t=4),
-                in_=result.rearrange("p (b t s i) -> p b s t i", b=count, i=4, t=4),
+        def round_out(block, grouped, copy):
+            result = results[block // 2][:, block % 2 * T : (block % 2 + 1) * T]
+            copy(
+                out=grouped.rearrange("p (s i t) -> p s t i", i=4, t=4),
+                in_=result.rearrange("p (t s i) -> p s t i", i=4, t=4),
             )
-            nc.vector.quantize_mx(out=out_codes[:, cols].bitcast(FP8X4), scales=out_plane[:, cols], in_=grouped[:])
+
+        def hand_on(block, grouped):
+            cols = slice(block * P, (block + 1) * P)
+            nc.vector.quantize_mx(out=out_codes[:, cols].bitcast(FP8X4), scales=out_plane[:, cols], in_=grouped)
             nc.sync.dma_start(
                 out=out_1[0].rearrange("p n t -> p (n t)").bitcast(I32)[:, cols],
                 in_=out_codes[:, cols].bitcast(I32),
             )
 
-        first_products(w2_raw[0:1], e[0:1], "w2a", 0, True)
-        first_products(w2_raw[1:2], e[1:2], "w2b", 1, True)
-        first_products(w2_raw[2:4], e[2:4], "w2c", 2, False)
-        first_products(w1_raw, y, "w1", 1, False)
+        w2_bf0 = sb([P, T], BF16, "w2_bf0")
+        w2_bf1 = sb([P, T], BF16, "w2_bf1")
+        w2_bf23 = sb([P, 2 * T], BF16, "w2_bf23")
+        w1_bf = sb([P, 4 * T], BF16, "w1_bf")
+
+        nc.vector.tensor_copy(out=low_view(w2_bf0[:]), in_=w2_raw[0][:, :, :, 0:2])
+        w2_q = quantize(w2_bf0[:], "w2a")
+        for half in range(2):
+            product(w2_q[0], banks[half][:, 0:HALF], e[0][:], slice(half * HALF, (half + 1) * HALF))
+        nc.scalar.copy(out=high_view(w2_bf23[:], 0), in_=w2_raw[0][:, :, :, 2:4])
+        nc.scalar.copy(out=low_view(w2_bf1[:]), in_=w2_raw[1][:, :, :, 0:2])
+        nc.scalar.copy(out=high_view(w2_bf23[:], 1), in_=w2_raw[1][:, :, :, 2:4])
+        w2_q = w2_q + quantize(w2_bf1[:], "w2b") + quantize(w2_bf23[:], "w2c")
+        product(w2_q[1], banks[2][:], e[1][:], slice(0, T))
+        for half in range(2):
+            nc.scalar.copy(out=low_view(w1_bf[:, half * T : (half + 1) * T]), in_=w1_raw[half][:, :, :, 0:2])
+            nc.scalar.copy(out=high_view(w1_bf[:, 2 * T : 4 * T], half), in_=w1_raw[half][:, :, :, 2:4])
+        for c in (2, 3):
+            product(w2_q[c], banks[c + 1][:], e[c][:], slice(0, T))
+        w1_q = quantize(w1_bf[:], "w1")
+        for c, bank in enumerate((0, 1, 2, 5)):
+            product(w1_q[c], banks[bank][:], y[c], slice(0, T))
         nc.vector.tensor_copy(
             out=w3_codes[:].bitcast(I32).rearrange("p (t s i) -> p s t i", t=4, i=4),
             in_=w3_raw[:].bitcast(I32).rearrange("p (s i t) -> p s t i", t=4, i=4),
@@ -263,33 +267,68 @@ def tile_picked_wedgecv_relu_lo_kernel(
             out=w3_plane[:].rearrange("p (t s i) -> p s t i", t=4, i=16),
             in_=w3_raw_plane[:].rearrange("p (s i t) -> p s t i", t=4, i=16),
         )
-        hold("w2c_bf", [("g1", 1), ("diff", 0)])
-        hold("w1_bf", [("g0", 3), ("pair", 2), ("g1", 3)])
-        gather(0, 0)
-        gather(0, 1)
-        for unit in range(8):
-            gather(unit + 1, 0)
-            first_max(unit)
-            gather(unit + 1, 1)
-            excess(unit)
-            edge_sum(unit)
-            if unit == 3:
-                quantize_z(0, 2)
-                hold("z_turned0", [("lift", 4), ("lift", 5)])
-                hold("z_bf0", [("g0", 7), ("pair", 6), ("g1", 7)])
-                project(0)
-                project(1)
-        gather(8, 2)
-        first_max(8)
-        second_max(8)
-        quantize_z(2, 1)
-        edge_sum(8)
-        quantize_z(3, 1)
-        hand_on(0, 2)
-        project(2)
-        project(3)
-        hand_on(2, 1)
-        hand_on(3, 1)
+
+        hold("w2_raw1", [("pair", 1), ("g2", 0), ("g2", 1)])
+        hold("w1_raw1", gathers(3, 4, 5) + [("lift", 0), ("lift", 1)])
+        for unit, d in ((0, 0), (0, 1), (1, 0)):
+            gather_low(unit, d)
+        larger("pair", 0, "g0", "g1")
+        gather_low(1, 1)
+        larger("pair", 1, "g0", "g1")
+        for unit in range(2):
+            gather_low(unit, 2)
+            lift_low(unit)
+        for unit in (2, 3):
+            for d in range(3):
+                gather_low(unit, d)
+            larger("pair", unit, "g0", "g1")
+            lift_low(unit)
+        sum_low(0, banks[6])
+        sum_low(2, banks[7])
+        turn_low(0, banks[0])
+        sum_low(1, banks[3])
+        sum_low(3, banks[4])
+        turn_low(1, banks[1])
+
+        fetch_high(0)
+        hold("z_turned0", [("sum", 4)])
+        sum_high(0)
+        fetch_high(1)
+        hold("top_4", [("sum", 5)])
+        sum_high(1)
+        z_q = quantize(z_bf[0][:], "z0")
+        hold("z_turned0", gathers(6))
+        fetch_high(2)
+        hold("top_5", [("sum", 6)])
+        sum_high(2)
+        project(0, z_q[0], banks[2], banks[2])
+        out_bf = {block: sb([P, T], BF16, "out_bf%d" % block)[:] for block in (0, 2, 3)}
+        round_out(0, out_bf[0], nc.scalar.copy)
+        z_q = quantize(z_bf[1][:], "z1")
+        hold("top_4", gathers(7))
+        for d, t in ((0, 0), (0, 1), (1, 0), (1, 1)):
+            gather_high(3, d, t)
+        edge_gather(3, 0)
+        larger("pair", 7, "g0", "g1")
+        edge_gather(3, 1)
+        project(1, z_q[0], banks[5], banks[5])
+        hold("top_5", [("sum", 7), ("rounded", 1)])
+        out_bf[1] = got[("rounded", 1)].bitcast(BF16)
+        round_out(1, out_bf[1], nc.scalar.copy)
+        nc.vector.tensor_tensor(by_tile(got[("sum", 7)]), by_tile(got[("pair", 7)]), centre_high(3), ADD)
+        z_q = quantize(z_bf[2][:], "z2")
+        nc.vector.scalar_tensor_tensor(
+            out=z_high(3), in0=by_centre(got[("sum", 7)]), scalar=0.0, in1=by_centre(got[("g2", 7)]), op0=MAX, op1=MAX
+        )
+        z_last = quantize(z_bf[3][:], "z3")
+        project(2, z_q[0], banks[6], banks[6])
+        hand_on(0, out_bf[0])
+        hand_on(1, out_bf[1])
+        round_out(2, out_bf[2], nc.vector.tensor_copy)
+        project(3, z_last[0], banks[7], banks[0])
+        hand_on(2, out_bf[2])
+        round_out(3, out_bf[3], nc.vector.tensor_copy)
+        hand_on(3, out_bf[3])
         for q in range(4):
             queue = nc.scalar if q % 2 else nc.sync
             queue.dma_start(

@@ -16,10 +16,19 @@ FP8X4 = mybir.dt.float8_e4m3fn_x4
 RELU = mybir.ActivationFunctionType.Relu
 MAX = mybir.AluOpType.max
 ADD = mybir.AluOpType.add
-SUBTRACT = mybir.AluOpType.subtract
 
 P = 128
 HALF = 256
+SPARE = 192
+UNITS = [
+    [(0, 0, T)],
+    [(1, 0, HALF)],
+    [(2, 0, HALF)],
+    [(3, 0, HALF)],
+    [(1, HALF, HALF)],
+    [(2, 2 * P, P), (3, 2 * P, P)],
+    [(2, 3 * P, P), (3, 3 * P, P)],
+]
 
 
 def tile_picked_wedgecv_relu_lo_kernel(
@@ -42,7 +51,7 @@ def tile_picked_wedgecv_relu_lo_kernel(
         w3_plane = sb([P, H], U8, "w3_plane")
         ident = sb([P, P], F32, "ident")
         warm = sb([P, 16], F32, "warm")
-        e = [sb([P, T], F32, "e%d" % c) for c in range(4)]
+        e = [sb([P, T + (SPARE if c == 0 else 0)], F32, "e%d" % c) for c in range(4)]
         y_low = [sb([P, T], F32, "y%d" % c) for c in range(2)]
         y_high = sb([P, 2 * T], F32, "y_high")
         y = [y_low[0][:], y_low[1][:], y_high[:, 0:T], y_high[:, T : 2 * T]]
@@ -50,6 +59,7 @@ def tile_picked_wedgecv_relu_lo_kernel(
         nc.gpsimd.memset(x_plane[:].bitcast(I32), 0)
         nc.gpsimd.memset(w3_raw_plane[:].bitcast(I32), 0)
         nc.vector.memset(warm[:, 0:8], 0.0)
+        nc.vector.memset(e[0][:, T : T + SPARE], 0.0)
         make_identity(nc, ident[:])
 
         def load_scales(plane, scales):
@@ -69,9 +79,10 @@ def tile_picked_wedgecv_relu_lo_kernel(
         w2_raw = [load_weight(w2, 0, "w2_raw0")]
         nc.sync.dma_start(out=x_codes[:].bitcast(I32), in_=x_words[0].rearrange("p n t -> p (n t)").bitcast(I32))
         load_scales(x_plane, x_scales)
-        for d, pos in enumerate((pos1, pos2, pos3)):
-            nc.sync.dma_start(lists[d][:], pos)
+        nc.sync.dma_start(lists[0][:], pos1)
+        nc.sync.dma_start(lists[1][:], pos2)
         w2_raw.append(load_weight(w2, 1, "w2_raw1"))
+        nc.sync.dma_start(lists[2][:], pos3)
         w1_raw = [load_weight(w1, half, "w1_raw%d" % half) for half in range(2)]
         nc.sync.dma_start(out=w3_raw[:].bitcast(I32), in_=w3_words[0].rearrange("p n t -> p (n t)").bitcast(I32))
         load_scales(w3_raw_plane, w3_scales)
@@ -92,7 +103,7 @@ def tile_picked_wedgecv_relu_lo_kernel(
             nc.vector.quantize_mx(out=codes[:].bitcast(FP8X4), scales=plane[:], in_=grouped)
             return [(codes[:, n * P : (n + 1) * P], plane[:, n * P : (n + 1) * P]) for n in range(width // P)]
 
-        def product(weight, acc, rows, cols):
+        def product(weight, acc, rows, cols, copy=nc.scalar.copy):
             nc.tensor.matmul_mx(
                 out=acc,
                 lhsT=weight[0].bitcast(FP8X4),
@@ -102,9 +113,12 @@ def tile_picked_wedgecv_relu_lo_kernel(
                 start=True,
                 stop=True,
             )
-            nc.scalar.copy(out=rows[:, cols], in_=acc)
+            copy(out=rows[:, cols], in_=acc)
 
         got = {}
+
+        def width(unit):
+            return sum(piece[2] for piece in UNITS[unit])
 
         def hold(tag, steps):
             held = sb([P, len(steps) * HALF], F32, "held_%s_%s" % steps[0], tag=tag)
@@ -113,58 +127,61 @@ def tile_picked_wedgecv_relu_lo_kernel(
 
         def place(kind, unit):
             if (kind, unit) not in got:
-                got[(kind, unit)] = sb([P, HALF], F32, "%s_%d" % (kind, unit))[:]
+                got[(kind, unit)] = sb([P, width(unit)], F32, "%s_%d" % (kind, unit))[:]
             return got[(kind, unit)]
 
         def gathers(*units):
             return [("g%d" % d, unit) for unit in units for d in range(3)]
 
-        def window(c, d, first, width):
-            return e[c][:].indirect(lists[d][:, first // 16 : (first + width) // 16])
+        def window(c, d, first, count):
+            return e[c][:].indirect(lists[d][:, first // 16 : (first + count) // 16])
+
+        def gather(unit, d, pieces=(0, 1)):
+            for n, (c, first, count) in enumerate(UNITS[unit]):
+                if n in pieces:
+                    nc.vector.tensor_copy(
+                        place("g%d" % d, unit)[:, n * count : (n + 1) * count], window(c, d, first, count)
+                    )
 
         def larger(kind, unit, a, b):
             nc.vector.tensor_tensor(place(kind, unit), got[(a, unit)], got[(b, unit)], MAX)
 
-        def gather_low(unit, d):
-            c, half = divmod(unit, 2)
-            nc.vector.tensor_copy(place("g%d" % d, unit), window(c, d, half * HALF, HALF))
+        z_turned = {0: sb([P, 2 * T], BF16, "z_turned0"), 2: sb([P, T], BF16, "z_turned2"), 3: sb([P, HALF], BF16, "z_turned3")}
+        z_bf = {0: sb([P, 2 * T], BF16, "z_bf0"), 2: sb([P, T], BF16, "z_bf2"), 3: sb([P, T], BF16, "z_bf3")}
 
-        def lift_low(unit):
-            nc.gpsimd.tensor_tensor(place("diff", unit), got[("g2", unit)], got[("pair", unit)], SUBTRACT)
-            nc.scalar.activation(place("lift", unit), got[("diff", unit)], RELU)
+        def turned(block):
+            if block < 2:
+                return z_turned[0][:, block * T : (block + 1) * T]
+            return z_turned[block][:]
 
-        z_turned = [sb([P, 2 * HALF], BF16, "z_turned%d" % half) for half in range(2)]
-        z_bf = [sb([P, 4 * P], BF16, "z_bf%d" % block) for block in range(4)]
+        def edge_sum(unit, bank, at=0):
+            top = got[("top", unit)]
+            for n, (c, first, count) in enumerate(UNITS[unit]):
+                for b in range(count // P):
+                    cols = slice(n * count + b * P, n * count + (b + 1) * P)
+                    acc = bank[:, at + cols.start : at + cols.stop]
+                    centre = y[c][:, first + b * P : first + (b + 1) * P]
+                    nc.tensor.matmul(acc, top[:, cols], ident[:], start=True, stop=False, is_transpose=True)
+                    nc.tensor.matmul(acc, centre, ident[:], start=False, stop=True, is_transpose=True)
 
-        def sum_low(unit, bank):
-            c, half = divmod(unit, 2)
-            for b in range(2):
-                cols = slice(b * P, (b + 1) * P)
-                first = half * HALF + b * P
-                terms = [got[("lift", unit)][:, cols], got[("pair", unit)][:, cols], y[c][:, first : first + P]]
-                for n, term in enumerate(terms):
-                    nc.tensor.matmul(bank[:, cols], term, ident[:], start=n == 0, stop=n == 2, is_transpose=True)
+        def relu_low_pair(c, bank):
             nc.scalar.activation(
-                z_turned[half][:].rearrange("v (b c s) -> v c b s", b=2, c=2)[:, c],
+                z_turned[0][:].rearrange("v (b c s) -> v c b s", b=2, c=4)[:, c],
                 bank[:, 0:HALF].rearrange("v (b s) -> v b s", b=2),
                 RELU,
             )
 
-        def turn_low(half, bank):
-            words = z_turned[half][:].bitcast(F32)
-            for b in range(2):
-                nc.tensor.transpose(bank[:, b * P : (b + 1) * P], words[:, b * P : (b + 1) * P], ident[:])
-            for b in range(2):
-                nc.scalar.copy(
-                    out=z_bf[2 * half + b][:].bitcast(F32).rearrange("p (v u) -> p v u", u=2)[:, :, 0],
-                    in_=bank[:, b * P : (b + 1) * P],
-                )
+        def relu_low(c, block, src):
+            nc.scalar.activation(turned(block)[:, c * P : (c + 1) * P], src, RELU)
 
-        def gather_high(block, d, t):
-            nc.vector.tensor_copy(place("g%d" % d, 4 + block)[:, t * P : (t + 1) * P], window(2 + t, d, block * P, P))
-
-        def centre_high(block):
-            return y_high[:].rearrange("p (t v) -> p t v", t=2)[:, :, block * P : (block + 1) * P]
+        def turn(block, count, bank):
+            words = z_turned[block][:].bitcast(F32)
+            for n in range(2 * count):
+                nc.tensor.transpose(bank[:, n * P : (n + 1) * P], words[:, n * P : (n + 1) * P], ident[:])
+            nc.scalar.copy(
+                out=z_bf[block][:].bitcast(F32).rearrange("p (b v u) -> p b v u", v=P, u=2),
+                in_=bank[:, 0 : 2 * count * P].rearrange("p (b u v) -> p b v u", v=P, u=2),
+            )
 
         def by_tile(ap):
             return ap.rearrange("p (t v) -> p t v", t=2)
@@ -172,27 +189,12 @@ def tile_picked_wedgecv_relu_lo_kernel(
         def by_centre(ap):
             return ap.rearrange("p (t v) -> p v t", t=2)
 
-        def z_high(block):
-            return z_bf[block][:].rearrange("p (v u t) -> p v u t", u=2, t=2)[:, :, 1, :]
-
-        def fetch_high(block):
-            unit = 4 + block
-            for d, t in ((0, 0), (0, 1), (1, 0), (1, 1), (2, 0)):
-                gather_high(block, d, t)
-            larger("pair", unit, "g0", "g1")
-            gather_high(block, 2, 1)
-            larger("top", unit, "pair", "g2")
-
-        def sum_high(block):
-            unit = 4 + block
-            nc.gpsimd.tensor_tensor(by_tile(place("sum", unit)), by_tile(got[("top", unit)]), centre_high(block), ADD)
-            nc.scalar.activation(z_high(block), by_centre(got[("sum", unit)]), RELU)
-
-        def edge_gather(block, t):
+        def edge_gather(unit, n):
+            c, first, count = UNITS[unit][n]
             nc.vector.tensor_tensor(
-                place("g2", 4 + block)[:, t * P : (t + 1) * P],
-                window(2 + t, 2, block * P, P),
-                y[2 + t][:, block * P : (block + 1) * P],
+                place("g2", unit)[:, n * count : (n + 1) * count],
+                window(c, 2, first, count),
+                y[c][:, first : first + count],
                 ADD,
             )
 
@@ -211,6 +213,8 @@ def tile_picked_wedgecv_relu_lo_kernel(
                     start=True,
                     stop=True,
                 )
+
+        def store(block, bank, second):
             result = results[block // 2][:, block % 2 * T : (block % 2 + 1) * T]
             if block == 3:
                 nc.scalar.copy(out=result[:, 0:HALF], in_=bank[:, 0:HALF])
@@ -244,8 +248,8 @@ def tile_picked_wedgecv_relu_lo_kernel(
 
         nc.vector.tensor_copy(out=low_view(w2_bf0[:]), in_=w2_raw[0][:, :, :, 0:2])
         w2_q = quantize(w2_bf0[:], "w2a")
-        for half in range(2):
-            product(w2_q[0], banks[half][:, 0:HALF], e[0][:], slice(half * HALF, (half + 1) * HALF))
+        for half, copy in enumerate((nc.scalar.copy, nc.vector.tensor_copy)):
+            product(w2_q[0], banks[half][:, 0:HALF], e[0][:], slice(half * HALF, (half + 1) * HALF), copy)
         nc.scalar.copy(out=high_view(w2_bf23[:], 0), in_=w2_raw[0][:, :, :, 2:4])
         nc.scalar.copy(out=low_view(w2_bf1[:]), in_=w2_raw[1][:, :, :, 0:2])
         nc.scalar.copy(out=high_view(w2_bf23[:], 1), in_=w2_raw[1][:, :, :, 2:4])
@@ -268,64 +272,91 @@ def tile_picked_wedgecv_relu_lo_kernel(
             in_=w3_raw_plane[:].rearrange("p (s i t) -> p s t i", t=4, i=16),
         )
 
-        hold("w2_raw1", [("pair", 1), ("g2", 0), ("g2", 1)])
-        hold("w1_raw1", gathers(3, 4, 5) + [("lift", 0), ("lift", 1)])
-        for unit, d in ((0, 0), (0, 1), (1, 0)):
-            gather_low(unit, d)
-        larger("pair", 0, "g0", "g1")
-        gather_low(1, 1)
-        larger("pair", 1, "g0", "g1")
-        for unit in range(2):
-            gather_low(unit, 2)
-            lift_low(unit)
-        for unit in (2, 3):
-            for d in range(3):
-                gather_low(unit, d)
+        third = sb([P, T], F32, "third", tag="w2_raw1")
+        got[("g2", 0)] = third[:]
+        hold("w1_raw1", gathers(2, 3, 4) + [("top", 1)] + gathers(5))
+        gather(0, 0)
+        for unit in range(4):
+            gather(unit, 1)
+            gather(unit, 2)
             larger("pair", unit, "g0", "g1")
-            lift_low(unit)
-        sum_low(0, banks[6])
-        sum_low(2, banks[7])
-        turn_low(0, banks[0])
-        sum_low(1, banks[3])
-        sum_low(3, banks[4])
-        turn_low(1, banks[1])
+            gather(unit + 1, 0)
+            larger("top", unit, "pair", "g2")
+        edge_sum(0, banks[6])
+        relu_low_pair(0, banks[6])
+        edge_sum(1, banks[7])
+        relu_low_pair(1, banks[7])
+        for block in (2, 3):
+            relu_low(0, block, banks[6][:, block * P : (block + 1) * P])
+        edge_sum(2, banks[3])
+        edge_sum(3, banks[3], HALF)
+        nc.scalar.activation(
+            z_turned[0][:].rearrange("v (b u q t) -> v u b q t", b=2, u=2, t=2)[:, 1],
+            banks[3][:].rearrange("v (t b q) -> v b q t", t=2, b=2),
+            RELU,
+        )
+        turn(0, 2, banks[0])
 
-        fetch_high(0)
-        hold("z_turned0", [("sum", 4)])
-        sum_high(0)
-        fetch_high(1)
-        hold("top_4", [("sum", 5)])
-        sum_high(1)
+        gather(4, 1)
+        gather(4, 2)
+        larger("pair", 4, "g0", "g1")
+        gather(5, 0, (0,))
+        larger("top", 4, "pair", "g2")
+        edge_sum(4, banks[0])
+        for block in (2, 3):
+            relu_low(1, block, banks[0][:, (block - 2) * P : (block - 1) * P])
+        nc.tensor.transpose(banks[1][:, 0:P], z_turned[3][:].bitcast(F32), ident[:])
+        nc.scalar.copy(out=z_bf[3][:].bitcast(F32).rearrange("p (v u) -> p v u", u=2)[:, :, 0], in_=banks[1][:, 0:P])
+
+        hold("top_4", [("top", 5)] + gathers(6))
+        gather(5, 0, (1,))
+        gather(5, 1)
+        gather(5, 2)
+        larger("pair", 5, "g0", "g1")
         z_q = quantize(z_bf[0][:], "z0")
-        hold("z_turned0", gathers(6))
-        fetch_high(2)
-        hold("top_5", [("sum", 6)])
-        sum_high(2)
         project(0, z_q[0], banks[2], banks[2])
-        out_bf = {block: sb([P, T], BF16, "out_bf%d" % block)[:] for block in (0, 2, 3)}
-        round_out(0, out_bf[0], nc.scalar.copy)
-        z_q = quantize(z_bf[1][:], "z1")
-        hold("top_4", gathers(7))
-        for d, t in ((0, 0), (0, 1), (1, 0), (1, 1)):
-            gather_high(3, d, t)
-        edge_gather(3, 0)
-        larger("pair", 7, "g0", "g1")
-        edge_gather(3, 1)
-        project(1, z_q[0], banks[5], banks[5])
-        hold("top_5", [("sum", 7), ("rounded", 1)])
-        out_bf[1] = got[("rounded", 1)].bitcast(BF16)
-        round_out(1, out_bf[1], nc.scalar.copy)
-        nc.vector.tensor_tensor(by_tile(got[("sum", 7)]), by_tile(got[("pair", 7)]), centre_high(3), ADD)
+        store(0, banks[2], banks[2])
+        larger("top", 5, "pair", "g2")
+        edge_sum(5, banks[7])
+        nc.scalar.activation(
+            z_turned[2][:, HALF:T].rearrange("v (q t) -> v q t", t=2),
+            banks[7][:, 0:HALF].rearrange("v (t q) -> v q t", t=2),
+            RELU,
+        )
+        turn(2, 1, banks[4])
+        project(1, z_q[1], banks[5], banks[5])
+        store(1, banks[5], banks[5])
+        out_bf = {block: sb([P, T], BF16, "out_bf%d" % block)[:] for block in (1, 2, 3)}
+
+        gather(6, 0)
+        gather(6, 1)
+        edge_gather(6, 0)
+        larger("pair", 6, "g0", "g1")
+        edge_gather(6, 1)
+        hold("z_turned2", [("sum", 6), ("rounded", 0)])
+        out_bf[0] = got[("rounded", 0)].bitcast(BF16)
+        nc.vector.tensor_tensor(
+            by_tile(got[("sum", 6)]), by_tile(got[("pair", 6)]), by_tile(y_high[:])[:, :, 3 * P : T], ADD
+        )
         z_q = quantize(z_bf[2][:], "z2")
         nc.vector.scalar_tensor_tensor(
-            out=z_high(3), in0=by_centre(got[("sum", 7)]), scalar=0.0, in1=by_centre(got[("g2", 7)]), op0=MAX, op1=MAX
+            out=z_bf[3][:].rearrange("p (v u t) -> p v u t", u=2, t=2)[:, :, 1, :],
+            in0=by_centre(got[("sum", 6)]),
+            scalar=0.0,
+            in1=by_centre(got[("g2", 6)]),
+            op0=MAX,
+            op1=MAX,
         )
         z_last = quantize(z_bf[3][:], "z3")
         project(2, z_q[0], banks[6], banks[6])
+        store(2, banks[6], banks[6])
+        round_out(0, out_bf[0], nc.scalar.copy)
+        round_out(1, out_bf[1], nc.vector.tensor_copy)
         hand_on(0, out_bf[0])
         hand_on(1, out_bf[1])
         round_out(2, out_bf[2], nc.vector.tensor_copy)
-        project(3, z_last[0], banks[7], banks[0])
+        project(3, z_last[0], banks[3], banks[0])
+        store(3, banks[3], banks[0])
         hand_on(2, out_bf[2])
         round_out(3, out_bf[3], nc.vector.tensor_copy)
         hand_on(3, out_bf[3])

@@ -50,7 +50,6 @@ def tile_picked_wedgecv_relu_lo_kernel(
         w3_codes = sb([P, H], U32, "w3_codes")
         w3_plane = sb([P, H], U8, "w3_plane")
         ident = sb([P, P], F32, "ident")
-        warm = sb([P, 16], F32, "warm")
         e = [sb([P, T + (SPARE if c == 0 else 0)], F32, "e%d" % c) for c in range(4)]
         y_low = [sb([P, T], F32, "y%d" % c) for c in range(2)]
         y_high = sb([P, 2 * T], F32, "y_high")
@@ -58,7 +57,6 @@ def tile_picked_wedgecv_relu_lo_kernel(
 
         nc.gpsimd.memset(x_plane[:].bitcast(I32), 0)
         nc.gpsimd.memset(w3_raw_plane[:].bitcast(I32), 0)
-        nc.vector.memset(warm[:, 0:8], 0.0)
         nc.vector.memset(e[0][:, T : T + SPARE], 0.0)
         make_identity(nc, ident[:])
 
@@ -86,7 +84,6 @@ def tile_picked_wedgecv_relu_lo_kernel(
         w1_raw = [load_weight(w1, half, "w1_raw%d" % half) for half in range(2)]
         nc.sync.dma_start(out=w3_raw[:].bitcast(I32), in_=w3_words[0].rearrange("p n t -> p (n t)").bitcast(I32))
         load_scales(w3_raw_plane, w3_scales)
-        nc.scalar.activation(warm[:, 8:16], warm[:, 0:8], RELU)
 
         banks = [psum.tile([P, T], F32, name="bank%d" % n) for n in range(8)]
 
@@ -96,9 +93,9 @@ def tile_picked_wedgecv_relu_lo_kernel(
         def high_view(grouped, half):
             return grouped.rearrange("p (t h m j) -> p h m j t", t=2, h=2, j=4)[:, half]
 
-        def quantize(grouped, name):
+        def quantize(grouped, name, tag=None):
             width = grouped.shape[1] // 4
-            codes = sb([P, width], U32, name + "_codes")
+            codes = sb([P, width], U32, name + "_codes", tag)
             plane = sb([P, width], U8, name + "_plane")
             nc.vector.quantize_mx(out=codes[:].bitcast(FP8X4), scales=plane[:], in_=grouped)
             return [(codes[:, n * P : (n + 1) * P], plane[:, n * P : (n + 1) * P]) for n in range(width // P)]
@@ -246,7 +243,8 @@ def tile_picked_wedgecv_relu_lo_kernel(
         w2_bf23 = sb([P, 2 * T], BF16, "w2_bf23")
         w1_bf = sb([P, 4 * T], BF16, "w1_bf")
 
-        nc.vector.tensor_copy(out=low_view(w2_bf0[:]), in_=w2_raw[0][:, :, :, 0:2])
+        nc.vector.tensor_copy(out=low_view(w2_bf0[:])[:, 0:40], in_=w2_raw[0][:, 0:40, :, 0:2])
+        nc.scalar.copy(out=low_view(w2_bf0[:])[:, 40:64], in_=w2_raw[0][:, 40:64, :, 0:2])
         w2_q = quantize(w2_bf0[:], "w2a")
         for half, copy in enumerate((nc.scalar.copy, nc.vector.tensor_copy)):
             product(w2_q[0], banks[half][:, 0:HALF], e[0][:], slice(half * HALF, (half + 1) * HALF), copy)
@@ -272,9 +270,18 @@ def tile_picked_wedgecv_relu_lo_kernel(
             in_=w3_raw_plane[:].rearrange("p (s i t) -> p s t i", t=4, i=16),
         )
 
-        third = sb([P, T], F32, "third", tag="w2_raw1")
-        got[("g2", 0)] = third[:]
-        hold("w1_raw1", gathers(2, 3, 4) + [("top", 1)] + gathers(5))
+        held = sb([P, 2 * T], F32, "held_first", tag="w2_raw1")
+        got[("g2", 0)] = held[:, 0:T]
+        got[("pair", 0)] = held[:, T : 2 * T]
+        hold("w1_raw1", gathers(2, 3) + [("top", 1), ("g0", 4)])
+        for later, earlier in (
+            (("g1", 4), ("g0", 3)),
+            (("g2", 4), ("g1", 3)),
+            (("g0", 5), ("g2", 3)),
+            (("g1", 5), ("g0", 4)),
+            (("g2", 5), ("g1", 4)),
+        ):
+            got[later] = got[earlier]
         gather(0, 0)
         for unit in range(4):
             gather(unit, 1)
@@ -333,12 +340,11 @@ def tile_picked_wedgecv_relu_lo_kernel(
         edge_gather(6, 0)
         larger("pair", 6, "g0", "g1")
         edge_gather(6, 1)
-        hold("z_turned2", [("sum", 6), ("rounded", 0)])
+        hold("z_turned2", [("rounded", 0)])
         out_bf[0] = got[("rounded", 0)].bitcast(BF16)
         nc.vector.tensor_tensor(
-            by_tile(got[("sum", 6)]), by_tile(got[("pair", 6)]), by_tile(y_high[:])[:, :, 3 * P : T], ADD
+            by_tile(place("sum", 6)), by_tile(got[("pair", 6)]), by_tile(y_high[:])[:, :, 3 * P : T], ADD
         )
-        z_q = quantize(z_bf[2][:], "z2")
         nc.vector.scalar_tensor_tensor(
             out=z_bf[3][:].rearrange("p (v u t) -> p v u t", u=2, t=2)[:, :, 1, :],
             in0=by_centre(got[("sum", 6)]),
@@ -347,7 +353,8 @@ def tile_picked_wedgecv_relu_lo_kernel(
             op0=MAX,
             op1=MAX,
         )
-        z_last = quantize(z_bf[3][:], "z3")
+        z_q = quantize(z_bf[2][:], "z2")
+        z_last = quantize(z_bf[3][:], "z3", "z_bf2")
         project(2, z_q[0], banks[6], banks[6])
         store(2, banks[6], banks[6])
         round_out(0, out_bf[0], nc.scalar.copy)

@@ -20,6 +20,7 @@ ADD = mybir.AluOpType.add
 P = 128
 HALF = 256
 SPARE = 192
+VECTOR_GROUPS = 40
 UNITS = [
     [(0, 0, T)],
     [(1, 0, HALF)],
@@ -94,11 +95,11 @@ def tile_picked_wedgecv_relu_lo_kernel(
             return grouped.rearrange("p (t h m j) -> p h m j t", t=2, h=2, j=4)[:, half]
 
         def quantize(grouped, name, tag=None):
-            width = grouped.shape[1] // 4
-            codes = sb([P, width], U32, name + "_codes", tag)
-            plane = sb([P, width], U8, name + "_plane")
+            words = grouped.shape[1] // 4
+            codes = sb([P, words], U32, name + "_codes", tag)
+            plane = sb([P, words], U8, name + "_plane")
             nc.vector.quantize_mx(out=codes[:].bitcast(FP8X4), scales=plane[:], in_=grouped)
-            return [(codes[:, n * P : (n + 1) * P], plane[:, n * P : (n + 1) * P]) for n in range(width // P)]
+            return [(codes[:, n * P : (n + 1) * P], plane[:, n * P : (n + 1) * P]) for n in range(words // P)]
 
         def product(weight, acc, rows, cols, copy=nc.scalar.copy):
             nc.tensor.matmul_mx(
@@ -143,13 +144,8 @@ def tile_picked_wedgecv_relu_lo_kernel(
         def larger(kind, unit, a, b):
             nc.vector.tensor_tensor(place(kind, unit), got[(a, unit)], got[(b, unit)], MAX)
 
-        z_turned = {0: sb([P, 2 * T], BF16, "z_turned0"), 2: sb([P, T], BF16, "z_turned2"), 3: sb([P, HALF], BF16, "z_turned3")}
-        z_bf = {0: sb([P, 2 * T], BF16, "z_bf0"), 2: sb([P, T], BF16, "z_bf2"), 3: sb([P, T], BF16, "z_bf3")}
-
-        def turned(block):
-            if block < 2:
-                return z_turned[0][:, block * T : (block + 1) * T]
-            return z_turned[block][:]
+        z_turned = {b: sb([P, cols], BF16, "z_turned%d" % b) for b, cols in ((0, 2 * T), (2, T), (3, HALF))}
+        z_bf = {b: sb([P, cols], BF16, "z_bf%d" % b) for b, cols in ((0, 2 * T), (2, T), (3, T))}
 
         def edge_sum(unit, bank, at=0):
             top = got[("top", unit)]
@@ -169,12 +165,12 @@ def tile_picked_wedgecv_relu_lo_kernel(
             )
 
         def relu_low(c, block, src):
-            nc.scalar.activation(turned(block)[:, c * P : (c + 1) * P], src, RELU)
+            nc.scalar.activation(z_turned[block][:, c * P : (c + 1) * P], src, RELU)
 
         def turn(block, count, bank):
-            words = z_turned[block][:].bitcast(F32)
+            pairs = z_turned[block][:].bitcast(F32)
             for n in range(2 * count):
-                nc.tensor.transpose(bank[:, n * P : (n + 1) * P], words[:, n * P : (n + 1) * P], ident[:])
+                nc.tensor.transpose(bank[:, n * P : (n + 1) * P], pairs[:, n * P : (n + 1) * P], ident[:])
             nc.scalar.copy(
                 out=z_bf[block][:].bitcast(F32).rearrange("p (b v u) -> p b v u", v=P, u=2),
                 in_=bank[:, 0 : 2 * count * P].rearrange("p (b u v) -> p b v u", v=P, u=2),
@@ -243,8 +239,8 @@ def tile_picked_wedgecv_relu_lo_kernel(
         w2_bf23 = sb([P, 2 * T], BF16, "w2_bf23")
         w1_bf = sb([P, 4 * T], BF16, "w1_bf")
 
-        nc.vector.tensor_copy(out=low_view(w2_bf0[:])[:, 0:40], in_=w2_raw[0][:, 0:40, :, 0:2])
-        nc.scalar.copy(out=low_view(w2_bf0[:])[:, 40:64], in_=w2_raw[0][:, 40:64, :, 0:2])
+        nc.vector.tensor_copy(out=low_view(w2_bf0[:])[:, 0:VECTOR_GROUPS], in_=w2_raw[0][:, 0:VECTOR_GROUPS, :, 0:2])
+        nc.scalar.copy(out=low_view(w2_bf0[:])[:, VECTOR_GROUPS:], in_=w2_raw[0][:, VECTOR_GROUPS:, :, 0:2])
         w2_q = quantize(w2_bf0[:], "w2a")
         for half, copy in enumerate((nc.scalar.copy, nc.vector.tensor_copy)):
             product(w2_q[0], banks[half][:, 0:HALF], e[0][:], slice(half * HALF, (half + 1) * HALF), copy)
@@ -270,9 +266,9 @@ def tile_picked_wedgecv_relu_lo_kernel(
             in_=w3_raw_plane[:].rearrange("p (s i t) -> p s t i", t=4, i=16),
         )
 
-        held = sb([P, 2 * T], F32, "held_first", tag="w2_raw1")
-        got[("g2", 0)] = held[:, 0:T]
-        got[("pair", 0)] = held[:, T : 2 * T]
+        held_first = sb([P, 2 * T], F32, "held_first", tag="w2_raw1")
+        got[("g2", 0)] = held_first[:, 0:T]
+        got[("pair", 0)] = held_first[:, T : 2 * T]
         hold("w1_raw1", gathers(2, 3) + [("top", 1), ("g0", 4)])
         for later, earlier in (
             (("g1", 4), ("g0", 3)),
@@ -320,9 +316,7 @@ def tile_picked_wedgecv_relu_lo_kernel(
         gather(5, 1)
         gather(5, 2)
         larger("pair", 5, "g0", "g1")
-        z_q = quantize(z_bf[0][:], "z0")
-        project(0, z_q[0], banks[2], banks[2])
-        store(0, banks[2], banks[2])
+        z_first = quantize(z_bf[0][:], "z0")
         larger("top", 5, "pair", "g2")
         edge_sum(5, banks[7])
         nc.scalar.activation(
@@ -330,8 +324,10 @@ def tile_picked_wedgecv_relu_lo_kernel(
             banks[7][:, 0:HALF].rearrange("v (t q) -> v q t", t=2),
             RELU,
         )
+        project(0, z_first[0], banks[0], banks[0])
         turn(2, 1, banks[4])
-        project(1, z_q[1], banks[5], banks[5])
+        store(0, banks[0], banks[0])
+        project(1, z_first[1], banks[5], banks[5])
         store(1, banks[5], banks[5])
         out_bf = {block: sb([P, T], BF16, "out_bf%d" % block)[:] for block in (1, 2, 3)}
 
@@ -353,17 +349,17 @@ def tile_picked_wedgecv_relu_lo_kernel(
             op0=MAX,
             op1=MAX,
         )
-        z_q = quantize(z_bf[2][:], "z2")
+        z_third = quantize(z_bf[2][:], "z2")
         z_last = quantize(z_bf[3][:], "z3", "z_bf2")
-        project(2, z_q[0], banks[6], banks[6])
+        project(2, z_third[0], banks[6], banks[6])
         store(2, banks[6], banks[6])
         round_out(0, out_bf[0], nc.scalar.copy)
         round_out(1, out_bf[1], nc.vector.tensor_copy)
         hand_on(0, out_bf[0])
         hand_on(1, out_bf[1])
         round_out(2, out_bf[2], nc.vector.tensor_copy)
-        project(3, z_last[0], banks[3], banks[0])
-        store(3, banks[3], banks[0])
+        project(3, z_last[0], banks[3], banks[2])
+        store(3, banks[3], banks[2])
         hand_on(2, out_bf[2])
         round_out(3, out_bf[3], nc.vector.tensor_copy)
         hand_on(3, out_bf[3])

@@ -48,10 +48,8 @@ def tile_picked_wedgecv_relu_lo_kernel(
         x_plane = sb([P, T], U8, "x_plane")
         w3_raw = sb([P, H], U32, "w3_raw")
         w3_raw_plane = sb([P, H], U8, "w3_raw_plane")
-        w3_codes = sb([P, H], U32, "w3_codes")
-        w3_plane = sb([P, H], U8, "w3_plane")
         ident = sb([P, P], F32, "ident")
-        e = [sb([P, T + (SPARE if c == 0 else 0)], F32, "e%d" % c) for c in range(4)]
+        e = [sb([P, T + (SPARE if c == 0 else 0)], F32, "e%d" % c) for c in range(1)]
         y_low = [sb([P, T], F32, "y%d" % c) for c in range(2)]
         y_high = sb([P, 2 * T], F32, "y_high")
         y = [y_low[0][:], y_low[1][:], y_high[:, 0:T], y_high[:, T : 2 * T]]
@@ -79,8 +77,8 @@ def tile_picked_wedgecv_relu_lo_kernel(
         nc.sync.dma_start(out=x_codes[:].bitcast(I32), in_=x_words[0].rearrange("p n t -> p (n t)").bitcast(I32))
         load_scales(x_plane, x_scales)
         nc.sync.dma_start(lists[0][:], pos1)
-        nc.sync.dma_start(lists[1][:], pos2)
         w2_raw.append(load_weight(w2, 1, "w2_raw1"))
+        nc.sync.dma_start(lists[1][:], pos2)
         nc.sync.dma_start(lists[2][:], pos3)
         w1_raw = [load_weight(w1, half, "w1_raw%d" % half) for half in range(2)]
         nc.sync.dma_start(out=w3_raw[:].bitcast(I32), in_=w3_words[0].rearrange("p n t -> p (n t)").bitcast(I32))
@@ -120,6 +118,7 @@ def tile_picked_wedgecv_relu_lo_kernel(
 
         def hold(tag, steps):
             held = sb([P, len(steps) * HALF], F32, "held_%s_%s" % steps[0], tag=tag)
+            got[tag] = held
             for n, step in enumerate(steps):
                 got[step] = held[:, n * HALF : (n + 1) * HALF]
 
@@ -144,36 +143,42 @@ def tile_picked_wedgecv_relu_lo_kernel(
         def larger(kind, unit, a, b):
             nc.vector.tensor_tensor(place(kind, unit), got[(a, unit)], got[(b, unit)], MAX)
 
-        z_turned = {b: sb([P, cols], BF16, "z_turned%d" % b) for b, cols in ((0, 2 * T), (2, T), (3, HALF))}
+        z_low = [sb([P, T], BF16, "z_low%d" % n) for n in range(2)]
+        z_high = [sb([P, HALF], BF16, "z_high%d" % b) for b in range(3)]
         z_bf = {b: sb([P, cols], BF16, "z_bf%d" % b) for b, cols in ((0, 2 * T), (2, T), (3, T))}
 
-        def edge_sum(unit, bank, at=0):
-            top = got[("top", unit)]
-            for n, (c, first, count) in enumerate(UNITS[unit]):
-                for b in range(count // P):
-                    cols = slice(n * count + b * P, n * count + (b + 1) * P)
-                    acc = bank[:, at + cols.start : at + cols.stop]
-                    centre = y[c][:, first + b * P : first + (b + 1) * P]
-                    nc.tensor.matmul(acc, top[:, cols], ident[:], start=True, stop=False, is_transpose=True)
-                    nc.tensor.matmul(acc, centre, ident[:], start=False, stop=True, is_transpose=True)
+        def edge_sum(unit, n, acc):
+            pieces = [(c, first + v) for c, first, count in UNITS[unit] for v in range(0, count, P)]
+            c, first = pieces[n]
+            top = got[("top", unit)][:, n * P : (n + 1) * P]
+            nc.tensor.matmul(acc, top, ident[:], start=True, stop=False, is_transpose=True)
+            nc.tensor.matmul(acc, y[c][:, first : first + P], ident[:], start=False, stop=True, is_transpose=True)
 
-        def relu_low_pair(c, bank):
+        def slot(bank, n, count=1):
+            return banks[bank][:, n * P : (n + count) * P]
+
+        def relu_low_pair(c, pair, src):
             nc.scalar.activation(
-                z_turned[0][:].rearrange("v (b c s) -> v c b s", b=2, c=4)[:, c],
-                bank[:, 0:HALF].rearrange("v (b s) -> v b s", b=2),
+                z_low[pair][:].rearrange("v (b c s) -> v c b s", b=2, c=2)[:, c],
+                src.rearrange("v (b s) -> v b s", b=2),
                 RELU,
             )
 
-        def relu_low(c, block, src):
-            nc.scalar.activation(z_turned[block][:, c * P : (c + 1) * P], src, RELU)
+        def relu_high(block, src):
+            nc.scalar.activation(
+                z_high[block][:].rearrange("v (q t) -> v q t", t=2), src.rearrange("v (t q) -> v q t", t=2), RELU
+            )
 
-        def turn(block, count, bank):
-            pairs = z_turned[block][:].bitcast(F32)
-            for n in range(2 * count):
-                nc.tensor.transpose(bank[:, n * P : (n + 1) * P], pairs[:, n * P : (n + 1) * P], ident[:])
+        def turn_low(block, acc):
+            pairs = z_low[block // 2][:].bitcast(F32)[:, block % 2 * P : (block % 2 + 1) * P]
+            nc.tensor.transpose(acc, pairs, ident[:])
+
+        def turn_high(block, acc):
+            nc.tensor.transpose(acc, z_high[block][:].bitcast(F32), ident[:])
+
+        def regroup(out, src):
             nc.scalar.copy(
-                out=z_bf[block][:].bitcast(F32).rearrange("p (b v u) -> p b v u", v=P, u=2),
-                in_=bank[:, 0 : 2 * count * P].rearrange("p (b u v) -> p b v u", v=P, u=2),
+                out=out.bitcast(F32).rearrange("p (v u) -> p v u", u=2), in_=src.rearrange("p (u v) -> p v u", u=2)
             )
 
         def by_tile(ap):
@@ -229,6 +234,8 @@ def tile_picked_wedgecv_relu_lo_kernel(
         def hand_on(block, grouped):
             cols = slice(block * P, (block + 1) * P)
             nc.vector.quantize_mx(out=out_codes[:, cols].bitcast(FP8X4), scales=out_plane[:, cols], in_=grouped)
+
+        def store_codes(cols):
             nc.sync.dma_start(
                 out=out_1[0].rearrange("p n t -> p (n t)").bitcast(I32)[:, cols],
                 in_=out_codes[:, cols].bitcast(I32),
@@ -237,106 +244,114 @@ def tile_picked_wedgecv_relu_lo_kernel(
         w2_bf0 = sb([P, T], BF16, "w2_bf0")
         w2_bf1 = sb([P, T], BF16, "w2_bf1")
         w2_bf23 = sb([P, 2 * T], BF16, "w2_bf23")
-        w1_bf = sb([P, 4 * T], BF16, "w1_bf")
+        w1_low = sb([P, 2 * T], BF16, "w1_low")
+        w1_high = sb([P, 2 * T], BF16, "w1_high")
 
         nc.vector.tensor_copy(out=low_view(w2_bf0[:])[:, 0:VECTOR_GROUPS], in_=w2_raw[0][:, 0:VECTOR_GROUPS, :, 0:2])
         nc.scalar.copy(out=low_view(w2_bf0[:])[:, VECTOR_GROUPS:], in_=w2_raw[0][:, VECTOR_GROUPS:, :, 0:2])
         w2_q = quantize(w2_bf0[:], "w2a")
-        for half, copy in enumerate((nc.scalar.copy, nc.vector.tensor_copy)):
+        for half, copy in enumerate((nc.vector.tensor_copy, nc.scalar.copy)):
             product(w2_q[0], banks[half][:, 0:HALF], e[0][:], slice(half * HALF, (half + 1) * HALF), copy)
         nc.scalar.copy(out=high_view(w2_bf23[:], 0), in_=w2_raw[0][:, :, :, 2:4])
         nc.scalar.copy(out=low_view(w2_bf1[:]), in_=w2_raw[1][:, :, :, 0:2])
         nc.scalar.copy(out=high_view(w2_bf23[:], 1), in_=w2_raw[1][:, :, :, 2:4])
         w2_q = w2_q + quantize(w2_bf1[:], "w2b") + quantize(w2_bf23[:], "w2c")
-        product(w2_q[1], banks[2][:], e[1][:], slice(0, T))
         for half in range(2):
-            nc.scalar.copy(out=low_view(w1_bf[:, half * T : (half + 1) * T]), in_=w1_raw[half][:, :, :, 0:2])
-            nc.scalar.copy(out=high_view(w1_bf[:, 2 * T : 4 * T], half), in_=w1_raw[half][:, :, :, 2:4])
-        for c in (2, 3):
+            nc.scalar.copy(out=low_view(w1_low[:, half * T : (half + 1) * T]), in_=w1_raw[half][:, :, :, 0:2])
+            nc.scalar.copy(out=high_view(w1_high[:], half), in_=w1_raw[half][:, :, :, 2:4])
+            if half == 0:
+                e.append(sb([P, T], F32, "e1", "w1_raw0"))
+                product(w2_q[1], banks[2][:], e[1][:], slice(0, T))
+        w1_q = quantize(w1_low[:], "w1a") + quantize(w1_high[:], "w1b")
+        for c, tag in ((2, "w1_low"), (3, "w1_high")):
+            e.append(sb([P, T], F32, "e%d" % c, tag))
             product(w2_q[c], banks[c + 1][:], e[c][:], slice(0, T))
-        w1_q = quantize(w1_bf[:], "w1")
         for c, bank in enumerate((0, 1, 2, 5)):
             product(w1_q[c], banks[bank][:], y[c], slice(0, T))
-        nc.vector.tensor_copy(
-            out=w3_codes[:].bitcast(I32).rearrange("p (t s i) -> p s t i", t=4, i=4),
-            in_=w3_raw[:].bitcast(I32).rearrange("p (s i t) -> p s t i", t=4, i=4),
-        )
-        nc.vector.tensor_copy(
-            out=w3_plane[:].rearrange("p (t s i) -> p s t i", t=4, i=16),
-            in_=w3_raw_plane[:].rearrange("p (s i t) -> p s t i", t=4, i=16),
-        )
 
         held_first = sb([P, 2 * T], F32, "held_first", tag="w2_raw1")
         got[("g2", 0)] = held_first[:, 0:T]
         got[("pair", 0)] = held_first[:, T : 2 * T]
-        hold("w1_raw1", gathers(2, 3) + [("top", 1), ("g0", 4)])
+        hold("w1_raw1", [("top", 1), ("g0", 2), ("g1", 2), ("g2", 2), ("g1", 3), ("g2", 3), ("g0", 3)])
         for later, earlier in (
+            (("g0", 4), ("g0", 2)),
             (("g1", 4), ("g0", 3)),
             (("g2", 4), ("g1", 3)),
-            (("g0", 5), ("g2", 3)),
-            (("g1", 5), ("g0", 4)),
-            (("g2", 5), ("g1", 4)),
         ):
             got[later] = got[earlier]
+        got[("g0", 5)] = got["w1_raw1"][:, 11 * P : 13 * P]
         gather(0, 0)
-        for unit in range(4):
+        for unit in range(5):
             gather(unit, 1)
             gather(unit, 2)
             larger("pair", unit, "g0", "g1")
-            gather(unit + 1, 0)
+            gather(unit + 1, 0, (0,))
             larger("top", unit, "pair", "g2")
-        edge_sum(0, banks[6])
-        relu_low_pair(0, banks[6])
-        edge_sum(1, banks[7])
-        relu_low_pair(1, banks[7])
-        for block in (2, 3):
-            relu_low(0, block, banks[6][:, block * P : (block + 1) * P])
-        edge_sum(2, banks[3])
-        edge_sum(3, banks[3], HALF)
-        nc.scalar.activation(
-            z_turned[0][:].rearrange("v (b u q t) -> v u b q t", b=2, u=2, t=2)[:, 1],
-            banks[3][:].rearrange("v (t b q) -> v b q t", t=2, b=2),
-            RELU,
-        )
-        turn(0, 2, banks[0])
-
-        gather(4, 1)
-        gather(4, 2)
-        larger("pair", 4, "g0", "g1")
-        gather(5, 0, (0,))
-        larger("top", 4, "pair", "g2")
-        edge_sum(4, banks[0])
-        for block in (2, 3):
-            relu_low(1, block, banks[0][:, (block - 2) * P : (block - 1) * P])
-        nc.tensor.transpose(banks[1][:, 0:P], z_turned[3][:].bitcast(F32), ident[:])
-        nc.scalar.copy(out=z_bf[3][:].bitcast(F32).rearrange("p (v u) -> p v u", u=2)[:, :, 0], in_=banks[1][:, 0:P])
-
-        hold("top_4", [("top", 5)] + gathers(6))
         gather(5, 0, (1,))
+        got[("g1", 5)] = got[("g0", 4)]
         gather(5, 1)
+        for n in range(3):
+            edge_sum(0, n, slot(6, n))
+        relu_low_pair(0, 0, slot(6, 0, 2))
+        for n in range(2):
+            edge_sum(1, n, slot(7, n))
+        relu_low_pair(1, 0, slot(7, 0, 2))
+        nc.scalar.activation(z_low[1][:, 0:P], slot(6, 2), RELU)
+        for block in range(2):
+            turn_low(block, slot(1 + block, 0))
+        for unit in (2, 3):
+            for block in range(2):
+                edge_sum(unit, block, slot(3 + block, unit - 2))
+        w3_codes = sb([P, H], U32, "w3_codes", "top_3")
+        nc.vector.tensor_copy(
+            out=w3_codes[:].bitcast(I32).rearrange("p (t s i) -> p s t i", t=4, i=4),
+            in_=w3_raw[:].bitcast(I32).rearrange("p (s i t) -> p s t i", t=4, i=4),
+        )
+        for block in range(2):
+            relu_high(block, slot(3 + block, 0, 2))
+        for block in range(2):
+            turn_high(block, slot(1 + block, 1))
+        w3_plane = sb([P, H], U8, "w3_plane", "z_high0")
+        nc.vector.tensor_copy(
+            out=w3_plane[:].rearrange("p (t s i) -> p s t i", t=4, i=16),
+            in_=w3_raw_plane[:].rearrange("p (s i t) -> p s t i", t=4, i=16),
+        )
+        for block in range(2):
+            regroup(z_bf[0][:, block * T : (block + 1) * T], slot(1 + block, 0, 2))
+        z_first = quantize(z_bf[0][:], "z0")
+        for n in range(2):
+            edge_sum(4, n, slot(1, n))
+        edge_sum(0, 3, slot(2, 0))
+        project(0, z_first[0], banks[0], banks[0])
+        project(1, z_first[1], banks[5], banks[5])
+        relu_low_pair(1, 1, slot(1, 0, 2))
+        nc.scalar.activation(z_low[1][:, HALF : HALF + P], slot(2, 0), RELU)
+        turn_low(2, slot(4, 0))
+        turn_low(3, slot(3, 0))
+        nc.scalar.copy(out=z_bf[3][:].bitcast(F32).rearrange("p (v u) -> p v u", u=2)[:, :, 0], in_=slot(3, 0))
+        store(0, banks[0], banks[0])
+        store(1, banks[5], banks[5])
+
+        hold("top_0", [("g2", 5), ("pair", 5), ("g0", 6)])
+        got[("g1", 6)] = got[("g0", 5)]
+        got[("g2", 6)] = got[("g1", 5)]
         gather(5, 2)
         larger("pair", 5, "g0", "g1")
-        z_first = quantize(z_bf[0][:], "z0")
+        gather(6, 0, (0,))
         larger("top", 5, "pair", "g2")
-        edge_sum(5, banks[7])
-        nc.scalar.activation(
-            z_turned[2][:, HALF:T].rearrange("v (q t) -> v q t", t=2),
-            banks[7][:, 0:HALF].rearrange("v (t q) -> v q t", t=2),
-            RELU,
-        )
-        project(0, z_first[0], banks[0], banks[0])
-        turn(2, 1, banks[4])
-        store(0, banks[0], banks[0])
-        project(1, z_first[1], banks[5], banks[5])
-        store(1, banks[5], banks[5])
-        out_bf = {block: sb([P, T], BF16, "out_bf%d" % block)[:] for block in (1, 2, 3)}
+        for n in range(2):
+            edge_sum(5, n, slot(7, n))
+        relu_high(2, slot(7, 0, 2))
+        turn_high(2, slot(4, 1))
+        regroup(z_bf[2][:], slot(4, 0, 2))
 
-        gather(6, 0)
+        gather(6, 0, (1,))
         gather(6, 1)
         edge_gather(6, 0)
         larger("pair", 6, "g0", "g1")
         edge_gather(6, 1)
-        hold("z_turned2", [("rounded", 0)])
+        hold("z_high2", [("rounded", 0)])
+        out_bf = {block: sb([P, T], BF16, "out_bf%d" % block)[:] for block in (2, 3)}
         out_bf[0] = got[("rounded", 0)].bitcast(BF16)
         nc.vector.tensor_tensor(
             by_tile(place("sum", 6)), by_tile(got[("pair", 6)]), by_tile(y_high[:])[:, :, 3 * P : T], ADD
@@ -351,6 +366,7 @@ def tile_picked_wedgecv_relu_lo_kernel(
         )
         z_third = quantize(z_bf[2][:], "z2")
         z_last = quantize(z_bf[3][:], "z3", "z_bf2")
+        out_bf[1] = sb([P, T], BF16, "out_bf1", "z_bf3")[:]
         project(2, z_third[0], banks[6], banks[6])
         store(2, banks[6], banks[6])
         round_out(0, out_bf[0], nc.scalar.copy)
@@ -360,9 +376,11 @@ def tile_picked_wedgecv_relu_lo_kernel(
         round_out(2, out_bf[2], nc.vector.tensor_copy)
         project(3, z_last[0], banks[3], banks[2])
         store(3, banks[3], banks[2])
+        store_codes(slice(0, HALF))
         hand_on(2, out_bf[2])
         round_out(3, out_bf[3], nc.vector.tensor_copy)
         hand_on(3, out_bf[3])
+        store_codes(slice(HALF, T))
         for q in range(4):
             queue = nc.scalar if q % 2 else nc.sync
             queue.dma_start(

@@ -76,12 +76,12 @@ def tile_picked_wedgecv_relu_lo_kernel(
         w2_raw = [load_weight(w2, 0, "w2_raw0")]
         nc.sync.dma_start(out=x_codes[:].bitcast(I32), in_=x_words[0].rearrange("p n t -> p (n t)").bitcast(I32))
         load_scales(x_plane, x_scales)
+        nc.sync.dma_start(out=w3_raw[:].bitcast(I32), in_=w3_words[0].rearrange("p n t -> p (n t)").bitcast(I32))
         nc.sync.dma_start(lists[0][:], pos1)
         w2_raw.append(load_weight(w2, 1, "w2_raw1"))
         nc.sync.dma_start(lists[1][:], pos2)
         nc.sync.dma_start(lists[2][:], pos3)
         w1_raw = [load_weight(w1, half, "w1_raw%d" % half) for half in range(2)]
-        nc.sync.dma_start(out=w3_raw[:].bitcast(I32), in_=w3_words[0].rearrange("p n t -> p (n t)").bitcast(I32))
         load_scales(w3_raw_plane, w3_scales)
 
         banks = [psum.tile([P, T], F32, name="bank%d" % n) for n in range(8)]
@@ -151,8 +151,9 @@ def tile_picked_wedgecv_relu_lo_kernel(
             pieces = [(c, first + v) for c, first, count in UNITS[unit] for v in range(0, count, P)]
             c, first = pieces[n]
             top = got[("top", unit)][:, n * P : (n + 1) * P]
-            nc.tensor.matmul(acc, top, ident[:], start=True, stop=False, is_transpose=True)
-            nc.tensor.matmul(acc, y[c][:, first : first + P], ident[:], start=False, stop=True, is_transpose=True)
+            terms = (top, y[c][:, first : first + P])
+            for k, term in enumerate(reversed(terms) if unit == 3 else terms):
+                nc.tensor.matmul(acc, term, ident[:], start=k == 0, stop=k == 1, is_transpose=True)
 
         def slot(bank, n, count=1):
             return banks[bank][:, n * P : (n + count) * P]
@@ -212,6 +213,17 @@ def tile_picked_wedgecv_relu_lo_kernel(
                     stop=True,
                 )
 
+        def warm_up(bank):
+            nc.tensor.matmul_mx(
+                out=bank[:],
+                lhsT=w2_q[3][0].bitcast(FP8X4),
+                lhsT_scale=w2_q[3][1],
+                rhs=x_codes[:].bitcast(FP8X4),
+                rhs_scale=x_plane[:],
+                start=True,
+                stop=True,
+            )
+
         def store(block, bank, second):
             result = results[block // 2][:, block % 2 * T : (block % 2 + 1) * T]
             if block == 3:
@@ -250,8 +262,8 @@ def tile_picked_wedgecv_relu_lo_kernel(
         nc.vector.tensor_copy(out=low_view(w2_bf0[:])[:, 0:VECTOR_GROUPS], in_=w2_raw[0][:, 0:VECTOR_GROUPS, :, 0:2])
         nc.scalar.copy(out=low_view(w2_bf0[:])[:, VECTOR_GROUPS:], in_=w2_raw[0][:, VECTOR_GROUPS:, :, 0:2])
         w2_q = quantize(w2_bf0[:], "w2a")
-        for half, copy in enumerate((nc.vector.tensor_copy, nc.scalar.copy)):
-            product(w2_q[0], banks[half][:, 0:HALF], e[0][:], slice(half * HALF, (half + 1) * HALF), copy)
+        for half in range(2):
+            product(w2_q[0], banks[half][:, 0:HALF], e[0][:], slice(half * HALF, (half + 1) * HALF))
         nc.scalar.copy(out=high_view(w2_bf23[:], 0), in_=w2_raw[0][:, :, :, 2:4])
         nc.scalar.copy(out=low_view(w2_bf1[:]), in_=w2_raw[1][:, :, :, 0:2])
         nc.scalar.copy(out=high_view(w2_bf23[:], 1), in_=w2_raw[1][:, :, :, 2:4])
@@ -302,7 +314,7 @@ def tile_picked_wedgecv_relu_lo_kernel(
         for unit in (2, 3):
             for block in range(2):
                 edge_sum(unit, block, slot(3 + block, unit - 2))
-        w3_codes = sb([P, H], U32, "w3_codes", "top_3")
+        w3_codes = sb([P, H], U32, "w3_codes")
         nc.vector.tensor_copy(
             out=w3_codes[:].bitcast(I32).rearrange("p (t s i) -> p s t i", t=4, i=4),
             in_=w3_raw[:].bitcast(I32).rearrange("p (s i t) -> p s t i", t=4, i=4),
@@ -319,13 +331,13 @@ def tile_picked_wedgecv_relu_lo_kernel(
         for block in range(2):
             regroup(z_bf[0][:, block * T : (block + 1) * T], slot(1 + block, 0, 2))
         z_first = quantize(z_bf[0][:], "z0")
+        edge_sum(0, 3, slot(1, 2))
         for n in range(2):
             edge_sum(4, n, slot(1, n))
-        edge_sum(0, 3, slot(2, 0))
         project(0, z_first[0], banks[0], banks[0])
         project(1, z_first[1], banks[5], banks[5])
         relu_low_pair(1, 1, slot(1, 0, 2))
-        nc.scalar.activation(z_low[1][:, HALF : HALF + P], slot(2, 0), RELU)
+        nc.scalar.activation(z_low[1][:, HALF : HALF + P], slot(1, 2), RELU)
         turn_low(2, slot(4, 0))
         turn_low(3, slot(3, 0))
         nc.scalar.copy(out=z_bf[3][:].bitcast(F32).rearrange("p (v u) -> p v u", u=2)[:, :, 0], in_=slot(3, 0))
@@ -341,8 +353,11 @@ def tile_picked_wedgecv_relu_lo_kernel(
         larger("top", 5, "pair", "g2")
         for n in range(2):
             edge_sum(5, n, slot(7, n))
+        warm_up(banks[5])
         relu_high(2, slot(7, 0, 2))
         turn_high(2, slot(4, 1))
+        warm_up(banks[7])
+        warm_up(banks[7])
         regroup(z_bf[2][:], slot(4, 0, 2))
 
         gather(6, 0, (1,))

@@ -297,8 +297,11 @@ def tile_picked_wedgecv_relu_lo_kernel(
             gather(unit, 1)
             gather(unit, 2)
             larger("pair", unit, "g0", "g1")
+            if unit == 1:
+                larger("top", unit, "pair", "g2")
             gather(unit + 1, 0, (0,))
-            larger("top", unit, "pair", "g2")
+            if unit != 1:
+                larger("top", unit, "pair", "g2")
         gather(5, 0, (1,))
         got[("g1", 5)] = got[("g0", 4)]
         gather(5, 1)

@@ -16,13 +16,13 @@ FP8X4 = mybir.dt.float8_e4m3fn_x4
 RELU = mybir.ActivationFunctionType.Relu
 MAX = mybir.AluOpType.max
 ADD = mybir.AluOpType.add
+SUBTRACT = mybir.AluOpType.subtract
 
 P = 128
 HALF = 256
-SPARE = 192
 VECTOR_GROUPS = 40
 UNITS = [
-    [(0, 0, T)],
+    [(0, 0, HALF), (0, HALF, HALF)],
     [(1, 0, HALF)],
     [(2, 0, HALF)],
     [(3, 0, HALF)],
@@ -49,14 +49,13 @@ def tile_picked_wedgecv_relu_lo_kernel(
         w3_raw = sb([P, H], U32, "w3_raw")
         w3_raw_plane = sb([P, H], U8, "w3_raw_plane")
         ident = sb([P, P], F32, "ident")
-        e = [sb([P, T + (SPARE if c == 0 else 0)], F32, "e%d" % c) for c in range(1)]
+        e = [sb([P, T], F32, "e0")]
         y_low = [sb([P, T], F32, "y%d" % c) for c in range(2)]
         y_high = sb([P, 2 * T], F32, "y_high")
         y = [y_low[0][:], y_low[1][:], y_high[:, 0:T], y_high[:, T : 2 * T]]
 
         nc.gpsimd.memset(x_plane[:].bitcast(I32), 0)
         nc.gpsimd.memset(w3_raw_plane[:].bitcast(I32), 0)
-        nc.vector.memset(e[0][:, T : T + SPARE], 0.0)
         make_identity(nc, ident[:])
 
         def load_scales(plane, scales):
@@ -136,9 +135,26 @@ def tile_picked_wedgecv_relu_lo_kernel(
         def gather(unit, d, pieces=(0, 1)):
             for n, (c, first, count) in enumerate(UNITS[unit]):
                 if n in pieces:
-                    nc.vector.tensor_copy(
-                        place("g%d" % d, unit)[:, n * count : (n + 1) * count], window(c, d, first, count)
-                    )
+                    cols = slice(n * count, (n + 1) * count)
+                    if d == 0:
+                        nc.vector.tensor_copy(place("g0", unit)[:, cols], window(c, d, first, count))
+                    else:
+                        nc.vector.tensor_tensor(
+                            place("g%d" % d, unit)[:, cols],
+                            window(c, d, first, count),
+                            got[("g0", unit)][:, cols],
+                            SUBTRACT,
+                        )
+
+        def excess(unit):
+            nc.vector.scalar_tensor_tensor(
+                out=place("top", unit),
+                in0=got[("g1", unit)],
+                scalar=0.0,
+                in1=got[("g2", unit)],
+                op0=MAX,
+                op1=MAX,
+            )
 
         def larger(kind, unit, a, b):
             nc.vector.tensor_tensor(place(kind, unit), got[(a, unit)], got[(b, unit)], MAX)
@@ -150,10 +166,10 @@ def tile_picked_wedgecv_relu_lo_kernel(
         def edge_sum(unit, n, acc):
             pieces = [(c, first + v) for c, first, count in UNITS[unit] for v in range(0, count, P)]
             c, first = pieces[n]
-            top = got[("top", unit)][:, n * P : (n + 1) * P]
-            terms = (top, y[c][:, first : first + P])
+            cols = slice(n * P, (n + 1) * P)
+            terms = (got[("top", unit)][:, cols], got[("g0", unit)][:, cols], y[c][:, first : first + P])
             for k, term in enumerate(reversed(terms) if unit == 3 else terms):
-                nc.tensor.matmul(acc, term, ident[:], start=k == 0, stop=k == 1, is_transpose=True)
+                nc.tensor.matmul(acc, term, ident[:], start=k == 0, stop=k == 2, is_transpose=True)
 
         def slot(bank, n, count=1):
             return banks[bank][:, n * P : (n + count) * P]
@@ -188,11 +204,11 @@ def tile_picked_wedgecv_relu_lo_kernel(
         def by_centre(ap):
             return ap.rearrange("p (t v) -> p v t", t=2)
 
-        def edge_gather(unit, n):
+        def edge_gather(unit, d, n):
             c, first, count = UNITS[unit][n]
             nc.vector.tensor_tensor(
-                place("g2", unit)[:, n * count : (n + 1) * count],
-                window(c, 2, first, count),
+                place("g%d" % d, unit)[:, n * count : (n + 1) * count],
+                window(c, d, first, count),
                 y[c][:, first : first + count],
                 ADD,
             )
@@ -275,35 +291,24 @@ def tile_picked_wedgecv_relu_lo_kernel(
                 e.append(sb([P, T], F32, "e1", "w1_raw0"))
                 product(w2_q[1], banks[2][:], e[1][:], slice(0, T))
         w1_q = quantize(w1_low[:], "w1a") + quantize(w1_high[:], "w1b")
-        for c, tag in ((2, "w1_low"), (3, "w1_high")):
-            e.append(sb([P, T], F32, "e%d" % c, tag))
+        for c in (2, 3):
+            e.append(sb([P, T], F32, "e%d" % c))
             product(w2_q[c], banks[c + 1][:], e[c][:], slice(0, T))
-        for c, bank in enumerate((0, 1, 2, 5)):
+        for c, bank in enumerate((5, 0, 1, 2)):
             product(w1_q[c], banks[bank][:], y[c], slice(0, T))
 
-        held_first = sb([P, 2 * T], F32, "held_first", tag="w2_raw1")
-        got[("g2", 0)] = held_first[:, 0:T]
-        got[("pair", 0)] = held_first[:, T : 2 * T]
-        hold("w1_raw1", [("top", 1), ("g0", 2), ("g1", 2), ("g2", 2), ("g1", 3), ("g2", 3), ("g0", 3)])
-        for later, earlier in (
-            (("g0", 4), ("g0", 2)),
-            (("g1", 4), ("g0", 3)),
-            (("g2", 4), ("g1", 3)),
-        ):
-            got[later] = got[earlier]
-        got[("g0", 5)] = got["w1_raw1"][:, 11 * P : 13 * P]
+        got[("g2", 0)] = sb([P, T], F32, "held_first", tag="w2_raw1")[:]
+        hold("w1_raw1", [("g2", 1)])
+        for unit in (2, 3, 4):
+            got[("g2", unit)] = got[("g2", 1)]
         gather(0, 0)
         for unit in range(5):
             gather(unit, 1)
             gather(unit, 2)
-            larger("pair", unit, "g0", "g1")
-            if unit == 1:
-                larger("top", unit, "pair", "g2")
-            gather(unit + 1, 0, (0,))
-            if unit != 1:
-                larger("top", unit, "pair", "g2")
-        gather(5, 0, (1,))
-        got[("g1", 5)] = got[("g0", 4)]
+            if unit > 0:
+                got[("g0", unit + 1)] = got[("g1", unit - 1)][:, 0:HALF]
+            gather(unit + 1, 0)
+            excess(unit)
         gather(5, 1)
         for n in range(3):
             edge_sum(0, n, slot(6, n))
@@ -347,13 +352,12 @@ def tile_picked_wedgecv_relu_lo_kernel(
         store(0, banks[0], banks[0])
         store(1, banks[5], banks[5])
 
-        hold("top_0", [("g2", 5), ("pair", 5), ("g0", 6)])
-        got[("g1", 6)] = got[("g0", 5)]
+        hold("top_0", [("g2", 5), ("g0", 6), ("g1", 6)])
         got[("g2", 6)] = got[("g1", 5)]
         gather(5, 2)
-        larger("pair", 5, "g0", "g1")
-        gather(6, 0, (0,))
-        larger("top", 5, "pair", "g2")
+        edge_gather(6, 0, 0)
+        edge_gather(6, 0, 1)
+        excess(5)
         for n in range(2):
             edge_sum(5, n, slot(7, n))
         warm_up(banks[5])
@@ -363,20 +367,17 @@ def tile_picked_wedgecv_relu_lo_kernel(
         warm_up(banks[7])
         regroup(z_bf[2][:], slot(4, 0, 2))
 
-        gather(6, 0, (1,))
-        gather(6, 1)
-        edge_gather(6, 0)
+        edge_gather(6, 1, 0)
+        edge_gather(6, 1, 1)
+        edge_gather(6, 2, 0)
         larger("pair", 6, "g0", "g1")
-        edge_gather(6, 1)
+        edge_gather(6, 2, 1)
         hold("z_high2", [("rounded", 0)])
         out_bf = {block: sb([P, T], BF16, "out_bf%d" % block)[:] for block in (2, 3)}
         out_bf[0] = got[("rounded", 0)].bitcast(BF16)
-        nc.vector.tensor_tensor(
-            by_tile(place("sum", 6)), by_tile(got[("pair", 6)]), by_tile(y_high[:])[:, :, 3 * P : T], ADD
-        )
         nc.vector.scalar_tensor_tensor(
             out=z_bf[3][:].rearrange("p (v u t) -> p v u t", u=2, t=2)[:, :, 1, :],
-            in0=by_centre(got[("sum", 6)]),
+            in0=by_centre(got[("pair", 6)]),
             scalar=0.0,
             in1=by_centre(got[("g2", 6)]),
             op0=MAX,

@@ -38,6 +38,7 @@ def tile_picked_wedgecv_relu_lo_kernel(
     nc = tc.nc
     with ExitStack() as ctx:
         keep = ctx.enter_context(tc.tile_pool(name="keep", bufs=1))
+        shared = ctx.enter_context(tc.tile_pool(name="shared", bufs=1))
         psum = ctx.enter_context(tc.psum_pool(name="psum", bufs=1))
 
         def sb(shape, dtype, name, tag=None):
@@ -65,22 +66,26 @@ def tile_picked_wedgecv_relu_lo_kernel(
                     in_=scales[0, 4 * q : 4 * q + 4, :].bitcast(I32),
                 )
 
-        def load_weight(w, half, name):
-            raw = sb([P, 4, HALF], F32, name)
+        def load_weight(w, half, raw):
             nc.sync.dma_start(
-                out=raw[:], in_=w.rearrange("(p j) c -> p j c", j=4)[:, :, half * HALF : (half + 1) * HALF]
+                out=raw.rearrange("p (j c) -> p j c", j=4),
+                in_=w.rearrange("(p j) c -> p j c", j=4)[:, :, half * HALF : (half + 1) * HALF],
             )
-            return raw[:].rearrange("p j (m t) -> p m j t", t=4)
+            return raw.rearrange("p (j m t) -> p m j t", j=4, t=4)
 
-        w2_raw = [load_weight(w2, 0, "w2_raw0")]
+        w2_raw = [load_weight(w2, 0, sb([P, 4 * HALF], F32, "w2_raw0")[:])]
         nc.sync.dma_start(out=x_codes[:].bitcast(I32), in_=x_words[0].rearrange("p n t -> p (n t)").bitcast(I32))
         load_scales(x_plane, x_scales)
         nc.sync.dma_start(out=w3_raw[:].bitcast(I32), in_=w3_words[0].rearrange("p n t -> p (n t)").bitcast(I32))
         nc.sync.dma_start(lists[0][:], pos1)
-        w2_raw.append(load_weight(w2, 1, "w2_raw1"))
+        first_room = sb([P, 5 * HALF], F32, "first_room")
+        w2_raw.append(load_weight(w2, 1, first_room[:, HALF:]))
         nc.sync.dma_start(lists[1][:], pos2)
         nc.sync.dma_start(lists[2][:], pos3)
-        w1_raw = [load_weight(w1, half, "w1_raw%d" % half) for half in range(2)]
+        w1_raw = [
+            load_weight(w1, half, shared.tile([P, 4 * HALF], F32, name="w1_raw%d" % half, offset=half * 4096)[:])
+            for half in range(2)
+        ]
         load_scales(w3_raw_plane, w3_scales)
 
         banks = [psum.tile([P, T], F32, name="bank%d" % n) for n in range(8)]
@@ -232,8 +237,8 @@ def tile_picked_wedgecv_relu_lo_kernel(
         def warm_up(bank):
             nc.tensor.matmul_mx(
                 out=bank[:],
-                lhsT=w2_q[3][0].bitcast(FP8X4),
-                lhsT_scale=w2_q[3][1],
+                lhsT=w1_q[3][0].bitcast(FP8X4),
+                lhsT_scale=w1_q[3][1],
                 rhs=x_codes[:].bitcast(FP8X4),
                 rhs_scale=x_plane[:],
                 start=True,
@@ -288,17 +293,22 @@ def tile_picked_wedgecv_relu_lo_kernel(
             nc.scalar.copy(out=low_view(w1_low[:, half * T : (half + 1) * T]), in_=w1_raw[half][:, :, :, 0:2])
             nc.scalar.copy(out=high_view(w1_high[:], half), in_=w1_raw[half][:, :, :, 2:4])
             if half == 0:
-                e.append(sb([P, T], F32, "e1", "w1_raw0"))
+                e.append(shared.tile([P, T], F32, name="e1", offset=0))
                 product(w2_q[1], banks[2][:], e[1][:], slice(0, T))
+                e.append(shared.tile([P, T], F32, name="e2", offset=2048))
+                product(w2_q[2], banks[3][:], e[2][:], slice(0, T))
         w1_q = quantize(w1_low[:], "w1a") + quantize(w1_high[:], "w1b")
-        for c in (2, 3):
-            e.append(sb([P, T], F32, "e%d" % c))
-            product(w2_q[c], banks[c + 1][:], e[c][:], slice(0, T))
-        for c, bank in enumerate((5, 0, 1, 2)):
+        e.append(shared.tile([P, T], F32, name="e3", offset=4096))
+        product(w2_q[3], banks[2][:], e[3][:], slice(0, T))
+        for c, bank in enumerate((5, 0, 1, 4)):
             product(w1_q[c], banks[bank][:], y[c], slice(0, T))
 
-        got[("g2", 0)] = sb([P, T], F32, "held_first", tag="w2_raw1")[:]
-        hold("w1_raw1", [("g2", 1)])
+        got[("g1", 0)] = first_room[:, 0:T]
+        got[("g2", 0)] = first_room[:, T : 2 * T]
+        second_room = sb([P, T + HALF], F32, "second_room", "w2c_codes")
+        got[("top", 0)] = second_room[:, 0:T]
+        got[("g1", 1)] = second_room[:, T:]
+        got[("g2", 1)] = shared.tile([P, HALF], F32, name="third", offset=6144)[:]
         for unit in (2, 3, 4):
             got[("g2", unit)] = got[("g2", 1)]
         gather(0, 0)
@@ -352,7 +362,7 @@ def tile_picked_wedgecv_relu_lo_kernel(
         store(0, banks[0], banks[0])
         store(1, banks[5], banks[5])
 
-        hold("top_0", [("g2", 5), ("g0", 6), ("g1", 6)])
+        hold("w2c_codes", [("g2", 5), ("g0", 6), ("g1", 6)])
         got[("g2", 6)] = got[("g1", 5)]
         gather(5, 2)
         edge_gather(6, 0, 0)

@@ -77,9 +77,9 @@ def tile_picked_wedgecv_relu_lo_kernel(
         nc.sync.dma_start(out=x_codes[:].bitcast(I32), in_=x_words[0].rearrange("p n t -> p (n t)").bitcast(I32))
         load_scales(x_plane, x_scales)
         nc.sync.dma_start(out=w3_raw[:].bitcast(I32), in_=w3_words[0].rearrange("p n t -> p (n t)").bitcast(I32))
-        nc.sync.dma_start(lists[0][:], pos1)
         first_room = sb([P, 5 * HALF], F32, "first_room")
         w2_raw.append(load_weight(w2, 1, first_room[:, HALF:]))
+        nc.sync.dma_start(lists[0][:], pos1)
         nc.sync.dma_start(lists[1][:], pos2)
         nc.sync.dma_start(lists[2][:], pos3)
         w1_raw = [
@@ -96,9 +96,12 @@ def tile_picked_wedgecv_relu_lo_kernel(
         def high_view(grouped, half):
             return grouped.rearrange("p (t h m j) -> p h m j t", t=2, h=2, j=4)[:, half]
 
-        def quantize(grouped, name, tag=None):
+        def quantize(grouped, name, offset=None):
             words = grouped.shape[1] // 4
-            codes = sb([P, words], U32, name + "_codes", tag)
+            if offset is None:
+                codes = sb([P, words], U32, name + "_codes")
+            else:
+                codes = shared.tile([P, words], U32, name=name + "_codes", offset=offset, align_bytes=64)
             plane = sb([P, words], U8, name + "_plane")
             nc.vector.quantize_mx(out=codes[:].bitcast(FP8X4), scales=plane[:], in_=grouped)
             return [(codes[:, n * P : (n + 1) * P], plane[:, n * P : (n + 1) * P]) for n in range(words // P)]
@@ -151,12 +154,12 @@ def tile_picked_wedgecv_relu_lo_kernel(
                             SUBTRACT,
                         )
 
-        def excess(unit):
+        def excess(unit, cols=slice(None)):
             nc.vector.scalar_tensor_tensor(
-                out=place("top", unit),
-                in0=got[("g1", unit)],
+                out=place("top", unit)[:, cols],
+                in0=got[("g1", unit)][:, cols],
                 scalar=0.0,
-                in1=got[("g2", unit)],
+                in1=got[("g2", unit)][:, cols],
                 op0=MAX,
                 op1=MAX,
             )
@@ -166,7 +169,7 @@ def tile_picked_wedgecv_relu_lo_kernel(
 
         z_low = [sb([P, T], BF16, "z_low%d" % n) for n in range(2)]
         z_high = [sb([P, HALF], BF16, "z_high%d" % b) for b in range(3)]
-        z_bf = {b: sb([P, cols], BF16, "z_bf%d" % b) for b, cols in ((0, 2 * T), (2, T), (3, T))}
+        z_bf = {b: sb([P, cols], BF16, "z_bf%d" % b) for b, cols in ((0, 2 * T), (2, T))}
 
         def edge_sum(unit, n, acc):
             pieces = [(c, first + v) for c, first, count in UNITS[unit] for v in range(0, count, P)]
@@ -178,6 +181,16 @@ def tile_picked_wedgecv_relu_lo_kernel(
 
         def slot(bank, n, count=1):
             return banks[bank][:, n * P : (n + count) * P]
+
+        def open_sums(unit, bank):
+            pieces = [(c, first + v) for c, first, count in UNITS[unit] for v in range(0, count, P)]
+            for n, (c, first) in enumerate(pieces):
+                for k, term in enumerate((y[c][:, first : first + P], got[("g0", unit)][:, n * P : (n + 1) * P])):
+                    nc.tensor.matmul(slot(bank, n), term, ident[:], start=n + k == 0, stop=False, is_transpose=True)
+
+        def close_sum(unit, bank, n):
+            excess_part = got[("top", unit)][:, n * P : (n + 1) * P]
+            nc.tensor.matmul(slot(bank, n), excess_part, ident[:], start=False, stop=n == 1, is_transpose=True)
 
         def relu_low_pair(c, pair, src):
             nc.scalar.activation(
@@ -218,7 +231,7 @@ def tile_picked_wedgecv_relu_lo_kernel(
                 ADD,
             )
 
-        results = [sb([P, 2 * T], F32, "result%d" % n) for n in range(2)]
+        results = {block: sb([P, T], F32, "result%d" % block)[:] for block in range(4)}
         out_codes = sb([P, T], U32, "out_codes")
         out_plane = sb([P, T], U8, "out_plane")
 
@@ -246,7 +259,7 @@ def tile_picked_wedgecv_relu_lo_kernel(
             )
 
         def store(block, bank, second):
-            result = results[block // 2][:, block % 2 * T : (block % 2 + 1) * T]
+            result = results[block]
             if block == 3:
                 nc.scalar.copy(out=result[:, 0:HALF], in_=bank[:, 0:HALF])
                 nc.vector.tensor_copy(out=result[:, HALF:T], in_=second[:, HALF:T])
@@ -258,7 +271,7 @@ def tile_picked_wedgecv_relu_lo_kernel(
             )
 
         def round_out(block, grouped, copy):
-            result = results[block // 2][:, block % 2 * T : (block % 2 + 1) * T]
+            result = results[block]
             copy(
                 out=grouped.rearrange("p (s i t) -> p s t i", i=4, t=4),
                 in_=result.rearrange("p (t s i) -> p s t i", i=4, t=4),
@@ -277,27 +290,28 @@ def tile_picked_wedgecv_relu_lo_kernel(
         w2_bf0 = sb([P, T], BF16, "w2_bf0")
         w2_bf1 = sb([P, T], BF16, "w2_bf1")
         w2_bf23 = sb([P, 2 * T], BF16, "w2_bf23")
-        w1_low = sb([P, 2 * T], BF16, "w1_low")
-        w1_high = sb([P, 2 * T], BF16, "w1_high")
+        w1_bf = sb([P, 4 * T], BF16, "w1_bf")
+        w1_low = w1_bf[:, 0 : 2 * T]
+        w1_high = w1_bf[:, 2 * T :]
 
         nc.vector.tensor_copy(out=low_view(w2_bf0[:])[:, 0:VECTOR_GROUPS], in_=w2_raw[0][:, 0:VECTOR_GROUPS, :, 0:2])
         nc.scalar.copy(out=low_view(w2_bf0[:])[:, VECTOR_GROUPS:], in_=w2_raw[0][:, VECTOR_GROUPS:, :, 0:2])
         w2_q = quantize(w2_bf0[:], "w2a")
-        for half in range(2):
-            product(w2_q[0], banks[half][:, 0:HALF], e[0][:], slice(half * HALF, (half + 1) * HALF))
+        for half, copy in enumerate((nc.vector.tensor_copy, nc.scalar.copy)):
+            product(w2_q[0], banks[half][:, 0:HALF], e[0][:], slice(half * HALF, (half + 1) * HALF), copy)
         nc.scalar.copy(out=high_view(w2_bf23[:], 0), in_=w2_raw[0][:, :, :, 2:4])
         nc.scalar.copy(out=low_view(w2_bf1[:]), in_=w2_raw[1][:, :, :, 0:2])
         nc.scalar.copy(out=high_view(w2_bf23[:], 1), in_=w2_raw[1][:, :, :, 2:4])
-        w2_q = w2_q + quantize(w2_bf1[:], "w2b") + quantize(w2_bf23[:], "w2c")
+        w2_q = w2_q + quantize(w2_bf1[:], "w2b") + quantize(w2_bf23[:], "w2c", 8192)
         for half in range(2):
             nc.scalar.copy(out=low_view(w1_low[:, half * T : (half + 1) * T]), in_=w1_raw[half][:, :, :, 0:2])
-            nc.scalar.copy(out=high_view(w1_high[:], half), in_=w1_raw[half][:, :, :, 2:4])
+            nc.scalar.copy(out=high_view(w1_high, half), in_=w1_raw[half][:, :, :, 2:4])
             if half == 0:
                 e.append(shared.tile([P, T], F32, name="e1", offset=0))
                 product(w2_q[1], banks[2][:], e[1][:], slice(0, T))
                 e.append(shared.tile([P, T], F32, name="e2", offset=2048))
                 product(w2_q[2], banks[3][:], e[2][:], slice(0, T))
-        w1_q = quantize(w1_low[:], "w1a") + quantize(w1_high[:], "w1b")
+        w1_q = quantize(w1_bf[:], "w1")
         e.append(shared.tile([P, T], F32, name="e3", offset=4096))
         product(w2_q[3], banks[2][:], e[3][:], slice(0, T))
         for c, bank in enumerate((5, 0, 1, 4)):
@@ -305,12 +319,13 @@ def tile_picked_wedgecv_relu_lo_kernel(
 
         got[("g1", 0)] = first_room[:, 0:T]
         got[("g2", 0)] = first_room[:, T : 2 * T]
-        second_room = sb([P, T + HALF], F32, "second_room", "w2c_codes")
+        second_room = shared.tile([P, T + HALF], F32, name="second_room", offset=8192)
         got[("top", 0)] = second_room[:, 0:T]
         got[("g1", 1)] = second_room[:, T:]
         got[("g2", 1)] = shared.tile([P, HALF], F32, name="third", offset=6144)[:]
         for unit in (2, 3, 4):
             got[("g2", unit)] = got[("g2", 1)]
+        got[("g1", 3)] = shared.tile([P, HALF], F32, name="late_first", offset=12288)[:]
         gather(0, 0)
         for unit in range(5):
             gather(unit, 1)
@@ -320,13 +335,13 @@ def tile_picked_wedgecv_relu_lo_kernel(
             gather(unit + 1, 0)
             excess(unit)
         gather(5, 1)
-        for n in range(3):
+        for n in range(4):
             edge_sum(0, n, slot(6, n))
         relu_low_pair(0, 0, slot(6, 0, 2))
         for n in range(2):
             edge_sum(1, n, slot(7, n))
         relu_low_pair(1, 0, slot(7, 0, 2))
-        nc.scalar.activation(z_low[1][:, 0:P], slot(6, 2), RELU)
+        relu_low_pair(0, 1, slot(6, 2, 2))
         for block in range(2):
             turn_low(block, slot(1 + block, 0))
         for unit in (2, 3):
@@ -339,52 +354,53 @@ def tile_picked_wedgecv_relu_lo_kernel(
         )
         for block in range(2):
             relu_high(block, slot(3 + block, 0, 2))
+        turn_high(0, slot(1, 1))
+        open_sums(4, 3)
+        turn_high(1, slot(2, 1))
+        close_sum(4, 3, 0)
+        close_sum(4, 3, 1)
         for block in range(2):
-            turn_high(block, slot(1 + block, 1))
-        w3_plane = sb([P, H], U8, "w3_plane", "z_high0")
+            regroup(z_bf[0][:, block * T : (block + 1) * T], slot(1 + block, 0, 2))
+        relu_low_pair(1, 1, slot(3, 0, 2))
+        open_sums(5, 2)
+        turn_low(2, slot(4, 0))
+
+        got[("g2", 5)] = got[("g2", 4)]
+        gather(5, 2)
+        for n in range(2):
+            excess(5, slice(n * P, (n + 1) * P))
+            close_sum(5, 2, n)
+        warm_up(banks[3])
+        z_first = quantize(z_bf[0][:], "z0")
+        w3_plane = shared.tile([P, H], U8, name="w3_plane", offset=12288, align_bytes=64)
         nc.vector.tensor_copy(
             out=w3_plane[:].rearrange("p (t s i) -> p s t i", t=4, i=16),
             in_=w3_raw_plane[:].rearrange("p (s i t) -> p s t i", t=4, i=16),
         )
-        for block in range(2):
-            regroup(z_bf[0][:, block * T : (block + 1) * T], slot(1 + block, 0, 2))
-        z_first = quantize(z_bf[0][:], "z0")
-        edge_sum(0, 3, slot(1, 2))
-        for n in range(2):
-            edge_sum(4, n, slot(1, n))
-        project(0, z_first[0], banks[0], banks[0])
-        project(1, z_first[1], banks[5], banks[5])
-        relu_low_pair(1, 1, slot(1, 0, 2))
-        nc.scalar.activation(z_low[1][:, HALF : HALF + P], slot(1, 2), RELU)
-        turn_low(2, slot(4, 0))
-        turn_low(3, slot(3, 0))
-        nc.scalar.copy(out=z_bf[3][:].bitcast(F32).rearrange("p (v u) -> p v u", u=2)[:, :, 0], in_=slot(3, 0))
-        store(0, banks[0], banks[0])
-        store(1, banks[5], banks[5])
-
-        hold("w2c_codes", [("g2", 5), ("g0", 6), ("g1", 6)])
-        got[("g2", 6)] = got[("g1", 5)]
-        gather(5, 2)
-        edge_gather(6, 0, 0)
-        edge_gather(6, 0, 1)
-        excess(5)
-        for n in range(2):
-            edge_sum(5, n, slot(7, n))
-        warm_up(banks[5])
-        relu_high(2, slot(7, 0, 2))
+        last_room = shared.tile([P, 3 * HALF], F32, name="last_room", offset=12288 + H)
+        for d in range(3):
+            got[("g%d" % d, 6)] = last_room[:, d * HALF : (d + 1) * HALF]
+        relu_high(2, slot(2, 0, 2))
         turn_high(2, slot(4, 1))
-        warm_up(banks[7])
-        warm_up(banks[7])
+        project(0, z_first[0], banks[2], banks[2])
         regroup(z_bf[2][:], slot(4, 0, 2))
+        turn_low(3, slot(4, 0))
+        project(1, z_first[1], banks[7], banks[7])
+        store(0, banks[2], banks[2])
+        warm_up(banks[2])
+        warm_up(banks[2])
 
-        edge_gather(6, 1, 0)
-        edge_gather(6, 1, 1)
+        for d in range(2):
+            for n in range(2):
+                edge_gather(6, d, n)
         edge_gather(6, 2, 0)
         larger("pair", 6, "g0", "g1")
         edge_gather(6, 2, 1)
-        hold("z_high2", [("rounded", 0)])
-        out_bf = {block: sb([P, T], BF16, "out_bf%d" % block)[:] for block in (2, 3)}
-        out_bf[0] = got[("rounded", 0)].bitcast(BF16)
+        z_third = quantize(z_bf[2][:], "z2")
+        z_bf[3] = sb([P, T], BF16, "z_bf3", "z_low1")
+        nc.scalar.copy(out=z_bf[3][:].bitcast(F32).rearrange("p (v u) -> p v u", u=2)[:, :, 0], in_=slot(4, 0))
+        store(1, banks[7], banks[7])
+        out_bf = {block: sb([P, T], BF16, "out_bf%d" % block)[:] for block in (0, 2, 3)}
         nc.vector.scalar_tensor_tensor(
             out=z_bf[3][:].rearrange("p (v u t) -> p v u t", u=2, t=2)[:, :, 1, :],
             in0=by_centre(got[("pair", 6)]),
@@ -393,21 +409,20 @@ def tile_picked_wedgecv_relu_lo_kernel(
             op0=MAX,
             op1=MAX,
         )
-        z_third = quantize(z_bf[2][:], "z2")
-        z_last = quantize(z_bf[3][:], "z3", "z_bf2")
-        out_bf[1] = sb([P, T], BF16, "out_bf1", "z_bf3")[:]
+        z_last = quantize(z_bf[3][:], "z3")
+        out_bf[1] = sb([P, T], BF16, "out_bf1", "z_low1")[:]
         project(2, z_third[0], banks[6], banks[6])
-        store(2, banks[6], banks[6])
         round_out(0, out_bf[0], nc.scalar.copy)
+        store(2, banks[6], banks[6])
         round_out(1, out_bf[1], nc.vector.tensor_copy)
         hand_on(0, out_bf[0])
         hand_on(1, out_bf[1])
-        round_out(2, out_bf[2], nc.vector.tensor_copy)
-        project(3, z_last[0], banks[3], banks[2])
-        store(3, banks[3], banks[2])
+        project(3, z_last[0], banks[3], banks[0])
+        store(3, banks[3], banks[0])
         store_codes(slice(0, HALF))
-        hand_on(2, out_bf[2])
+        round_out(2, out_bf[2], nc.vector.tensor_copy)
         round_out(3, out_bf[3], nc.vector.tensor_copy)
+        hand_on(2, out_bf[2])
         hand_on(3, out_bf[3])
         store_codes(slice(HALF, T))
         for q in range(4):

@@ -21,6 +21,8 @@ SUBTRACT = mybir.AluOpType.subtract
 P = 128
 HALF = 256
 VECTOR_GROUPS = 40
+W1_FIRST, W1_SECOND, LATE = 0, 4096, 12288
+E_BYTES = 4 * T
 UNITS = [
     [(0, 0, HALF), (0, HALF, HALF)],
     [(1, 0, HALF)],
@@ -83,8 +85,8 @@ def tile_picked_wedgecv_relu_lo_kernel(
         nc.sync.dma_start(lists[1][:], pos2)
         nc.sync.dma_start(lists[2][:], pos3)
         w1_raw = [
-            load_weight(w1, half, shared.tile([P, 4 * HALF], F32, name="w1_raw%d" % half, offset=half * 4096)[:])
-            for half in range(2)
+            load_weight(w1, half, shared.tile([P, 4 * HALF], F32, name="w1_raw%d" % half, offset=offset)[:])
+            for half, offset in enumerate((W1_FIRST, W1_SECOND))
         ]
         load_scales(w3_raw_plane, w3_scales)
 
@@ -96,12 +98,9 @@ def tile_picked_wedgecv_relu_lo_kernel(
         def high_view(grouped, half):
             return grouped.rearrange("p (t h m j) -> p h m j t", t=2, h=2, j=4)[:, half]
 
-        def quantize(grouped, name, offset=None):
+        def quantize(grouped, name):
             words = grouped.shape[1] // 4
-            if offset is None:
-                codes = sb([P, words], U32, name + "_codes")
-            else:
-                codes = shared.tile([P, words], U32, name=name + "_codes", offset=offset, align_bytes=64)
+            codes = sb([P, words], U32, name + "_codes")
             plane = sb([P, words], U8, name + "_plane")
             nc.vector.quantize_mx(out=codes[:].bitcast(FP8X4), scales=plane[:], in_=grouped)
             return [(codes[:, n * P : (n + 1) * P], plane[:, n * P : (n + 1) * P]) for n in range(words // P)]
@@ -120,39 +119,30 @@ def tile_picked_wedgecv_relu_lo_kernel(
 
         got = {}
 
-        def width(unit):
-            return sum(piece[2] for piece in UNITS[unit])
-
-        def hold(tag, steps):
-            held = sb([P, len(steps) * HALF], F32, "held_%s_%s" % steps[0], tag=tag)
-            got[tag] = held
-            for n, step in enumerate(steps):
-                got[step] = held[:, n * HALF : (n + 1) * HALF]
-
         def place(kind, unit):
             if (kind, unit) not in got:
-                got[(kind, unit)] = sb([P, width(unit)], F32, "%s_%d" % (kind, unit))[:]
+                width = sum(piece[2] for piece in UNITS[unit])
+                got[(kind, unit)] = sb([P, width], F32, "%s_%d" % (kind, unit))[:]
             return got[(kind, unit)]
 
-        def gathers(*units):
-            return [("g%d" % d, unit) for unit in units for d in range(3)]
+        def part(ap, n):
+            return ap[:, n * P : (n + 1) * P]
 
         def window(c, d, first, count):
             return e[c][:].indirect(lists[d][:, first // 16 : (first + count) // 16])
 
-        def gather(unit, d, pieces=(0, 1)):
+        def gather(unit, d):
             for n, (c, first, count) in enumerate(UNITS[unit]):
-                if n in pieces:
-                    cols = slice(n * count, (n + 1) * count)
-                    if d == 0:
-                        nc.vector.tensor_copy(place("g0", unit)[:, cols], window(c, d, first, count))
-                    else:
-                        nc.vector.tensor_tensor(
-                            place("g%d" % d, unit)[:, cols],
-                            window(c, d, first, count),
-                            got[("g0", unit)][:, cols],
-                            SUBTRACT,
-                        )
+                cols = slice(n * count, (n + 1) * count)
+                if d == 0:
+                    nc.vector.tensor_copy(place("g0", unit)[:, cols], window(c, d, first, count))
+                else:
+                    nc.vector.tensor_tensor(
+                        place("g%d" % d, unit)[:, cols],
+                        window(c, d, first, count),
+                        got[("g0", unit)][:, cols],
+                        SUBTRACT,
+                    )
 
         def excess(unit, cols=slice(None)):
             nc.vector.scalar_tensor_tensor(
@@ -164,33 +154,32 @@ def tile_picked_wedgecv_relu_lo_kernel(
                 op1=MAX,
             )
 
-        def larger(kind, unit, a, b):
-            nc.vector.tensor_tensor(place(kind, unit), got[(a, unit)], got[(b, unit)], MAX)
-
         z_low = [sb([P, T], BF16, "z_low%d" % n) for n in range(2)]
         z_high = [sb([P, HALF], BF16, "z_high%d" % b) for b in range(3)]
         z_bf = {b: sb([P, cols], BF16, "z_bf%d" % b) for b, cols in ((0, 2 * T), (2, T))}
 
-        def edge_sum(unit, n, acc):
-            pieces = [(c, first + v) for c, first, count in UNITS[unit] for v in range(0, count, P)]
-            c, first = pieces[n]
-            cols = slice(n * P, (n + 1) * P)
-            terms = (got[("top", unit)][:, cols], got[("g0", unit)][:, cols], y[c][:, first : first + P])
-            for k, term in enumerate(reversed(terms) if unit == 3 else terms):
-                nc.tensor.matmul(acc, term, ident[:], start=k == 0, stop=k == 2, is_transpose=True)
-
         def slot(bank, n, count=1):
             return banks[bank][:, n * P : (n + count) * P]
 
+        def add_term(bank, n, term, start, stop):
+            nc.tensor.matmul(slot(bank, n), term, ident[:], start=start, stop=stop, is_transpose=True)
+
+        def y_part(unit, n):
+            c, first = [(c, first + v) for c, first, count in UNITS[unit] for v in range(0, count, P)][n]
+            return y[c][:, first : first + P]
+
+        def edge_sum(unit, n, bank, at):
+            terms = (part(got[("top", unit)], n), part(got[("g0", unit)], n), y_part(unit, n))
+            for k, term in enumerate(reversed(terms) if unit == 3 else terms):
+                add_term(bank, at, term, k == 0, k == 2)
+
         def open_sums(unit, bank):
-            pieces = [(c, first + v) for c, first, count in UNITS[unit] for v in range(0, count, P)]
-            for n, (c, first) in enumerate(pieces):
-                for k, term in enumerate((y[c][:, first : first + P], got[("g0", unit)][:, n * P : (n + 1) * P])):
-                    nc.tensor.matmul(slot(bank, n), term, ident[:], start=n + k == 0, stop=False, is_transpose=True)
+            for n in range(2):
+                add_term(bank, n, y_part(unit, n), n == 0, False)
+                add_term(bank, n, part(got[("g0", unit)], n), False, False)
 
         def close_sum(unit, bank, n):
-            excess_part = got[("top", unit)][:, n * P : (n + 1) * P]
-            nc.tensor.matmul(slot(bank, n), excess_part, ident[:], start=False, stop=n == 1, is_transpose=True)
+            add_term(bank, n, part(got[("top", unit)], n), False, n == 1)
 
         def relu_low_pair(c, pair, src):
             nc.scalar.activation(
@@ -216,20 +205,12 @@ def tile_picked_wedgecv_relu_lo_kernel(
                 out=out.bitcast(F32).rearrange("p (v u) -> p v u", u=2), in_=src.rearrange("p (u v) -> p v u", u=2)
             )
 
-        def by_tile(ap):
-            return ap.rearrange("p (t v) -> p t v", t=2)
-
         def by_centre(ap):
             return ap.rearrange("p (t v) -> p v t", t=2)
 
-        def edge_gather(unit, d, n):
-            c, first, count = UNITS[unit][n]
-            nc.vector.tensor_tensor(
-                place("g%d" % d, unit)[:, n * count : (n + 1) * count],
-                window(c, d, first, count),
-                y[c][:, first : first + count],
-                ADD,
-            )
+        def last_gather(d, n):
+            c, first, count = UNITS[6][n]
+            nc.vector.tensor_tensor(part(got[("g%d" % d, 6)], n), window(c, d, first, count), y_part(6, n), ADD)
 
         results = {block: sb([P, T], F32, "result%d" % block)[:] for block in range(4)}
         out_codes = sb([P, T], U32, "out_codes")
@@ -302,30 +283,30 @@ def tile_picked_wedgecv_relu_lo_kernel(
         nc.scalar.copy(out=high_view(w2_bf23[:], 0), in_=w2_raw[0][:, :, :, 2:4])
         nc.scalar.copy(out=low_view(w2_bf1[:]), in_=w2_raw[1][:, :, :, 0:2])
         nc.scalar.copy(out=high_view(w2_bf23[:], 1), in_=w2_raw[1][:, :, :, 2:4])
-        w2_q = w2_q + quantize(w2_bf1[:], "w2b") + quantize(w2_bf23[:], "w2c", 8192)
+        w2_q = w2_q + quantize(w2_bf1[:], "w2b") + quantize(w2_bf23[:], "w2c")
         for half in range(2):
             nc.scalar.copy(out=low_view(w1_low[:, half * T : (half + 1) * T]), in_=w1_raw[half][:, :, :, 0:2])
             nc.scalar.copy(out=high_view(w1_high, half), in_=w1_raw[half][:, :, :, 2:4])
             if half == 0:
-                e.append(shared.tile([P, T], F32, name="e1", offset=0))
-                product(w2_q[1], banks[2][:], e[1][:], slice(0, T))
-                e.append(shared.tile([P, T], F32, name="e2", offset=2048))
-                product(w2_q[2], banks[3][:], e[2][:], slice(0, T))
+                for c in (1, 2):
+                    e.append(shared.tile([P, T], F32, name="e%d" % c, offset=W1_FIRST + (c - 1) * E_BYTES))
+                    product(w2_q[c], banks[c + 1][:], e[c][:], slice(0, T))
         w1_q = quantize(w1_bf[:], "w1")
-        e.append(shared.tile([P, T], F32, name="e3", offset=4096))
-        product(w2_q[3], banks[2][:], e[3][:], slice(0, T))
-        for c, bank in enumerate((5, 0, 1, 4)):
+        e.append(shared.tile([P, T], F32, name="e3", offset=W1_SECOND))
+        product(w2_q[3], banks[4][:], e[3][:], slice(0, T))
+        for c, bank in enumerate((5, 0, 1, 6)):
             product(w1_q[c], banks[bank][:], y[c], slice(0, T))
 
         got[("g1", 0)] = first_room[:, 0:T]
         got[("g2", 0)] = first_room[:, T : 2 * T]
-        second_room = shared.tile([P, T + HALF], F32, name="second_room", offset=8192)
-        got[("top", 0)] = second_room[:, 0:T]
-        got[("g1", 1)] = second_room[:, T:]
-        got[("g2", 1)] = shared.tile([P, HALF], F32, name="third", offset=6144)[:]
-        for unit in (2, 3, 4):
+        second_room = sb([P, 8 * P], F32, "second_room")
+        got[("g0", 0)] = second_room[:, P : 5 * P]
+        got[("top", 0)] = second_room[:, 4 * P : 8 * P]
+        got[("g1", 1)] = second_room[:, 0:HALF]
+        got[("g2", 1)] = shared.tile([P, HALF], F32, name="third", offset=W1_SECOND + E_BYTES)[:]
+        for unit in range(2, 6):
             got[("g2", unit)] = got[("g2", 1)]
-        got[("g1", 3)] = shared.tile([P, HALF], F32, name="late_first", offset=12288)[:]
+        got[("g1", 3)] = shared.tile([P, HALF], F32, name="late_first", offset=LATE)[:]
         gather(0, 0)
         for unit in range(5):
             gather(unit, 1)
@@ -333,20 +314,25 @@ def tile_picked_wedgecv_relu_lo_kernel(
             if unit > 0:
                 got[("g0", unit + 1)] = got[("g1", unit - 1)][:, 0:HALF]
             gather(unit + 1, 0)
+            if unit == 0:
+                for k, n in enumerate((1, 2, 3, 0)):
+                    add_term(2, n, part(got[("g0", 0)], n), k == 0, False)
             excess(unit)
         gather(5, 1)
         for n in range(4):
-            edge_sum(0, n, slot(6, n))
-        relu_low_pair(0, 0, slot(6, 0, 2))
+            add_term(2, n, part(got[("top", 0)], n), False, False)
+        for n in range(4):
+            add_term(2, n, y_part(0, n), False, n == 3)
+        relu_low_pair(0, 0, slot(2, 0, 2))
         for n in range(2):
-            edge_sum(1, n, slot(7, n))
+            edge_sum(1, n, 7, n)
         relu_low_pair(1, 0, slot(7, 0, 2))
-        relu_low_pair(0, 1, slot(6, 2, 2))
+        relu_low_pair(0, 1, slot(2, 2, 2))
         for block in range(2):
             turn_low(block, slot(1 + block, 0))
         for unit in (2, 3):
             for block in range(2):
-                edge_sum(unit, block, slot(3 + block, unit - 2))
+                edge_sum(unit, block, 3 + block, unit - 2)
         w3_codes = sb([P, H], U32, "w3_codes")
         nc.vector.tensor_copy(
             out=w3_codes[:].bitcast(I32).rearrange("p (t s i) -> p s t i", t=4, i=4),
@@ -365,19 +351,18 @@ def tile_picked_wedgecv_relu_lo_kernel(
         open_sums(5, 2)
         turn_low(2, slot(4, 0))
 
-        got[("g2", 5)] = got[("g2", 4)]
         gather(5, 2)
         for n in range(2):
             excess(5, slice(n * P, (n + 1) * P))
             close_sum(5, 2, n)
         warm_up(banks[3])
         z_first = quantize(z_bf[0][:], "z0")
-        w3_plane = shared.tile([P, H], U8, name="w3_plane", offset=12288, align_bytes=64)
+        w3_plane = shared.tile([P, H], U8, name="w3_plane", offset=LATE, align_bytes=64)
         nc.vector.tensor_copy(
             out=w3_plane[:].rearrange("p (t s i) -> p s t i", t=4, i=16),
             in_=w3_raw_plane[:].rearrange("p (s i t) -> p s t i", t=4, i=16),
         )
-        last_room = shared.tile([P, 3 * HALF], F32, name="last_room", offset=12288 + H)
+        last_room = shared.tile([P, 3 * HALF], F32, name="last_room", offset=LATE + H)
         for d in range(3):
             got[("g%d" % d, 6)] = last_room[:, d * HALF : (d + 1) * HALF]
         relu_high(2, slot(2, 0, 2))
@@ -392,10 +377,10 @@ def tile_picked_wedgecv_relu_lo_kernel(
 
         for d in range(2):
             for n in range(2):
-                edge_gather(6, d, n)
-        edge_gather(6, 2, 0)
-        larger("pair", 6, "g0", "g1")
-        edge_gather(6, 2, 1)
+                last_gather(d, n)
+        last_gather(2, 0)
+        nc.vector.tensor_tensor(place("pair", 6), got[("g0", 6)], got[("g1", 6)], MAX)
+        last_gather(2, 1)
         z_third = quantize(z_bf[2][:], "z2")
         z_bf[3] = sb([P, T], BF16, "z_bf3", "z_low1")
         nc.scalar.copy(out=z_bf[3][:].bitcast(F32).rearrange("p (v u) -> p v u", u=2)[:, :, 0], in_=slot(4, 0))

@@ -21,7 +21,8 @@ SUBTRACT = mybir.AluOpType.subtract
 P = 128
 HALF = 256
 VECTOR_GROUPS = 40
-W1_FIRST, W1_SECOND, LATE = 0, 4096, 12288
+W1_FIRST, W1_SECOND, LATE, LOW = 0, 4096, 12288, 20480
+OVERLAP = 64
 E_BYTES = 4 * T
 UNITS = [
     [(0, 0, HALF), (0, HALF, HALF)],
@@ -144,19 +145,19 @@ def tile_picked_wedgecv_relu_lo_kernel(
                         SUBTRACT,
                     )
 
-        def excess(unit, cols=slice(None)):
+        def excess(unit):
             nc.vector.scalar_tensor_tensor(
-                out=place("top", unit)[:, cols],
-                in0=got[("g1", unit)][:, cols],
+                out=place("top", unit),
+                in0=got[("g1", unit)],
                 scalar=0.0,
-                in1=got[("g2", unit)][:, cols],
+                in1=got[("g2", unit)],
                 op0=MAX,
                 op1=MAX,
             )
 
-        z_low = [sb([P, T], BF16, "z_low%d" % n) for n in range(2)]
-        z_high = [sb([P, HALF], BF16, "z_high%d" % b) for b in range(3)]
-        z_bf = {b: sb([P, cols], BF16, "z_bf%d" % b) for b, cols in ((0, 2 * T), (2, T))}
+        z_low = [sb([P, T], BF16, "z_low0"), shared.tile([P, T], BF16, name="z_low1", offset=LOW)]
+        z_high = [sb([P, HALF], BF16, "z_high%d" % b) for b in range(2)]
+        z_early = sb([P, 2 * T], BF16, "z_early")
 
         def slot(bank, n, count=1):
             return banks[bank][:, n * P : (n + count) * P]
@@ -172,14 +173,6 @@ def tile_picked_wedgecv_relu_lo_kernel(
             terms = (part(got[("top", unit)], n), part(got[("g0", unit)], n), y_part(unit, n))
             for k, term in enumerate(reversed(terms) if unit == 3 else terms):
                 add_term(bank, at, term, k == 0, k == 2)
-
-        def open_sums(unit, bank):
-            for n in range(2):
-                add_term(bank, n, y_part(unit, n), n == 0, False)
-                add_term(bank, n, part(got[("g0", unit)], n), False, False)
-
-        def close_sum(unit, bank, n):
-            add_term(bank, n, part(got[("top", unit)], n), False, n == 1)
 
         def relu_low_pair(c, pair, src):
             nc.scalar.activation(
@@ -208,9 +201,27 @@ def tile_picked_wedgecv_relu_lo_kernel(
         def by_centre(ap):
             return ap.rearrange("p (t v) -> p v t", t=2)
 
-        def last_gather(d, n):
-            c, first, count = UNITS[6][n]
-            nc.vector.tensor_tensor(part(got[("g%d" % d, 6)], n), window(c, d, first, count), y_part(6, n), ADD)
+        def direct_gather(unit, d, n):
+            c, first, count = UNITS[unit][n]
+            nc.vector.tensor_tensor(part(got[("g%d" % d, unit)], n), window(c, d, first, count), y_part(unit, n), ADD)
+
+        def direct_gathers(unit):
+            for d in range(2):
+                for n in range(2):
+                    direct_gather(unit, d, n)
+            direct_gather(unit, 2, 0)
+            nc.vector.tensor_tensor(place("pair", unit), got[("g0", unit)], got[("g1", unit)], MAX)
+            direct_gather(unit, 2, 1)
+
+        def high_words(unit, z_block):
+            nc.vector.scalar_tensor_tensor(
+                out=z_block.rearrange("p (v u t) -> p v u t", u=2, t=2)[:, :, 1, :],
+                in0=by_centre(got[("pair", unit)]),
+                scalar=0.0,
+                in1=by_centre(got[("g2", unit)]),
+                op0=MAX,
+                op1=MAX,
+            )
 
         results = {block: sb([P, T], F32, "result%d" % block)[:] for block in range(4)}
         out_codes = sb([P, T], U32, "out_codes")
@@ -306,9 +317,9 @@ def tile_picked_wedgecv_relu_lo_kernel(
         got[("g2", 1)] = shared.tile([P, HALF], F32, name="third", offset=W1_SECOND + E_BYTES)[:]
         for unit in range(2, 6):
             got[("g2", unit)] = got[("g2", 1)]
-        got[("g1", 3)] = shared.tile([P, HALF], F32, name="late_first", offset=LATE)[:]
+        got[("g1", 3)] = shared.tile([P, HALF], F32, name="late_second", offset=LATE)[:]
         gather(0, 0)
-        for unit in range(5):
+        for unit in range(4):
             gather(unit, 1)
             gather(unit, 2)
             if unit > 0:
@@ -318,7 +329,17 @@ def tile_picked_wedgecv_relu_lo_kernel(
                 for k, n in enumerate((1, 2, 3, 0)):
                     add_term(2, n, part(got[("g0", 0)], n), k == 0, False)
             excess(unit)
-        gather(5, 1)
+        gather(4, 1)
+        gather(4, 2)
+        w3_plane = shared.tile([P, H], U8, name="w3_plane", offset=LATE + OVERLAP - H, align_bytes=64)
+        nc.vector.tensor_copy(
+            out=w3_plane[:].rearrange("p (t s i) -> p s t i", t=4, i=16),
+            in_=w3_raw_plane[:].rearrange("p (s i t) -> p s t i", t=4, i=16),
+        )
+        excess(4)
+        got[("g0", 5)] = shared.tile([P, HALF], F32, name="fifth_first", offset=LATE + OVERLAP)[:]
+        got[("g1", 5)] = got[("g1", 4)]
+        direct_gathers(5)
         for n in range(4):
             add_term(2, n, part(got[("top", 0)], n), False, False)
         for n in range(4):
@@ -341,61 +362,36 @@ def tile_picked_wedgecv_relu_lo_kernel(
         for block in range(2):
             relu_high(block, slot(3 + block, 0, 2))
         turn_high(0, slot(1, 1))
-        open_sums(4, 3)
-        turn_high(1, slot(2, 1))
-        close_sum(4, 3, 0)
-        close_sum(4, 3, 1)
-        for block in range(2):
-            regroup(z_bf[0][:, block * T : (block + 1) * T], slot(1 + block, 0, 2))
-        relu_low_pair(1, 1, slot(3, 0, 2))
-        open_sums(5, 2)
-        turn_low(2, slot(4, 0))
-
-        gather(5, 2)
         for n in range(2):
-            excess(5, slice(n * P, (n + 1) * P))
-            close_sum(5, 2, n)
-        warm_up(banks[3])
-        z_first = quantize(z_bf[0][:], "z0")
-        w3_plane = shared.tile([P, H], U8, name="w3_plane", offset=LATE, align_bytes=64)
-        nc.vector.tensor_copy(
-            out=w3_plane[:].rearrange("p (t s i) -> p s t i", t=4, i=16),
-            in_=w3_raw_plane[:].rearrange("p (s i t) -> p s t i", t=4, i=16),
-        )
-        last_room = shared.tile([P, 3 * HALF], F32, name="last_room", offset=LATE + H)
+            add_term(3, n, y_part(4, n), n == 0, False)
+            add_term(3, n, part(got[("g0", 4)], n), False, False)
+        turn_high(1, slot(2, 1))
+        for n in range(2):
+            add_term(3, n, part(got[("top", 4)], n), False, n == 1)
+        for block in range(2):
+            regroup(z_early[:, block * T : (block + 1) * T], slot(1 + block, 0, 2))
+        relu_low_pair(1, 1, slot(3, 0, 2))
+        for n in range(2):
+            turn_low(2 + n, slot(2, n))
+        z_first = quantize(z_early[:], "z0")
+        late_offset = LOW + OVERLAP - 4 * T
+        z_late = shared.tile([P, 2 * T], BF16, name="z_late", offset=late_offset, align_bytes=64)
+        nc.scalar.copy(out=z_late[:].bitcast(F32).rearrange("p (v u) -> p v u", u=2)[:, :, 0], in_=slot(2, 0, 2))
+        high_words(5, z_late[:, 0:T])
+        for block, bank in ((0, 5), (1, 7)):
+            project(block, z_first[block], banks[bank], banks[bank])
+            store(block, banks[bank], banks[bank])
+        for bank in (5, 5, 7):
+            warm_up(banks[bank])
+        last_room = shared.tile([P, 3 * HALF], F32, name="last_room", offset=LOW + OVERLAP)
         for d in range(3):
             got[("g%d" % d, 6)] = last_room[:, d * HALF : (d + 1) * HALF]
-        relu_high(2, slot(2, 0, 2))
-        turn_high(2, slot(4, 1))
-        project(0, z_first[0], banks[2], banks[2])
-        regroup(z_bf[2][:], slot(4, 0, 2))
-        turn_low(3, slot(4, 0))
-        project(1, z_first[1], banks[7], banks[7])
-        store(0, banks[2], banks[2])
-        warm_up(banks[2])
-        warm_up(banks[2])
-
-        for d in range(2):
-            for n in range(2):
-                last_gather(d, n)
-        last_gather(2, 0)
-        nc.vector.tensor_tensor(place("pair", 6), got[("g0", 6)], got[("g1", 6)], MAX)
-        last_gather(2, 1)
-        z_third = quantize(z_bf[2][:], "z2")
-        z_bf[3] = sb([P, T], BF16, "z_bf3", "z_low1")
-        nc.scalar.copy(out=z_bf[3][:].bitcast(F32).rearrange("p (v u) -> p v u", u=2)[:, :, 0], in_=slot(4, 0))
-        store(1, banks[7], banks[7])
+        direct_gathers(6)
+        z_third = quantize(z_late[:, 0:T], "z2")
+        high_words(6, z_late[:, T:])
+        z_last = quantize(z_late[:, T:], "z3")
         out_bf = {block: sb([P, T], BF16, "out_bf%d" % block)[:] for block in (0, 2, 3)}
-        nc.vector.scalar_tensor_tensor(
-            out=z_bf[3][:].rearrange("p (v u t) -> p v u t", u=2, t=2)[:, :, 1, :],
-            in0=by_centre(got[("pair", 6)]),
-            scalar=0.0,
-            in1=by_centre(got[("g2", 6)]),
-            op0=MAX,
-            op1=MAX,
-        )
-        z_last = quantize(z_bf[3][:], "z3")
-        out_bf[1] = sb([P, T], BF16, "out_bf1", "z_low1")[:]
+        out_bf[1] = shared.tile([P, T], BF16, name="out_bf1", offset=late_offset, align_bytes=64)[:]
         project(2, z_third[0], banks[6], banks[6])
         round_out(0, out_bf[0], nc.scalar.copy)
         store(2, banks[6], banks[6])

@@ -1,7 +1,6 @@
 from contextlib import ExitStack
 
 import concourse.mybir as mybir
-from concourse.masks import make_identity
 
 K, T, H = 512, 512, 512
 FLOPS = 3 * 2 * K * T * H
@@ -13,26 +12,16 @@ U32 = mybir.dt.uint32
 U16 = mybir.dt.uint16
 U8 = mybir.dt.uint8
 FP8X4 = mybir.dt.float8_e4m3fn_x4
-RELU = mybir.ActivationFunctionType.Relu
+COPY = mybir.ActivationFunctionType.Copy
 MAX = mybir.AluOpType.max
 ADD = mybir.AluOpType.add
-SUBTRACT = mybir.AluOpType.subtract
 
 P = 128
 HALF = 256
-VECTOR_GROUPS = 40
-W1_FIRST, W1_SECOND, LATE, LOW = 0, 4096, 12288, 20480
-OVERLAP = 64
-E_BYTES = 4 * T
-UNITS = [
-    [(0, 0, HALF), (0, HALF, HALF)],
-    [(1, 0, HALF)],
-    [(2, 0, HALF)],
-    [(3, 0, HALF)],
-    [(1, HALF, HALF)],
-    [(2, 2 * P, P), (3, 2 * P, P)],
-    [(2, 3 * P, P), (3, 3 * P, P)],
-]
+VECTOR_GROUPS = 42
+WIDE = 704
+W1_RAW = (4096, 16384)
+W1_BF = 28672
 
 
 def tile_picked_wedgecv_relu_lo_kernel(
@@ -44,23 +33,23 @@ def tile_picked_wedgecv_relu_lo_kernel(
         shared = ctx.enter_context(tc.tile_pool(name="shared", bufs=1))
         psum = ctx.enter_context(tc.psum_pool(name="psum", bufs=1))
 
-        def sb(shape, dtype, name, tag=None):
-            return keep.tile(shape, dtype, name=name, tag=tag or name, align_bytes=64)
+        def sb(shape, dtype, name):
+            return keep.tile(shape, dtype, name=name, tag=name, align_bytes=64)
+
+        def at(shape, dtype, name, offset):
+            return shared.tile(shape, dtype, name=name, offset=offset, align_bytes=64)
 
         lists = [keep.tile([P, T // 16], U16, name="pos%d" % d) for d in range(3)]
         x_codes = sb([P, T], U32, "x_codes")
         x_plane = sb([P, T], U8, "x_plane")
         w3_raw = sb([P, H], U32, "w3_raw")
         w3_raw_plane = sb([P, H], U8, "w3_raw_plane")
-        ident = sb([P, P], F32, "ident")
-        e = [sb([P, T], F32, "e0")]
-        y_low = [sb([P, T], F32, "y%d" % c) for c in range(2)]
-        y_high = sb([P, 2 * T], F32, "y_high")
-        y = [y_low[0][:], y_low[1][:], y_high[:, 0:T], y_high[:, T : 2 * T]]
+        e = [sb([P, WIDE if t < 2 else T], F32, "e%d" % t) for t in range(4)]
 
-        nc.gpsimd.memset(x_plane[:].bitcast(I32), 0)
-        nc.gpsimd.memset(w3_raw_plane[:].bitcast(I32), 0)
-        make_identity(nc, ident[:])
+        nc.vector.memset(x_plane[:].bitcast(I32), 0)
+        nc.vector.memset(w3_raw_plane[:].bitcast(I32), 0)
+        for t in range(2):
+            nc.vector.memset(e[t][:, T:], 0.0)
 
         def load_scales(plane, scales):
             for q in range(4):
@@ -77,27 +66,23 @@ def tile_picked_wedgecv_relu_lo_kernel(
             return raw.rearrange("p (j m t) -> p m j t", j=4, t=4)
 
         w2_raw = [load_weight(w2, 0, sb([P, 4 * HALF], F32, "w2_raw0")[:])]
-        nc.sync.dma_start(out=x_codes[:].bitcast(I32), in_=x_words[0].rearrange("p n t -> p (n t)").bitcast(I32))
         load_scales(x_plane, x_scales)
-        nc.sync.dma_start(out=w3_raw[:].bitcast(I32), in_=w3_words[0].rearrange("p n t -> p (n t)").bitcast(I32))
-        first_room = sb([P, 5 * HALF], F32, "first_room")
-        w2_raw.append(load_weight(w2, 1, first_room[:, HALF:]))
+        nc.sync.dma_start(out=x_codes[:].bitcast(I32), in_=x_words[0].rearrange("p n t -> p (n t)").bitcast(I32))
+        w2_raw.append(load_weight(w2, 1, sb([P, 4 * HALF], F32, "w2_raw1")[:]))
         nc.sync.dma_start(lists[0][:], pos1)
         nc.sync.dma_start(lists[1][:], pos2)
         nc.sync.dma_start(lists[2][:], pos3)
-        w1_raw = [
-            load_weight(w1, half, shared.tile([P, 4 * HALF], F32, name="w1_raw%d" % half, offset=offset)[:])
-            for half, offset in enumerate((W1_FIRST, W1_SECOND))
-        ]
+        w1_raw = [load_weight(w1, h, at([P, 4 * HALF], F32, "w1_raw%d" % h, W1_RAW[h])[:]) for h in range(2)]
+        nc.sync.dma_start(out=w3_raw[:].bitcast(I32), in_=w3_words[0].rearrange("p n t -> p (n t)").bitcast(I32))
         load_scales(w3_raw_plane, w3_scales)
 
         banks = [psum.tile([P, T], F32, name="bank%d" % n) for n in range(8)]
 
-        def low_view(grouped):
-            return grouped.rearrange("p (m t j) -> p m j t", t=2, j=4)
+        def grouped_view(grouped, half):
+            return grouped.rearrange("p (t h m j) -> p h m j t", t=4, h=2, j=4)[:, half]
 
-        def high_view(grouped, half):
-            return grouped.rearrange("p (t h m j) -> p h m j t", t=2, h=2, j=4)[:, half]
+        def scalar_copy(out, in_):
+            nc.scalar.activation(out, in_, COPY)
 
         def quantize(grouped, name):
             words = grouped.shape[1] // 4
@@ -106,172 +91,103 @@ def tile_picked_wedgecv_relu_lo_kernel(
             nc.vector.quantize_mx(out=codes[:].bitcast(FP8X4), scales=plane[:], in_=grouped)
             return [(codes[:, n * P : (n + 1) * P], plane[:, n * P : (n + 1) * P]) for n in range(words // P)]
 
-        def product(weight, acc, rows, cols, copy=nc.scalar.copy):
+        def mx(acc, weight, moving):
             nc.tensor.matmul_mx(
                 out=acc,
                 lhsT=weight[0].bitcast(FP8X4),
                 lhsT_scale=weight[1],
-                rhs=x_codes[:, cols].bitcast(FP8X4),
-                rhs_scale=x_plane[:, cols],
+                rhs=moving[0].bitcast(FP8X4),
+                rhs_scale=moving[1],
                 start=True,
                 stop=True,
             )
-            copy(out=rows[:, cols], in_=acc)
 
-        got = {}
+        def x_cols(first, count):
+            return x_codes[:, first : first + count], x_plane[:, first : first + count]
 
-        def place(kind, unit):
-            if (kind, unit) not in got:
-                width = sum(piece[2] for piece in UNITS[unit])
-                got[(kind, unit)] = sb([P, width], F32, "%s_%d" % (kind, unit))[:]
-            return got[(kind, unit)]
+        def part(ap, n, width=P):
+            return ap[:, n * width : (n + 1) * width]
 
-        def part(ap, n):
-            return ap[:, n * P : (n + 1) * P]
+        def window(t, d, first, count):
+            return e[t][:].indirect(lists[d][:, first // 16 : (first + count) // 16])
 
-        def window(c, d, first, count):
-            return e[c][:].indirect(lists[d][:, first // 16 : (first + count) // 16])
+        def woven(ap):
+            return ap.rearrange("p (s i t) -> p s t i", i=4, t=4)
 
-        def gather(unit, d):
-            for n, (c, first, count) in enumerate(UNITS[unit]):
-                cols = slice(n * count, (n + 1) * count)
-                if d == 0:
-                    nc.vector.tensor_copy(place("g0", unit)[:, cols], window(c, d, first, count))
-                else:
-                    nc.vector.tensor_tensor(
-                        place("g%d" % d, unit)[:, cols],
-                        window(c, d, first, count),
-                        got[("g0", unit)][:, cols],
-                        SUBTRACT,
-                    )
-
-        def excess(unit):
-            nc.vector.scalar_tensor_tensor(
-                out=place("top", unit),
-                in0=got[("g1", unit)],
-                scalar=0.0,
-                in1=got[("g2", unit)],
-                op0=MAX,
-                op1=MAX,
+        def by_tile(ap, width, n):
+            return ap.rearrange("p (t v) -> p t v", t=4)[:, :, n * P : (n + 1) * P].rearrange(
+                "p t (s i) -> p s t i", i=4
             )
 
-        z_low = [sb([P, T], BF16, "z_low0"), shared.tile([P, T], BF16, name="z_low1", offset=LOW)]
-        z_high = [sb([P, HALF], BF16, "z_high%d" % b) for b in range(2)]
+        w1_bf = at([P, 4 * T], BF16, "w1_bf", W1_BF)
+        w2_low = [sb([P, T], BF16, "w2_low%d" % h) for h in range(2)]
+        w2_high = sb([P, 2 * T], BF16, "w2_high")
+
+        def low_view(h):
+            return w2_low[h][:].rearrange("p (t m j) -> p m j t", t=2, j=4)
+
+        def high_view(h):
+            return w2_high[:].rearrange("p (t h m j) -> p h m j t", t=2, h=2, j=4)[:, h]
+
+        nc.vector.tensor_copy(out=low_view(0)[:, 0:VECTOR_GROUPS], in_=w2_raw[0][:, 0:VECTOR_GROUPS, :, 0:2])
+        scalar_copy(low_view(0)[:, VECTOR_GROUPS:], w2_raw[0][:, VECTOR_GROUPS:, :, 0:2])
+        w2_q = quantize(w2_low[0][:], "w2a")
+        scalar_copy(high_view(0), w2_raw[0][:, :, :, 2:4])
+        for h, copy in enumerate((nc.vector.tensor_copy, nc.scalar.copy)):
+            mx(banks[h][:, 0:HALF], w2_q[0], x_cols(h * HALF, HALF))
+            copy(out=part(e[0], h, HALF), in_=banks[h][:, 0:HALF])
+        nc.vector.tensor_copy(out=low_view(1), in_=w2_raw[1][:, :, :, 0:2])
+        nc.vector.tensor_copy(out=high_view(1), in_=w2_raw[1][:, :, :, 2:4])
+        w2_q = w2_q + quantize(w2_low[1][:], "w2b") + quantize(w2_high[:], "w2c")
+        e_banks = [None, banks[2], banks[3], banks[0]]
+        for t in (1, 2, 3):
+            mx(e_banks[t][:], w2_q[t], x_cols(0, T))
+
+        raw = [[sb([P, T], F32, "raw%d_%d" % (d, t)) for t in range(2)] for d in range(3)]
+        ab = [sb([P, T], F32, "ab0"), sb([P, T], F32, "ab1"), at([P, T], F32, "ab01", W1_BF)]
+        m = sb([P, 4 * T], F32, "m")
+        m_second = at([P, T], F32, "m_second", W1_RAW[0])
+        m_view = m[:].rearrange("p (t v) -> p t v", t=4)
+        z_sum = sb([P, 2 * T], BF16, "z_sum")
+        z_sum_late = [sb([P, T], BF16, "z_sum%d" % b) for b in (2, 3)]
         z_early = sb([P, 2 * T], BF16, "z_early")
+        z_late = [sb([P, T], BF16, "z%d" % b) for b in (2, 3)]
+        y_banks = banks[4:8]
 
-        def slot(bank, n, count=1):
-            return banks[bank][:, n * P : (n + count) * P]
+        def vector_copy(out, in_):
+            nc.vector.tensor_copy(out, in_)
 
-        def add_term(bank, n, term, start, stop):
-            nc.tensor.matmul(slot(bank, n), term, ident[:], start=start, stop=stop, is_transpose=True)
+        def top(out, in0, in1):
+            nc.vector.tensor_tensor(out, in0, in1, MAX)
 
-        def y_part(unit, n):
-            c, first = [(c, first + v) for c, first, count in UNITS[unit] for v in range(0, count, P)][n]
-            return y[c][:, first : first + P]
+        def pair(ap):
+            return ap.rearrange("p (t v) -> p t v", t=2)
 
-        def edge_sum(unit, n, bank, at):
-            terms = (part(got[("top", unit)], n), part(got[("g0", unit)], n), y_part(unit, n))
-            for k, term in enumerate(reversed(terms) if unit == 3 else terms):
-                add_term(bank, at, term, k == 0, k == 2)
+        def add_y(block, out):
+            nc.vector.tensor_tensor(woven(out), by_tile(y_banks[block][:], P, 0), by_tile(m[:], P, block), ADD)
 
-        def relu_low_pair(c, pair, src):
-            nc.scalar.activation(
-                z_low[pair][:].rearrange("v (b c s) -> v c b s", b=2, c=2)[:, c],
-                src.rearrange("v (b s) -> v b s", b=2),
-                RELU,
-            )
-
-        def relu_high(block, src):
-            nc.scalar.activation(
-                z_high[block][:].rearrange("v (q t) -> v q t", t=2), src.rearrange("v (t q) -> v q t", t=2), RELU
-            )
-
-        def turn_low(block, acc):
-            pairs = z_low[block // 2][:].bitcast(F32)[:, block % 2 * P : (block % 2 + 1) * P]
-            nc.tensor.transpose(acc, pairs, ident[:])
-
-        def turn_high(block, acc):
-            nc.tensor.transpose(acc, z_high[block][:].bitcast(F32), ident[:])
-
-        def regroup(out, src):
-            nc.scalar.copy(
-                out=out.bitcast(F32).rearrange("p (v u) -> p v u", u=2), in_=src.rearrange("p (u v) -> p v u", u=2)
-            )
-
-        def by_centre(ap):
-            return ap.rearrange("p (t v) -> p v t", t=2)
-
-        def direct_gather(unit, d, n):
-            c, first, count = UNITS[unit][n]
-            nc.vector.tensor_tensor(part(got[("g%d" % d, unit)], n), window(c, d, first, count), y_part(unit, n), ADD)
-
-        def direct_gathers(unit):
-            for d in range(2):
-                for n in range(2):
-                    direct_gather(unit, d, n)
-            direct_gather(unit, 2, 0)
-            nc.vector.tensor_tensor(place("pair", unit), got[("g0", unit)], got[("g1", unit)], MAX)
-            direct_gather(unit, 2, 1)
-
-        def high_words(unit, z_block):
-            nc.vector.scalar_tensor_tensor(
-                out=z_block.rearrange("p (v u t) -> p v u t", u=2, t=2)[:, :, 1, :],
-                in0=by_centre(got[("pair", unit)]),
-                scalar=0.0,
-                in1=by_centre(got[("g2", unit)]),
-                op0=MAX,
-                op1=MAX,
-            )
-
-        results = {block: sb([P, T], F32, "result%d" % block)[:] for block in range(4)}
+        results = [sb([P, T], F32, "result%d" % b) for b in range(4)]
+        out_bf = [sb([P, T], BF16, "out_bf%d" % b) for b in range(4)]
         out_codes = sb([P, T], U32, "out_codes")
         out_plane = sb([P, T], U8, "out_plane")
 
-        def project(block, z_q, bank, second):
+        def project(z_q, bank, second):
             for t in range(4):
-                nc.tensor.matmul_mx(
-                    out=(bank if t < 2 else second)[:, t * P : (t + 1) * P],
-                    lhsT=w3_codes[:, t * P : (t + 1) * P].bitcast(FP8X4),
-                    lhsT_scale=w3_plane[:, t * P : (t + 1) * P],
-                    rhs=z_q[0].bitcast(FP8X4),
-                    rhs_scale=z_q[1],
-                    start=True,
-                    stop=True,
-                )
+                mx(part(bank if t < 2 else second, t), w3_q[t], z_q)
 
-        def warm_up(bank):
-            nc.tensor.matmul_mx(
-                out=bank[:],
-                lhsT=w1_q[3][0].bitcast(FP8X4),
-                lhsT_scale=w1_q[3][1],
-                rhs=x_codes[:].bitcast(FP8X4),
-                rhs_scale=x_plane[:],
-                start=True,
-                stop=True,
-            )
-
-        def store(block, bank, second):
-            result = results[block]
-            if block == 3:
-                nc.scalar.copy(out=result[:, 0:HALF], in_=bank[:, 0:HALF])
-                nc.vector.tensor_copy(out=result[:, HALF:T], in_=second[:, HALF:T])
-            else:
-                nc.scalar.copy(out=result, in_=bank[:])
+        def store(block):
             nc.sync.dma_start(
                 out=out_0.rearrange("(p t) v -> p t v", t=4)[:, :, block * P : (block + 1) * P],
-                in_=result.rearrange("p (t v) -> p t v", t=4),
+                in_=results[block][:].rearrange("p (t v) -> p t v", t=4),
             )
 
-        def round_out(block, grouped, copy):
-            result = results[block]
-            copy(
-                out=grouped.rearrange("p (s i t) -> p s t i", i=4, t=4),
-                in_=result.rearrange("p (t s i) -> p s t i", i=4, t=4),
-            )
+        def round_out(block, copy, src):
+            copy(out=woven(out_bf[block][:]), in_=by_tile(src, P, 0))
 
-        def hand_on(block, grouped):
-            cols = slice(block * P, (block + 1) * P)
-            nc.vector.quantize_mx(out=out_codes[:, cols].bitcast(FP8X4), scales=out_plane[:, cols], in_=grouped)
+        def hand_on(block):
+            nc.vector.quantize_mx(
+                out=part(out_codes, block).bitcast(FP8X4), scales=part(out_plane, block), in_=out_bf[block][:]
+            )
 
         def store_codes(cols):
             nc.sync.dma_start(
@@ -279,133 +195,87 @@ def tile_picked_wedgecv_relu_lo_kernel(
                 in_=out_codes[:, cols].bitcast(I32),
             )
 
-        w2_bf0 = sb([P, T], BF16, "w2_bf0")
-        w2_bf1 = sb([P, T], BF16, "w2_bf1")
-        w2_bf23 = sb([P, 2 * T], BF16, "w2_bf23")
-        w1_bf = sb([P, 4 * T], BF16, "w1_bf")
-        w1_low = w1_bf[:, 0 : 2 * T]
-        w1_high = w1_bf[:, 2 * T :]
-
-        nc.vector.tensor_copy(out=low_view(w2_bf0[:])[:, 0:VECTOR_GROUPS], in_=w2_raw[0][:, 0:VECTOR_GROUPS, :, 0:2])
-        nc.scalar.copy(out=low_view(w2_bf0[:])[:, VECTOR_GROUPS:], in_=w2_raw[0][:, VECTOR_GROUPS:, :, 0:2])
-        w2_q = quantize(w2_bf0[:], "w2a")
-        for half, copy in enumerate((nc.vector.tensor_copy, nc.scalar.copy)):
-            product(w2_q[0], banks[half][:, 0:HALF], e[0][:], slice(half * HALF, (half + 1) * HALF), copy)
-        nc.scalar.copy(out=high_view(w2_bf23[:], 0), in_=w2_raw[0][:, :, :, 2:4])
-        nc.scalar.copy(out=low_view(w2_bf1[:]), in_=w2_raw[1][:, :, :, 0:2])
-        nc.scalar.copy(out=high_view(w2_bf23[:], 1), in_=w2_raw[1][:, :, :, 2:4])
-        w2_q = w2_q + quantize(w2_bf1[:], "w2b") + quantize(w2_bf23[:], "w2c")
-        for half in range(2):
-            nc.scalar.copy(out=low_view(w1_low[:, half * T : (half + 1) * T]), in_=w1_raw[half][:, :, :, 0:2])
-            nc.scalar.copy(out=high_view(w1_high, half), in_=w1_raw[half][:, :, :, 2:4])
-            if half == 0:
-                for c in (1, 2):
-                    e.append(shared.tile([P, T], F32, name="e%d" % c, offset=W1_FIRST + (c - 1) * E_BYTES))
-                    product(w2_q[c], banks[c + 1][:], e[c][:], slice(0, T))
+        for t in range(2):
+            for d in range(2):
+                scalar_copy(raw[d][t][:], window(t, d, 0, T))
+            if t == 0:
+                vector_copy(raw[2][0][:], window(0, 2, 0, T))
+                vector_copy(e[1][:, 0:T], e_banks[1][:])
+        top(ab[0][:], raw[0][0][:], raw[1][0][:])
+        vector_copy(raw[2][1][:], window(1, 2, 0, T))
+        top(m_view[:, 0], ab[0][:], raw[2][0][:])
+        nc.sync.dma_start(out=m[0:64, T : 2 * T], in_=m[64:P, 0:T])
+        vector_copy(e[2][:], e_banks[2][:])
+        nc.scalar.copy(out=e[3][:], in_=e_banks[3][:])
+        top(ab[1][:], raw[0][1][:], raw[1][1][:])
+        vector_copy(grouped_view(w1_bf[:], 0), w1_raw[0])
+        top(m_second[:], ab[1][:], raw[2][1][:])
+        vector_copy(grouped_view(w1_bf[:], 1), w1_raw[1])
+        nc.sync.dma_start(out=m[64:P, 0:T], in_=m_second[0:64, :])
+        nc.sync.dma_start(out=m[64:P, T : 2 * T], in_=m_second[64:P, :])
         w1_q = quantize(w1_bf[:], "w1")
-        e.append(shared.tile([P, T], F32, name="e3", offset=W1_SECOND))
-        product(w2_q[3], banks[4][:], e[3][:], slice(0, T))
-        for c, bank in enumerate((5, 0, 1, 6)):
-            product(w1_q[c], banks[bank][:], y[c], slice(0, T))
-
-        got[("g1", 0)] = first_room[:, 0:T]
-        got[("g2", 0)] = first_room[:, T : 2 * T]
-        second_room = sb([P, 8 * P], F32, "second_room")
-        got[("g0", 0)] = second_room[:, P : 5 * P]
-        got[("top", 0)] = second_room[:, 4 * P : 8 * P]
-        got[("g1", 1)] = second_room[:, 0:HALF]
-        got[("g2", 1)] = shared.tile([P, HALF], F32, name="third", offset=W1_SECOND + E_BYTES)[:]
-        for unit in range(2, 6):
-            got[("g2", unit)] = got[("g2", 1)]
-        got[("g1", 3)] = shared.tile([P, HALF], F32, name="late_second", offset=LATE)[:]
-        gather(0, 0)
-        for unit in range(4):
-            gather(unit, 1)
-            gather(unit, 2)
-            if unit > 0:
-                got[("g0", unit + 1)] = got[("g1", unit - 1)][:, 0:HALF]
-            gather(unit + 1, 0)
-            if unit == 0:
-                for k, n in enumerate((1, 2, 3, 0)):
-                    add_term(2, n, part(got[("g0", 0)], n), k == 0, False)
-            excess(unit)
-        gather(4, 1)
-        gather(4, 2)
-        w3_plane = shared.tile([P, H], U8, name="w3_plane", offset=LATE + OVERLAP - H, align_bytes=64)
-        nc.vector.tensor_copy(
-            out=w3_plane[:].rearrange("p (t s i) -> p s t i", t=4, i=16),
-            in_=w3_raw_plane[:].rearrange("p (s i t) -> p s t i", t=4, i=16),
+        for block in range(4):
+            for t in range(4):
+                mx(part(y_banks[block], t), w1_q[t], x_cols(block * P, P))
+        w3_codes = at([P, H], U32, "w3_codes", W1_RAW[1])
+        vector_copy(
+            w3_codes[:].bitcast(I32).rearrange("p (t s i) -> p s t i", t=4, i=4),
+            w3_raw[:].bitcast(I32).rearrange("p (s i t) -> p s t i", t=4, i=4),
         )
-        excess(4)
-        got[("g0", 5)] = shared.tile([P, HALF], F32, name="fifth_first", offset=LATE + OVERLAP)[:]
-        got[("g1", 5)] = got[("g1", 4)]
-        direct_gathers(5)
-        for n in range(4):
-            add_term(2, n, part(got[("top", 0)], n), False, False)
-        for n in range(4):
-            add_term(2, n, y_part(0, n), False, n == 3)
-        relu_low_pair(0, 0, slot(2, 0, 2))
-        for n in range(2):
-            edge_sum(1, n, 7, n)
-        relu_low_pair(1, 0, slot(7, 0, 2))
-        relu_low_pair(0, 1, slot(2, 2, 2))
-        for block in range(2):
-            turn_low(block, slot(1 + block, 0))
-        for unit in (2, 3):
-            for block in range(2):
-                edge_sum(unit, block, 3 + block, unit - 2)
-        w3_codes = sb([P, H], U32, "w3_codes")
-        nc.vector.tensor_copy(
-            out=w3_codes[:].bitcast(I32).rearrange("p (t s i) -> p s t i", t=4, i=4),
-            in_=w3_raw[:].bitcast(I32).rearrange("p (s i t) -> p s t i", t=4, i=4),
-        )
-        for block in range(2):
-            relu_high(block, slot(3 + block, 0, 2))
-        turn_high(0, slot(1, 1))
-        for n in range(2):
-            add_term(3, n, y_part(4, n), n == 0, False)
-            add_term(3, n, part(got[("g0", 4)], n), False, False)
-        turn_high(1, slot(2, 1))
-        for n in range(2):
-            add_term(3, n, part(got[("top", 4)], n), False, n == 1)
-        for block in range(2):
-            regroup(z_early[:, block * T : (block + 1) * T], slot(1 + block, 0, 2))
-        relu_low_pair(1, 1, slot(3, 0, 2))
-        for n in range(2):
-            turn_low(2 + n, slot(2, n))
-        z_first = quantize(z_early[:], "z0")
-        late_offset = LOW + OVERLAP - 4 * T
-        z_late = shared.tile([P, 2 * T], BF16, name="z_late", offset=late_offset, align_bytes=64)
-        nc.scalar.copy(out=z_late[:].bitcast(F32).rearrange("p (v u) -> p v u", u=2)[:, :, 0], in_=slot(2, 0, 2))
-        high_words(5, z_late[:, 0:T])
-        for block, bank in ((0, 5), (1, 7)):
-            project(block, z_first[block], banks[bank], banks[bank])
-            store(block, banks[bank], banks[bank])
-        for bank in (5, 5, 7):
-            warm_up(banks[bank])
-        last_room = shared.tile([P, 3 * HALF], F32, name="last_room", offset=LOW + OVERLAP)
+        early = [sb([P, T], F32, "early%d" % d) for d in range(3)]
+        late = [sb([P, T], F32, "late%d" % d) for d in range(3)]
         for d in range(3):
-            got[("g%d" % d, 6)] = last_room[:, d * HALF : (d + 1) * HALF]
-        direct_gathers(6)
-        z_third = quantize(z_late[:, 0:T], "z2")
-        high_words(6, z_late[:, T:])
-        z_last = quantize(z_late[:, T:], "z3")
-        out_bf = {block: sb([P, T], BF16, "out_bf%d" % block)[:] for block in (0, 2, 3)}
-        out_bf[1] = shared.tile([P, T], BF16, name="out_bf1", offset=late_offset, align_bytes=64)[:]
-        project(2, z_third[0], banks[6], banks[6])
-        round_out(0, out_bf[0], nc.scalar.copy)
-        store(2, banks[6], banks[6])
-        round_out(1, out_bf[1], nc.vector.tensor_copy)
-        hand_on(0, out_bf[0])
-        hand_on(1, out_bf[1])
-        project(3, z_last[0], banks[3], banks[0])
-        store(3, banks[3], banks[0])
-        store_codes(slice(0, HALF))
-        round_out(2, out_bf[2], nc.vector.tensor_copy)
-        round_out(3, out_bf[3], nc.vector.tensor_copy)
-        hand_on(2, out_bf[2])
-        hand_on(3, out_bf[3])
-        store_codes(slice(HALF, T))
+            for t in (2, 3):
+                scalar_copy(part(early[d], t - 2, HALF), window(t, d, 0, HALF))
+        w3_plane = at([P, H], U8, "w3_plane", W1_BF + 2048)
+        w3_q = [(part(w3_codes, t), part(w3_plane, t)) for t in range(4)]
+        top(ab[2][:], early[0][:], early[1][:])
+        vector_copy(
+            w3_plane[:].rearrange("p (t s i) -> p s t i", t=4, i=16),
+            w3_raw_plane[:].rearrange("p (s i t) -> p s t i", t=4, i=16),
+        )
+        top(m_view[:, 2:4, 0:HALF], pair(ab[2][:]), pair(early[2][:]))
+        for block in (2, 3):
+            for d in range(3):
+                for t in (2, 3):
+                    scalar_copy(part(late[d], 2 * (block - 2) + t - 2), window(t, d, block * P, P))
+        add_y(0, z_sum[:, 0:T])
+        add_y(1, z_sum[:, T:])
+        ab2 = m_view[:, 0:2, 0:P]
+        ab3 = z_sum[:].bitcast(F32)[:, 0:HALF]
+        top(ab2, pair(late[0][:, 0:HALF]), pair(late[1][:, 0:HALF]))
+        nc.vector.tensor_scalar_max(z_early[:], z_sum[:], 0.0)
+        top(m_view[:, 2:4, HALF : HALF + P], ab2, pair(late[2][:, 0:HALF]))
+        z_q = quantize(z_early[:], "z01")
+        for block in range(2):
+            project(z_q[block], banks[1 + block], banks[1 + block])
+        add_y(2, z_sum_late[0][:])
+        top(ab3, late[0][:, HALF:], late[1][:, HALF:])
+        nc.vector.tensor_scalar_max(z_late[0][:], z_sum_late[0][:], 0.0)
+        top(m_view[:, 2:4, HALF + P :], pair(ab3), pair(late[2][:, HALF:]))
+        project(quantize(z_late[0][:], "z2")[0], banks[3], banks[3])
+        add_y(3, z_sum_late[1][:])
+        nc.scalar.copy(out=results[0][:], in_=banks[1][:])
+        store(0)
+        round_out(0, nc.scalar.copy, banks[1][:])
+        nc.scalar.copy(out=results[1][:], in_=banks[2][:])
+        store(1)
+        nc.scalar.copy(out=results[2][:], in_=banks[3][:])
+        store(2)
+        round_out(1, nc.scalar.copy, banks[2][:])
+        nc.vector.tensor_scalar_max(z_late[1][:], z_sum_late[1][:], 0.0)
+        hand_on(0)
+        project(quantize(z_late[1][:], "z3")[0], banks[0], banks[4])
+        round_out(2, nc.vector.tensor_copy, results[2][:])
+        hand_on(1)
+        hand_on(2)
+        store_codes(slice(0, 3 * P))
+        nc.scalar.copy(out=results[3][:, 0:HALF], in_=banks[0][:, 0:HALF])
+        vector_copy(results[3][:, HALF:], banks[4][:, HALF:])
+        store(3)
+        round_out(3, nc.vector.tensor_copy, results[3][:])
+        hand_on(3)
+        store_codes(slice(3 * P, T))
         for q in range(4):
             queue = nc.scalar if q % 2 else nc.sync
             queue.dma_start(

@@ -205,7 +205,7 @@ def tile_picked_wedgecv_relu_lo_kernel(
         vector_copy(raw[2][1][:], window(1, 2, 0, T))
         top(m_view[:, 0], ab[0][:], raw[2][0][:])
         nc.sync.dma_start(out=m[0:64, T : 2 * T], in_=m[64:P, 0:T])
-        vector_copy(e[2][:], e_banks[2][:])
+        nc.scalar.copy(out=e[2][:], in_=e_banks[2][:])
         nc.scalar.copy(out=e[3][:], in_=e_banks[3][:])
         top(ab[1][:], raw[0][1][:], raw[1][1][:])
         vector_copy(grouped_view(w1_bf[:], 0), w1_raw[0])

@@ -22,6 +22,7 @@ VECTOR_GROUPS = 42
 WIDE = 704
 W1_RAW = (4096, 16384)
 W1_BF = 28672
+EARLY = 40960
 
 
 def tile_picked_wedgecv_relu_lo_kernel(
@@ -68,8 +69,8 @@ def tile_picked_wedgecv_relu_lo_kernel(
         w2_raw = [load_weight(w2, 0, sb([P, 4 * HALF], F32, "w2_raw0")[:])]
         load_scales(x_plane, x_scales)
         nc.sync.dma_start(out=x_codes[:].bitcast(I32), in_=x_words[0].rearrange("p n t -> p (n t)").bitcast(I32))
-        w2_raw.append(load_weight(w2, 1, sb([P, 4 * HALF], F32, "w2_raw1")[:]))
         nc.sync.dma_start(lists[0][:], pos1)
+        w2_raw.append(load_weight(w2, 1, sb([P, 4 * HALF], F32, "w2_raw1")[:]))
         nc.sync.dma_start(lists[1][:], pos2)
         nc.sync.dma_start(lists[2][:], pos3)
         w1_raw = [load_weight(w1, h, at([P, 4 * HALF], F32, "w1_raw%d" % h, W1_RAW[h])[:]) for h in range(2)]
@@ -133,9 +134,9 @@ def tile_picked_wedgecv_relu_lo_kernel(
         scalar_copy(low_view(0)[:, VECTOR_GROUPS:], w2_raw[0][:, VECTOR_GROUPS:, :, 0:2])
         w2_q = quantize(w2_low[0][:], "w2a")
         scalar_copy(high_view(0), w2_raw[0][:, :, :, 2:4])
-        for h, copy in enumerate((nc.vector.tensor_copy, nc.scalar.copy)):
-            mx(banks[h][:, 0:HALF], w2_q[0], x_cols(h * HALF, HALF))
-            copy(out=part(e[0], h, HALF), in_=banks[h][:, 0:HALF])
+        for n, copy in enumerate((nc.scalar.copy, nc.vector.tensor_copy) * 2):
+            mx(banks[4 + n][:, 0:P], w2_q[0], x_cols(n * P, P))
+            copy(out=part(e[0], n), in_=banks[4 + n][:, 0:P])
         nc.vector.tensor_copy(out=low_view(1), in_=w2_raw[1][:, :, :, 0:2])
         nc.vector.tensor_copy(out=high_view(1), in_=w2_raw[1][:, :, :, 2:4])
         w2_q = w2_q + quantize(w2_low[1][:], "w2b") + quantize(w2_high[:], "w2c")
@@ -144,7 +145,9 @@ def tile_picked_wedgecv_relu_lo_kernel(
             mx(e_banks[t][:], w2_q[t], x_cols(0, T))
 
         raw = [[sb([P, T], F32, "raw%d_%d" % (d, t)) for t in range(2)] for d in range(3)]
-        ab = [sb([P, T], F32, "ab0"), sb([P, T], F32, "ab1"), at([P, T], F32, "ab01", W1_BF)]
+        third_room = sb([P, 3 * P + T], F32, "third_room")
+        raw[2][1] = third_room[:, 3 * P :]
+        ab = [sb([P, T], F32, "ab0"), sb([P, T], F32, "ab1"), at([P, T], F32, "ab01", W1_RAW[1])]
         m = sb([P, 4 * T], F32, "m")
         m_second = at([P, T], F32, "m_second", W1_RAW[0])
         m_view = m[:].rearrange("p (t v) -> p t v", t=4)
@@ -199,8 +202,9 @@ def tile_picked_wedgecv_relu_lo_kernel(
             for d in range(2):
                 scalar_copy(raw[d][t][:], window(t, d, 0, T))
             if t == 0:
-                vector_copy(raw[2][0][:], window(0, 2, 0, T))
+                vector_copy(raw[2][0][:, 0:HALF], window(0, 2, 0, HALF))
                 vector_copy(e[1][:, 0:T], e_banks[1][:])
+                vector_copy(raw[2][0][:, HALF:], window(0, 2, HALF, HALF))
         top(ab[0][:], raw[0][0][:], raw[1][0][:])
         vector_copy(raw[2][1][:], window(1, 2, 0, T))
         top(m_view[:, 0], ab[0][:], raw[2][0][:])
@@ -213,28 +217,31 @@ def tile_picked_wedgecv_relu_lo_kernel(
         vector_copy(grouped_view(w1_bf[:], 1), w1_raw[1])
         nc.sync.dma_start(out=m[64:P, 0:T], in_=m_second[0:64, :])
         nc.sync.dma_start(out=m[64:P, T : 2 * T], in_=m_second[64:P, :])
+        vector_copy(third_room[:, 3 * P : T], window(3, 2, P, P))
         w1_q = quantize(w1_bf[:], "w1")
         for block in range(4):
             for t in range(4):
                 mx(part(y_banks[block], t), w1_q[t], x_cols(block * P, P))
-        w3_codes = at([P, H], U32, "w3_codes", W1_RAW[1])
+        early = [at([P, T], F32, "early0", EARLY), sb([P, T], F32, "early1"), third_room[:, 0:T]]
+        late = [sb([P, T], F32, "late%d" % d) for d in range(3)]
+        for d in range(2):
+            for t in (2, 3):
+                scalar_copy(part(early[d], t - 2, HALF), window(t, d, 0, HALF))
+        scalar_copy(part(early[2], 0, HALF), window(2, 2, 0, HALF))
+        scalar_copy(part(early[2], 2), window(3, 2, 0, P))
+        top(ab[2][:], early[0][:], early[1][:])
+        w3_codes = at([P, H], U32, "w3_codes", W1_BF)
         vector_copy(
             w3_codes[:].bitcast(I32).rearrange("p (t s i) -> p s t i", t=4, i=4),
             w3_raw[:].bitcast(I32).rearrange("p (s i t) -> p s t i", t=4, i=4),
         )
-        early = [sb([P, T], F32, "early%d" % d) for d in range(3)]
-        late = [sb([P, T], F32, "late%d" % d) for d in range(3)]
-        for d in range(3):
-            for t in (2, 3):
-                scalar_copy(part(early[d], t - 2, HALF), window(t, d, 0, HALF))
-        w3_plane = at([P, H], U8, "w3_plane", W1_BF + 2048)
-        w3_q = [(part(w3_codes, t), part(w3_plane, t)) for t in range(4)]
-        top(ab[2][:], early[0][:], early[1][:])
+        top(m_view[:, 2:4, 0:HALF], pair(ab[2][:]), pair(early[2][:]))
+        w3_plane = at([P, H], U8, "w3_plane", EARLY)
         vector_copy(
             w3_plane[:].rearrange("p (t s i) -> p s t i", t=4, i=16),
             w3_raw_plane[:].rearrange("p (s i t) -> p s t i", t=4, i=16),
         )
-        top(m_view[:, 2:4, 0:HALF], pair(ab[2][:]), pair(early[2][:]))
+        w3_q = [(part(w3_codes, t), part(w3_plane, t)) for t in range(4)]
         for block in (2, 3):
             for d in range(3):
                 for t in (2, 3):
@@ -265,13 +272,16 @@ def tile_picked_wedgecv_relu_lo_kernel(
         round_out(1, nc.scalar.copy, banks[2][:])
         nc.vector.tensor_scalar_max(z_late[1][:], z_sum_late[1][:], 0.0)
         hand_on(0)
-        project(quantize(z_late[1][:], "z3")[0], banks[0], banks[4])
+        z_last = quantize(z_late[1][:], "z3")[0]
+        last_banks = (banks[0], banks[4], banks[5], banks[6])
+        for t in range(4):
+            mx(last_banks[t][:, 0:P], w3_q[t], z_last)
         round_out(2, nc.vector.tensor_copy, results[2][:])
         hand_on(1)
         hand_on(2)
         store_codes(slice(0, 3 * P))
-        nc.scalar.copy(out=results[3][:, 0:HALF], in_=banks[0][:, 0:HALF])
-        vector_copy(results[3][:, HALF:], banks[4][:, HALF:])
+        for t, copy in enumerate((nc.vector.tensor_copy, nc.scalar.copy, nc.scalar.copy, nc.vector.tensor_copy)):
+            copy(out=part(results[3], t), in_=last_banks[t][:, 0:P])
         store(3)
         round_out(3, nc.vector.tensor_copy, results[3][:])
         hand_on(3)

@@ -257,6 +257,7 @@ def tile_picked_wedgecv_relu_lo_kernel(
         for block in range(2):
             project(z_q[block], banks[1 + block], banks[1 + block])
         add_y(2, z_sum_late[0][:])
+        mx(y_banks[2][:], w1_q[3], x_cols(0, T))
         top(ab3, late[0][:, HALF:], late[1][:, HALF:])
         nc.vector.tensor_scalar_max(z_late[0][:], z_sum_late[0][:], 0.0)
         top(m_view[:, 2:4, HALF + P :], pair(ab3), pair(late[2][:, HALF:]))

@@ -155,7 +155,7 @@ def tile_picked_wedgecv_relu_lo_kernel(
         z_sum_late = [sb([P, T], BF16, "z_sum%d" % b) for b in (2, 3)]
         z_early = sb([P, 2 * T], BF16, "z_early")
         z_late = [sb([P, T], BF16, "z%d" % b) for b in (2, 3)]
-        y_banks = banks[4:8]
+        y_banks = [banks[4], banks[5]] * 2
 
         def vector_copy(out, in_):
             nc.vector.tensor_copy(out, in_)
@@ -219,9 +219,13 @@ def tile_picked_wedgecv_relu_lo_kernel(
         nc.sync.dma_start(out=m[64:P, T : 2 * T], in_=m_second[64:P, :])
         vector_copy(third_room[:, 3 * P : T], window(3, 2, P, P))
         w1_q = quantize(w1_bf[:], "w1")
-        for block in range(4):
+
+        def centre_product(block):
             for t in range(4):
                 mx(part(y_banks[block], t), w1_q[t], x_cols(block * P, P))
+
+        centre_product(0)
+        centre_product(1)
         early = [at([P, T], F32, "early0", EARLY), sb([P, T], F32, "early1"), third_room[:, 0:T]]
         late = [sb([P, T], F32, "late%d" % d) for d in range(3)]
         for d in range(2):
@@ -247,7 +251,9 @@ def tile_picked_wedgecv_relu_lo_kernel(
                 for t in (2, 3):
                     scalar_copy(part(late[d], 2 * (block - 2) + t - 2), window(t, d, block * P, P))
         add_y(0, z_sum[:, 0:T])
+        centre_product(2)
         add_y(1, z_sum[:, T:])
+        centre_product(3)
         ab2 = m_view[:, 0:2, 0:P]
         ab3 = z_sum[:].bitcast(F32)[:, 0:HALF]
         top(ab2, pair(late[0][:, 0:HALF]), pair(late[1][:, 0:HALF]))
@@ -257,11 +263,12 @@ def tile_picked_wedgecv_relu_lo_kernel(
         for block in range(2):
             project(z_q[block], banks[1 + block], banks[1 + block])
         add_y(2, z_sum_late[0][:])
-        mx(y_banks[2][:], w1_q[3], x_cols(0, T))
         top(ab3, late[0][:, HALF:], late[1][:, HALF:])
         nc.vector.tensor_scalar_max(z_late[0][:], z_sum_late[0][:], 0.0)
         top(m_view[:, 2:4, HALF + P :], pair(ab3), pair(late[2][:, HALF:]))
-        project(quantize(z_late[0][:], "z2")[0], banks[3], banks[3])
+        z_third = quantize(z_late[0][:], "z2")[0]
+        project(z_third, banks[3], banks[3])
+        mx(banks[7][:], z_third, x_cols(0, T))
         add_y(3, z_sum_late[1][:])
         nc.scalar.copy(out=results[0][:], in_=banks[1][:])
         store(0)

@@ -42,13 +42,12 @@ def tile_picked_wedgecv_relu_lo_kernel(
 
         lists = [keep.tile([P, T // 16], U16, name="pos%d" % d) for d in range(3)]
         x_codes = sb([P, T], U32, "x_codes")
-        x_plane = sb([P, T], U8, "x_plane")
+        loaded_planes = sb([P, T + H], U8, "loaded_planes")
+        x_plane, w3_raw_plane = loaded_planes[:, 0:T], loaded_planes[:, T:]
         w3_raw = sb([P, H], U32, "w3_raw")
-        w3_raw_plane = sb([P, H], U8, "w3_raw_plane")
         e = [sb([P, WIDE if t < 2 else T], F32, "e%d" % t) for t in range(4)]
 
-        nc.vector.memset(x_plane[:].bitcast(I32), 0)
-        nc.vector.memset(w3_raw_plane[:].bitcast(I32), 0)
+        nc.vector.memset(loaded_planes[:].bitcast(I32), 0)
         for t in range(2):
             nc.vector.memset(e[t][:, T:], 0.0)
 
@@ -295,7 +294,7 @@ def tile_picked_wedgecv_relu_lo_kernel(
         hand_on(3)
         store_codes(slice(3 * P, T))
         for q in range(4):
-            queue = nc.scalar if q % 2 else nc.sync
+            queue = nc.scalar if q == 3 else nc.sync
             queue.dma_start(
                 out=out_2[0, 4 * q : 4 * q + 4, :].bitcast(I32),
                 in_=out_plane[32 * q : 32 * q + 4, :].bitcast(I32),

from contextlib import ExitStack

import concourse.mybir as mybir

K, T, H = 512, 512, 512
FLOPS = 3 * 2 * K * T * H

F32 = mybir.dt.float32
BF16 = mybir.dt.bfloat16
I32 = mybir.dt.int32
U32 = mybir.dt.uint32
U16 = mybir.dt.uint16
U8 = mybir.dt.uint8
FP8X4 = mybir.dt.float8_e4m3fn_x4
COPY = mybir.ActivationFunctionType.Copy
MAX = mybir.AluOpType.max
ADD = mybir.AluOpType.add

P = 128
HALF = 256
VECTOR_GROUPS = 42
WIDE = 704
W1_RAW = (4096, 16384)
W1_BF = 28672
EARLY = 40960


def tile_picked_wedgecv_relu_lo_kernel(
    tc, x_words, x_scales, w1, w2, w3_words, w3_scales, pos1, pos2, pos3, out_0, out_1, out_2
):
    nc = tc.nc
    with ExitStack() as ctx:
        keep = ctx.enter_context(tc.tile_pool(name="keep", bufs=1))
        shared = ctx.enter_context(tc.tile_pool(name="shared", bufs=1))
        psum = ctx.enter_context(tc.psum_pool(name="psum", bufs=1))

        def sb(shape, dtype, name):
            return keep.tile(shape, dtype, name=name, tag=name, align_bytes=64)

        def at(shape, dtype, name, offset):
            return shared.tile(shape, dtype, name=name, offset=offset, align_bytes=64)

        lists = [keep.tile([P, T // 16], U16, name="pos%d" % d) for d in range(3)]
        x_codes = sb([P, T], U32, "x_codes")
        loaded_planes = sb([P, T + H], U8, "loaded_planes")
        x_plane, w3_raw_plane = loaded_planes[:, 0:T], loaded_planes[:, T:]
        w3_raw = sb([P, H], U32, "w3_raw")
        e = [sb([P, WIDE if t < 2 else T], F32, "e%d" % t) for t in range(4)]

        nc.vector.memset(loaded_planes[:].bitcast(I32), 0)
        for t in range(2):
            nc.vector.memset(e[t][:, T:], 0.0)

        def load_scales(plane, scales):
            for q in range(4):
                nc.sync.dma_start(
                    out=plane[32 * q : 32 * q + 4, :].bitcast(I32),
                    in_=scales[0, 4 * q : 4 * q + 4, :].bitcast(I32),
                )

        def load_weight(w, half, raw):
            nc.sync.dma_start(
                out=raw.rearrange("p (j c) -> p j c", j=4),
                in_=w.rearrange("(p j) c -> p j c", j=4)[:, :, half * HALF : (half + 1) * HALF],
            )
            return raw.rearrange("p (j m t) -> p m j t", j=4, t=4)

        w2_raw = [load_weight(w2, 0, sb([P, 4 * HALF], F32, "w2_raw0")[:])]
        load_scales(x_plane, x_scales)
        nc.sync.dma_start(out=x_codes[:].bitcast(I32), in_=x_words[0].rearrange("p n t -> p (n t)").bitcast(I32))
        nc.sync.dma_start(lists[0][:], pos1)
        w2_raw.append(load_weight(w2, 1, sb([P, 4 * HALF], F32, "w2_raw1")[:]))
        nc.sync.dma_start(lists[1][:], pos2)
        nc.sync.dma_start(lists[2][:], pos3)
        w1_raw = [load_weight(w1, h, at([P, 4 * HALF], F32, "w1_raw%d" % h, W1_RAW[h])[:]) for h in range(2)]
        nc.sync.dma_start(out=w3_raw[:].bitcast(I32), in_=w3_words[0].rearrange("p n t -> p (n t)").bitcast(I32))
        load_scales(w3_raw_plane, w3_scales)

        banks = [psum.tile([P, T], F32, name="bank%d" % n) for n in range(8)]

        def grouped_view(grouped, half):
            return grouped.rearrange("p (t h m j) -> p h m j t", t=4, h=2, j=4)[:, half]

        def scalar_copy(out, in_):
            nc.scalar.activation(out, in_, COPY)

        def quantize(grouped, name):
            words = grouped.shape[1] // 4
            codes = sb([P, words], U32, name + "_codes")
            plane = sb([P, words], U8, name + "_plane")
            nc.vector.quantize_mx(out=codes[:].bitcast(FP8X4), scales=plane[:], in_=grouped)
            return [(codes[:, n * P : (n + 1) * P], plane[:, n * P : (n + 1) * P]) for n in range(words // P)]

        def mx(acc, weight, moving):
            nc.tensor.matmul_mx(
                out=acc,
                lhsT=weight[0].bitcast(FP8X4),
                lhsT_scale=weight[1],
                rhs=moving[0].bitcast(FP8X4),
                rhs_scale=moving[1],
                start=True,
                stop=True,
            )

        def x_cols(first, count):
            return x_codes[:, first : first + count], x_plane[:, first : first + count]

        def part(ap, n, width=P):
            return ap[:, n * width : (n + 1) * width]

        def window(t, d, first, count):
            return e[t][:].indirect(lists[d][:, first // 16 : (first + count) // 16])

        def woven(ap):
            return ap.rearrange("p (s i t) -> p s t i", i=4, t=4)

        def by_tile(ap, width, n):
            return ap.rearrange("p (t v) -> p t v", t=4)[:, :, n * P : (n + 1) * P].rearrange(
                "p t (s i) -> p s t i", i=4
            )

        w1_bf = at([P, 4 * T], BF16, "w1_bf", W1_BF)
        w2_low = [sb([P, T], BF16, "w2_low%d" % h) for h in range(2)]
        w2_high = sb([P, 2 * T], BF16, "w2_high")

        def low_view(h):
            return w2_low[h][:].rearrange("p (t m j) -> p m j t", t=2, j=4)

        def high_view(h):
            return w2_high[:].rearrange("p (t h m j) -> p h m j t", t=2, h=2, j=4)[:, h]

        nc.vector.tensor_copy(out=low_view(0)[:, 0:VECTOR_GROUPS], in_=w2_raw[0][:, 0:VECTOR_GROUPS, :, 0:2])
        scalar_copy(low_view(0)[:, VECTOR_GROUPS:], w2_raw[0][:, VECTOR_GROUPS:, :, 0:2])
        w2_q = quantize(w2_low[0][:], "w2a")
        scalar_copy(high_view(0), w2_raw[0][:, :, :, 2:4])
        for n, copy in enumerate((nc.scalar.copy, nc.vector.tensor_copy) * 2):
            mx(banks[4 + n][:, 0:P], w2_q[0], x_cols(n * P, P))
            copy(out=part(e[0], n), in_=banks[4 + n][:, 0:P])
        nc.vector.tensor_copy(out=low_view(1), in_=w2_raw[1][:, :, :, 0:2])
        nc.vector.tensor_copy(out=high_view(1), in_=w2_raw[1][:, :, :, 2:4])
        w2_q = w2_q + quantize(w2_low[1][:], "w2b") + quantize(w2_high[:], "w2c")
        e_banks = [None, banks[2], banks[3], banks[0]]
        for t in (1, 2, 3):
            mx(e_banks[t][:], w2_q[t], x_cols(0, T))

        raw = [[sb([P, T], F32, "raw%d_%d" % (d, t)) for t in range(2)] for d in range(3)]
        third_room = sb([P, 3 * P + T], F32, "third_room")
        raw[2][1] = third_room[:, 3 * P :]
        ab = [sb([P, T], F32, "ab0"), sb([P, T], F32, "ab1"), at([P, T], F32, "ab01", W1_RAW[1])]
        m = sb([P, 4 * T], F32, "m")
        m_second = at([P, T], F32, "m_second", W1_RAW[0])
        m_view = m[:].rearrange("p (t v) -> p t v", t=4)
        z_sum = sb([P, 2 * T], BF16, "z_sum")
        z_sum_late = [sb([P, T], BF16, "z_sum%d" % b) for b in (2, 3)]
        z_early = sb([P, 2 * T], BF16, "z_early")
        z_late = [sb([P, T], BF16, "z%d" % b) for b in (2, 3)]
        y_banks = [banks[4], banks[5]] * 2

        def vector_copy(out, in_):
            nc.vector.tensor_copy(out, in_)

        def top(out, in0, in1):
            nc.vector.tensor_tensor(out, in0, in1, MAX)

        def pair(ap):
            return ap.rearrange("p (t v) -> p t v", t=2)

        def add_y(block, out):
            nc.vector.tensor_tensor(woven(out), by_tile(y_banks[block][:], P, 0), by_tile(m[:], P, block), ADD)

        results = [sb([P, T], F32, "result%d" % b) for b in range(4)]
        out_bf = [sb([P, T], BF16, "out_bf%d" % b) for b in range(4)]
        out_codes = sb([P, T], U32, "out_codes")
        out_plane = sb([P, T], U8, "out_plane")

        def project(z_q, bank, second):
            for t in range(4):
                mx(part(bank if t < 2 else second, t), w3_q[t], z_q)

        def store(block):
            nc.sync.dma_start(
                out=out_0.rearrange("(p t) v -> p t v", t=4)[:, :, block * P : (block + 1) * P],
                in_=results[block][:].rearrange("p (t v) -> p t v", t=4),
            )

        def round_out(block, copy, src):
            copy(out=woven(out_bf[block][:]), in_=by_tile(src, P, 0))

        def hand_on(block):
            nc.vector.quantize_mx(
                out=part(out_codes, block).bitcast(FP8X4), scales=part(out_plane, block), in_=out_bf[block][:]
            )

        def store_codes(cols):
            nc.sync.dma_start(
                out=out_1[0].rearrange("p n t -> p (n t)").bitcast(I32)[:, cols],
                in_=out_codes[:, cols].bitcast(I32),
            )

        for t in range(2):
            for d in range(2):
                scalar_copy(raw[d][t][:], window(t, d, 0, T))
            if t == 0:
                vector_copy(raw[2][0][:, 0:HALF], window(0, 2, 0, HALF))
                vector_copy(e[1][:, 0:T], e_banks[1][:])
                vector_copy(raw[2][0][:, HALF:], window(0, 2, HALF, HALF))
        top(ab[0][:], raw[0][0][:], raw[1][0][:])
        vector_copy(raw[2][1][:], window(1, 2, 0, T))
        top(m_view[:, 0], ab[0][:], raw[2][0][:])
        nc.sync.dma_start(out=m[0:64, T : 2 * T], in_=m[64:P, 0:T])
        nc.scalar.copy(out=e[2][:], in_=e_banks[2][:])
        nc.scalar.copy(out=e[3][:], in_=e_banks[3][:])
        top(ab[1][:], raw[0][1][:], raw[1][1][:])
        vector_copy(grouped_view(w1_bf[:], 0), w1_raw[0])
        top(m_second[:], ab[1][:], raw[2][1][:])
        vector_copy(grouped_view(w1_bf[:], 1), w1_raw[1])
        nc.sync.dma_start(out=m[64:P, 0:T], in_=m_second[0:64, :])
        nc.sync.dma_start(out=m[64:P, T : 2 * T], in_=m_second[64:P, :])
        vector_copy(third_room[:, 3 * P : T], window(3, 2, P, P))
        w1_q = quantize(w1_bf[:], "w1")

        def centre_product(block):
            for t in range(4):
                mx(part(y_banks[block], t), w1_q[t], x_cols(block * P, P))

        centre_product(0)
        centre_product(1)
        early = [at([P, T], F32, "early0", EARLY), sb([P, T], F32, "early1"), third_room[:, 0:T]]
        late = [sb([P, T], F32, "late%d" % d) for d in range(3)]
        for d in range(2):
            for t in (2, 3):
                scalar_copy(part(early[d], t - 2, HALF), window(t, d, 0, HALF))
        scalar_copy(part(early[2], 0, HALF), window(2, 2, 0, HALF))
        scalar_copy(part(early[2], 2), window(3, 2, 0, P))
        top(ab[2][:], early[0][:], early[1][:])
        w3_codes = at([P, H], U32, "w3_codes", W1_BF)
        vector_copy(
            w3_codes[:].bitcast(I32).rearrange("p (t s i) -> p s t i", t=4, i=4),
            w3_raw[:].bitcast(I32).rearrange("p (s i t) -> p s t i", t=4, i=4),
        )
        top(m_view[:, 2:4, 0:HALF], pair(ab[2][:]), pair(early[2][:]))
        w3_plane = at([P, H], U8, "w3_plane", EARLY)
        vector_copy(
            w3_plane[:].rearrange("p (t s i) -> p s t i", t=4, i=16),
            w3_raw_plane[:].rearrange("p (s i t) -> p s t i", t=4, i=16),
        )
        w3_q = [(part(w3_codes, t), part(w3_plane, t)) for t in range(4)]
        for block in (2, 3):
            for d in range(3):
                for t in (2, 3):
                    scalar_copy(part(late[d], 2 * (block - 2) + t - 2), window(t, d, block * P, P))
        add_y(0, z_sum[:, 0:T])
        centre_product(2)
        add_y(1, z_sum[:, T:])
        centre_product(3)
        ab2 = m_view[:, 0:2, 0:P]
        ab3 = z_sum[:].bitcast(F32)[:, 0:HALF]
        top(ab2, pair(late[0][:, 0:HALF]), pair(late[1][:, 0:HALF]))
        nc.vector.tensor_scalar_max(z_early[:], z_sum[:], 0.0)
        top(m_view[:, 2:4, HALF : HALF + P], ab2, pair(late[2][:, 0:HALF]))
        z_q = quantize(z_early[:], "z01")
        for block in range(2):
            project(z_q[block], banks[1 + block], banks[1 + block])
        add_y(2, z_sum_late[0][:])
        top(ab3, late[0][:, HALF:], late[1][:, HALF:])
        nc.vector.tensor_scalar_max(z_late[0][:], z_sum_late[0][:], 0.0)
        top(m_view[:, 2:4, HALF + P :], pair(ab3), pair(late[2][:, HALF:]))
        z_third = quantize(z_late[0][:], "z2")[0]
        project(z_third, banks[3], banks[3])
        mx(banks[7][:], z_third, x_cols(0, T))
        add_y(3, z_sum_late[1][:])
        nc.scalar.copy(out=results[0][:], in_=banks[1][:])
        store(0)
        round_out(0, nc.scalar.copy, banks[1][:])
        nc.scalar.copy(out=results[1][:], in_=banks[2][:])
        store(1)
        nc.scalar.copy(out=results[2][:], in_=banks[3][:])
        store(2)
        round_out(1, nc.scalar.copy, banks[2][:])
        nc.vector.tensor_scalar_max(z_late[1][:], z_sum_late[1][:], 0.0)
        hand_on(0)
        z_last = quantize(z_late[1][:], "z3")[0]
        last_banks = (banks[0], banks[4], banks[5], banks[6])
        for t in range(4):
            mx(last_banks[t][:, 0:P], w3_q[t], z_last)
        round_out(2, nc.vector.tensor_copy, results[2][:])
        hand_on(1)
        hand_on(2)
        store_codes(slice(0, 3 * P))
        for t, copy in enumerate((nc.vector.tensor_copy, nc.scalar.copy, nc.scalar.copy, nc.vector.tensor_copy)):
            copy(out=part(results[3], t), in_=last_banks[t][:, 0:P])
        store(3)
        round_out(3, nc.vector.tensor_copy, results[3][:])
        hand_on(3)
        store_codes(slice(3 * P, T))
        for q in range(4):
            queue = nc.scalar if q == 3 else nc.sync
            queue.dma_start(
                out=out_2[0, 4 * q : 4 * q + 4, :].bitcast(I32),
                in_=out_plane[32 * q : 32 * q + 4, :].bitcast(I32),
            )
